import numpy as np, ml_dtypes
CORES = [16,18,20,22]
N = 4
BF = ml_dtypes.bfloat16
def gentries(a):
    return np.ascontiguousarray(a.reshape(8, 16, -1).transpose(0, 2, 1)).reshape(8, -1)
def gtable(e):
    e = np.asarray(e); return np.ascontiguousarray(e.reshape(8, -1, 16).transpose(0, 2, 1)).reshape(128, -1).astype(np.int32)
S, RO, M, KS = 1024, 6, 32, 4096
W = N * S
def pair(o):
    p = np.empty(W, np.int64); p[o] = o[np.arange(W) ^ 1]; return p
def match(rng):
    return pair(rng.permutation(W))
def inside(rng):
    return pair(np.concatenate([q * S + rng.permutation(S) for q in range(N)]))
def across(rng):
    return pair(np.stack([np.arange(W // 2), W // 2 + rng.permutation(W // 2)], axis=1).reshape(-1))
def four(o, k):
    p = np.empty(W, np.int64); p[o.reshape(-1)] = o[:, np.arange(4) ^ k].reshape(-1); return p
def eights(rng):
    k = W // 8; i = np.arange(k); z = rng.permutation(np.arange(k, W - 2 * k)).reshape(k, 5)
    o = np.stack([z[:, 0], i, z[:, 1], W - 2 - 2 * i, W - 1 - 2 * i, z[:, 2], z[:, 3], z[:, 4]], axis=1)
    e = np.concatenate([np.full((k, 8), 28), rng.choice(np.array([8, 12, 16]), (k, 7)), np.ones((k, 1), np.int64)], axis=1)
    e = np.take_along_axis(e, np.argsort(rng.random((k, 16)), axis=1), 1)
    lo = rng.integers(0, M - 28, (k, 16)); hi = lo + e; one = lo + (e == 1)
    a = np.empty((16, W), np.int64); a[:, o.reshape(-1)] = np.stack([one, hi, hi, lo, lo, hi, hi, hi], axis=1).reshape(W, 16).T
    return pair(o.reshape(-1)), pair(np.roll(o, -1, axis=1).reshape(-1)), a
def parts(rng):
    share = rng.permutation(np.array([0.1, 0.2, 0.3, 0.5, 0.7, 1.0, 1.0, 1.0])).reshape(8, 1, 1)
    a = rng.integers(0, M, (8, 16, W)); b = np.where(rng.random((8, 16, W)) < share, rng.integers(0, M, (8, 16, W)), 0)
    return a, b, np.stack([match(rng) for g in range(8)]), np.stack([np.stack([match(rng) for t in range(RO)]) for g in range(8)])
def pack(a, b, lk, cd):
    side = lambda v: np.ascontiguousarray(v.reshape(128, N, S).transpose(1, 0, 2)).astype(np.float32).astype(BF)
    return {"x": side(a), "u": side(b), "link": np.stack([gtable(lk[:, q * S:(q + 1) * S]) for q in range(N)]),
            "cand": np.stack([gtable(cd[:, :, q * S:(q + 1) * S].reshape(8, RO * S)) for q in range(N)])}
def setup_inputs(rng):
    return pack(*parts(rng))
def setup_inputs_ties(rng):
    a, b, lk, cd = parts(rng)
    pa = rng.integers(0, M, (8, 16, 4)); pb = rng.integers(0, M, (8, 16, 4))
    pa[2:4] = 0; pa[2:4, 0, 2:] = 1; pb[2:4] = 0
    kind = np.broadcast_to(rng.integers(0, 4, (8, 1, W)), (8, 16, W))
    a[2:] = np.take_along_axis(pa, kind, 2)[2:]; b[2:] = np.take_along_axis(pb, kind, 2)[2:]
    for g in range(2):
        o = rng.permutation(W).reshape(W // 4, 4); lk[g] = four(o, 1)
        for t in range(RO): cd[g, t] = four(o, (2, 3, 1)[t % 3])
    return pack(a, b, lk, cd)
def setup_inputs_again(rng):
    a, b, lk, cd = parts(rng); b = rng.integers(0, 2, b.shape)
    for g in (0, 1): cd[g, 1:] = cd[g, :1]
    for g in (2, 3): cd[g, 0] = lk[g]
    for g in (4, 5): cd[g, 2:] = cd[g, np.arange(2, RO) % 2]
    for g in (6, 7):
        o = rng.permutation(W); lk[g] = pair(o); h = W // 2
        for t in range(RO): cd[g, t] = pair(np.concatenate([o[:h], rng.permutation(o[h:])]))
    return pack(a, b, lk, cd)
def setup_inputs_places(rng):
    a, b, lk, cd = parts(rng); v = np.arange(W)
    lk[0] = v ^ 1; lk[1] = W - 1 - v; lk[2] = (v + W // 2) % W; lk[3] = inside(rng); lk[4] = inside(rng); lk[5] = across(rng)
    for t in range(RO):
        cd[0, t] = W - 1 - v if t % 2 == 0 else v ^ 2
        cd[1, t] = v ^ (1 << (t % 4)); cd[2, t] = inside(rng); cd[3, t] = inside(rng); cd[4, t] = across(rng); cd[5, t] = across(rng)
    o = np.concatenate([np.stack([q * S + rng.permutation(S) for q in four_ranks], axis=1) for four_ranks in rng.permutation(N).reshape(N // 4, 4)])
    lk[7] = four(o, 1); cd[7, 0] = four(o, 2); cd[7, 1] = cd[7, 0]
    p = rng.integers(0, M, (W // 4, 16)); e = (p + rng.integers(M // 4, M - M // 4 + 1, (W // 4, 16))) & (M - 1)
    a[7][:, o.reshape(-1)] = np.stack([p, e, p, e], axis=1).reshape(W, 16).T
    b[6] = rng.integers(0, M, (16, W))
    return pack(a, b, lk, cd)
def setup_inputs_far(rng):
    a, b, lk, cd = parts(rng); v = np.arange(W)
    for g in range(8):
        flip = (rng.random(W) < 0.5)[np.minimum(v, lk[g])]
        s = flip if g % 2 else flip ^ (v < lk[g])
        a[g] = np.where(s, 31, 0)[None, :]
        b[g] = rng.choice(np.array([0, 31]), W)[None, :]
    lk[3], cd[3, 1], a[3] = eights(rng)
    lk[4], last, a[4] = eights(rng); b[4] = 0; cd[4, 1:RO - 1] = lk[4]; cd[4, RO - 1] = last
    o = np.concatenate([np.arange(W // 2).reshape(W // 4, 2), (W // 2 + rng.permutation(W // 2)).reshape(W // 4, 2)], axis=1)
    lk[6] = four(o, 1); cd[6, 1] = four(o, 2); s = np.zeros(W, bool)
    s[o.reshape(-1)] = ((rng.random((W // 4, 1)) < 0.5) ^ (np.arange(4) % 2 == 1)[None, :]).reshape(-1)
    a[6] = np.where(s, 31, 0)[None, :]
    a[7] = rng.integers(0, M, (16, 1)); b[7] = 0
    cd[:, 0] = lk
    return pack(a, b, lk, cd)
def setup_inputs_spread(rng):
    a, b, lk, cd = parts(rng)
    a = np.minimum((np.exp2(5 * rng.random((8, 1, W))) * rng.random(a.shape) * 1.25).astype(np.int64), M - 1)
    b = np.minimum((np.exp2(5 * rng.random((8, 1, W))) * rng.random(b.shape) ** 2).astype(np.int64), M - 1) * (rng.random((8, 1, W)) < 0.75)
    return pack(a, b, lk, cd)
def joined(a, n):
    e = np.stack([gentries(b) for b in a]).astype(np.int64).reshape(N, 8, n, S)
    return np.ascontiguousarray(e.transpose(1, 2, 0, 3)).reshape(8, n, W)
def check_inputs(d):
    bad = []
    for k in ("x", "u"):
        a = np.asarray(d[k]).astype(np.float32)
        if not np.all((a >= 0) & (a <= M - 1) & (a == np.floor(a))): bad.append("range of " + k)
    for k, n in (("link", 1), ("cand", RO)):
        a = np.asarray(d[k])
        if np.min(a) < 0 or np.max(a) > W - 1: bad.append("range of " + k); continue
        e = joined(a, n); v = np.arange(W)
        if np.any(e == v): bad.append("a satellite paired with itself in " + k)
        if np.any(np.take_along_axis(e, e, 2) != v): bad.append("pairs of " + k)
    return bad
def pick(a, i):
    return np.take_along_axis(a, i, 1) if a.ndim == 2 else np.take_along_axis(a, i[:, None, :], 2)
def cost(a, b):
    e = np.abs(a - b)
    return np.add.reduce(e, axis=1)
def reference(x, u, link, cand):
    xs, us = [np.ascontiguousarray(a.astype(np.float32).astype(np.int64).transpose(1, 0, 2)).reshape(8, 16, W) for a in (x, u)]
    lk = joined(link, 1)[:, 0]; cd = joined(cand, RO); v = np.arange(W)
    for t in range(RO):
        b = lk; c = cd[:, t]; d = pick(lk, c)
        xb = pick(xs, b); xc = pick(xs, c); xd = pick(xs, d)
        g = cost(xs, xb) + cost(xc, xd) - cost(xs, xc) - cost(xb, xd)
        key = KS * g - np.minimum(v, c)
        go = (g > 0) & (key > pick(key, b)) & (key > pick(key, d))
        new = np.where(go, c, np.where(pick(go, b), pick(d, b), b))
        ch = np.roll(new != lk, -1, axis=0).astype(np.int64)
        xs = (xs + us * ch[:, None, :]) & (M - 1)
        lk = new
    return {"ylink": np.stack([gtable(lk[:, q * S:(q + 1) * S]) for q in range(N)]).astype(np.float32)}

@@ -1,0 +1,483 @@
+from concourse.bass import DstId, RemoteDMATransfer
+from concourse.mybir import AluOpType as A, ActivationFunctionType as AF, AxisListType
+
+RO, S, W, N = 6, 1024, 4096, 4
+BF, F32, I32, U16 = "bfloat16", "float32", "int32", "uint16"
+THETA = -256.0 * 4096.0
+CHUNKS = [(0, 512), (512, 768), (768, 1024)]
+TDCUT = 384
+MATS = ["BP", "BM", "MM", "Ao", "Ab", "Ad", "Ae", "Bs", "Be", "Bt", "Br"]
+
+SCRATCH = {
+    "XT": ("sbuf", [128, RO * W], BF), "TA": ("sbuf", [128, W], BF), "TZ": ("sbuf", [128, W], BF), "KK": ("sbuf", [128, W], BF),
+    "U": ("sbuf", [128, S], BF), "SG": ("sbuf", [128, S], BF), "SN": ("sbuf", [128, S], BF),
+    "TC": ("sbuf", [128, S], BF), "TB": ("sbuf", [128, S], BF), "TD": ("sbuf", [128, S], BF), "TE": ("sbuf", [128, S], BF),
+    "XV": ("sbuf", [128, S], BF), "XB": ("sbuf", [128, S], BF), "XD": ("sbuf", [128, S], BF),
+    "M1": ("sbuf", [128, S], BF), "M2": ("sbuf", [128, S], BF), "M3": ("sbuf", [128, S], BF), "M4": ("sbuf", [128, S], BF),
+    "GK": ("sbuf", [128, 3 * S], BF),
+    "R0": ("sbuf", [128, S], BF), "R": ("sbuf", [128, S], BF), "RS": ("sbuf", [128, S], BF),
+    "IN": ("sbuf", [128, 7 * 64], I32), "HI": ("sbuf", [128, 128], I32), "LO": ("sbuf", [128, 128], I32),
+    "S0": ("sbuf", [128, 256], BF), "SV": ("sbuf", [128, 128], BF), "SP": ("sbuf", [128, 256], BF),
+    "CL": ("sbuf", [128, RO * 64], U16), "KL": ("sbuf", [128, 192], U16), "PL": ("sbuf", [128, 64], U16),
+    "LCB": ("sbuf", [128, 64], U16),
+    "AV": ("sbuf", [128, 64], U16), "AB": ("sbuf", [128, 64], U16), "AC": ("sbuf", [128, 64], U16), "AD": ("sbuf", [128, 64], U16),
+    "Y": ("sbuf", [128, 64], F32), "MN": ("sbuf", [128, 64], I32), "J": ("sbuf", [128, 256], I32), "JV": ("sbuf", [128, 128], I32),
+    "VAL": ("sbuf", [128, 144], F32), "PC": ("sbuf", [128, 8], I32), "CF": ("sbuf", [128, 8], F32),
+    "OH": ("sbuf", [128, 16], F32), "GM": ("sbuf", [128, 32], F32), "WC": ("sbuf", [128, 32], F32), "VR": ("sbuf", [128, 64], I32),
+    "ZL": ("sbuf", [128, 144], BF), "ZA": ("sbuf", [128, 144], BF), "ZC": ("sbuf", [128, 144], BF),
+    "MAT": ("sbuf", [128, len(MATS) * 128], BF), "ID": ("sbuf", [128, 128], BF),
+    "F0": ("psum", [128, 512], F32), "F1": ("psum", [128, 512], F32), "F2": ("psum", [128, 512], F32),
+    "G0": ("psum", [128, 512], F32), "G1": ("psum", [128, 512], F32),
+    "C0": ("psum", [128, 512], F32), "C1": ("psum", [128, 512], F32), "C2": ("psum", [128, 512], F32),
+}
+PSUM = [k for k, v in SCRATCH.items() if v[0] == "psum"]
+SEMAPHORES = (["sV", "sS", "sP", "sG", "ldl", "ldc", "ldx", "ldu", "dself", "dfirst", "out", "lK0", "lK1", "lT0", "lT1", "lO"]
+              + ["%s%d" % (n, t) for n in ("aX", "aK", "aT", "dR") for t in range(RO)])
+
+
+def make_plan():
+    ops, last_w, readers, cnt = [], {}, {}, {}
+
+    def add(q, fn, r=(), w=(), sem=None, inc=1, acc=False, whole=False):
+        deps = set()
+        for k in r:
+            deps.add(last_w[k])
+            if k in PSUM:
+                deps.update(o for o in readers.get(k, ()) if ops[o]["q"] != q)
+        for k in w:
+            if k in last_w and not (acc and ops[last_w[k]]["q"] == q):
+                deps.add(last_w[k])
+            deps.update(readers.get(k, ()))
+        sem = sem or {"V": "sV", "S": "sS", "P": "sP", "G": "sG"}[q]
+        cnt[sem] = cnt.get(sem, 0) + inc
+        me = len(ops)
+        ops.append(dict(q=q, fn=fn, deps=sorted(deps), sem=sem, n=cnt[sem], inc=inc, whole=whole))
+        for k in r:
+            readers.setdefault(k, []).append(me)
+        for k in w:
+            last_w[k] = me
+            readers[k] = []
+        return me
+
+    def emit(queues, T):
+        clock = {q: {} for q in queues}
+        seen = {}
+        for me, o in enumerate(ops):
+            q = o["q"]
+            if q == "X":
+                o["clock"] = {}
+                seen[o["sem"]] = o["n"]
+                continue
+            ck = clock[q]
+            for d in sorted(o["deps"], reverse=True):
+                p = ops[d]
+                n = seen[p["sem"]] if p["whole"] else p["n"]
+                if ck.get(p["sem"], 0) >= n:
+                    continue
+                queues[q].wait_ge(T.sem[p["sem"]], n)
+                ck[p["sem"]] = n
+                for z in ([y for y in ops[:me] if y["sem"] == p["sem"]] if p["whole"] else [p]):
+                    for s, v in z["clock"].items():
+                        if ck.get(s, 0) < v:
+                            ck[s] = v
+            o["clock"] = dict(ck)
+            seen[o["sem"]] = o["n"]
+            ins = o["fn"]()
+            if ins is not None:
+                ins.then_inc(T.sem[o["sem"]], o["inc"])
+        for s, n in cnt.items():
+            if clock["G"].get(s, 0) < n:
+                queues["G"].wait_ge(T.sem[s], n)
+
+    return add, emit
+
+
+def rank_program(g, core, T, topo):
+    q = T.rank_of(core)
+    if q is None:
+        return
+    V, SC, PE, SY = g.vector, g.scalar, g.tensor, g.sync
+    add, emit = make_plan()
+    peers = [c for c in T.cores if c != core]
+    mask = topo.mask(core, peers[0])
+    for c in peers:
+        mask &= topo.mask(core, c)
+    nen = bin(mask).count("1")
+
+    def send(ap, rsem, lsem, r):
+        def fn():
+            ids = [DstId(rid=topo.addr(c)[0], pnc=topo.addr(c)[1]) for c in peers]
+            g.remote_dma_fused([RemoteDMATransfer(dst_ids=ids, dma_engine_mask=mask, remote_sem=T.sem[rsem],
+                                                  srcs=[ap], dsts=[ap] * len(ids))], local_sem=T.sem[lsem])
+        add("G", fn, r=r, sem=lsem, inc=nen, whole=True)
+
+    def arrival(sem, keys, calls=1):
+        add("X", None, w=keys, sem=sem, inc=nen * len(peers) * calls)
+
+    def dma(qu, out, in_, r, w, sem):
+        e = SY if qu == "Y" else SC
+        add(qu, lambda: e.dma_start(out, in_), r=r, w=w, sem=sem, inc=16, whole=True)
+
+    def vcopy(out, in_, r, w):
+        add("V", lambda: V.tensor_copy(out, in_), r=r, w=w)
+
+    def vts(out, in0, s1, s2, op0, op1, r, w):
+        if op1 is None:
+            add("V", lambda: V.tensor_scalar(out, in0, s1, None, op0), r=r, w=w)
+        else:
+            add("V", lambda: V.tensor_scalar(out, in0, s1, s2, op0, op1), r=r, w=w)
+
+    def vtt(out, a, b, op, r, w):
+        add("V", lambda: V.tensor_tensor(out, a, b, op), r=r, w=w)
+
+    def act(out, in_, func, bias, r, w):
+        add("S", lambda: SC.activation(out, in_, func, bias=bias), r=r, w=w)
+
+    def gather(qu, out, win, off, r, w):
+        if qu == "V":
+            add("V", lambda: V.tensor_copy(out, win.indirect(off)), r=r, w=w)
+        else:
+            add("S", lambda: SC.activation(out, win.indirect(off), AF.Copy), r=r, w=w)
+
+    def conv(bank, z, src, a, r):
+        def fn():
+            for i in range(16):
+                ins = PE.matmul(T[bank][:, 0:64], T[z][:, 15 - i:143 - i], T[src][:, a + i:a + S:16], i == 0, i == 15)
+            return ins
+        add("P", fn, r=r + [z], w=[bank])
+
+    matkeys = {"ID": ["ID"]}
+
+    def mat(l):
+        if l in MATS:
+            m = MATS.index(l)
+            return T.MAT[:, m * 128:(m + 1) * 128]
+        return T[l][:, :]
+
+    def mms(bank, n, terms, start, stop, r):
+        def fn():
+            for j, (l, x) in enumerate(terms):
+                ins = PE.matmul(T[bank][:, 0:n], mat(l), x, start and j == 0, stop and j == len(terms) - 1)
+            return ins
+        add("P", fn, r=r + [k for l, _ in terms for k in matkeys[l]], w=[bank], acc=not start)
+
+    own = q * S
+    hv = [(0, 512), (512, S)]
+    FB, GB, BB, PB = ["F0", "F1", "F2"], ["G0", "G1", "C2"], ["C1", "F1"], ["C0", "C1"]
+    TT = [T.TA, T.TZ]
+
+    def xown(n, a=0, b=S):
+        return T.XT[:, n * W + own + a:n * W + own + b]
+
+    def xkeys(n):
+        return ["X%s%d" % (s, m) for m in range(n + 1) for s in ("a", "b", "r")]
+
+    def build(n):
+        for h, (a, b) in enumerate(hv):
+            mms(BB[h], 512, [("ID", xown(n - 1, a, b)), ("ID", T.U[:, a:b])], True, True, ["X%s%d" % ("ab"[h], n - 1), "U"])
+        for h, (a, b) in enumerate(hv):
+            vts(T.SG[:, a:b], T[BB[h]][:, :], 32.0, -32.0, A.is_ge, A.mult, [BB[h]], ["SG%d" % h])
+        for h, (a, b) in enumerate(hv):
+            vtt(xown(n, a, b), T[BB[h]][:, :], T.SG[:, a:b], A.add, [BB[h], "SG%d" % h], ["X%s%d" % ("ab"[h], n)])
+
+    def cand(t):
+        return T.IN[:, 64 + t * 64:128 + t * 64]
+
+    def statics(t):
+        k = "IN0" if t == 0 else "IN"
+        vtt(T.MN[:, :], cand(t), T.VR[:, :], A.min, [k, "VR"], ["MN"])
+        n = 128
+        if t + 1 < RO:
+            vts(T.J[:, 128:192], cand(t + 1), 6, None, A.arith_shift_right, None, [k], ["J2"])
+            vts(T.J[:, 192:256], cand(t + 1), 63, None, A.bitwise_and, None, [k], ["J3"])
+            n = 256
+        vts(T.J[:, 0:64], T.MN[:, :], 6, None, A.arith_shift_right, None, ["MN"], ["J0"])
+        vts(T.J[:, 64:128], T.MN[:, :], 63, None, A.bitwise_and, None, ["MN"], ["J1"])
+        vcopy(T.SP[:, 0:n], T.J[:, 0:n], ["J0", "J1", "J2", "J3"], ["SP"])
+
+    def lay(t, extra):
+        for p, lane in enumerate([2, 3, 13, 14][:4 if t + 1 < RO else 2]):
+            dma("Y", T.R[lane:128:16, :], T.SP[:, p * 64:(p + 1) * 64], ["SP"] + extra, ["R%d" % p], "dR%d" % t)
+
+    rk = ["R%d" % p for p in range(4)]
+
+    dma("Y", T.IN[:, 0:64], T.link[:, :], [], ["INl"], "ldl")
+    dma("S", T.IN[:, 64:192], T.cand[:, 0:128], [], ["IN0"], "ldl")
+    dma("Y", xown(0), T.x[:, :], [], ["Xa0", "Xb0"], "ldx")
+    add("G", lambda: g.iota(T.PC[:, 0:1], [[1, 1]], 0, 1), w=["PC0"])
+    add("G", lambda: g.iota(T.VAL[:, :], [[1, 144]], 0, 0, allow_small_or_imprecise_dtypes=True), w=["VAL"])
+    r0k = ["R0%d" % p for p in range(6)]
+    add("V", lambda: V.memset(T.R0[:, :], 0.0), w=r0k)
+    vts(T.PC[:, 1:2], T.PC[:, 0:1], 15, None, A.bitwise_and, None, ["PC0"], ["PC1"])
+    vts(T.PC[:, 2:3], T.PC[:, 0:1], 4, None, A.arith_shift_right, None, ["PC0"], ["PC2"])
+    vts(T.CF[:, 1:2], T.PC[:, 1:2], float(own), None, A.add, None, ["PC1"], ["CF1"])
+    vcopy(T.CF[:, 0:1], T.PC[:, 1:2], ["PC1"], ["CF0"])
+    vts(T.VR[:, :], T.VAL[:, 0:64], 16.0, T.CF[:, 1:2], A.mult, A.add, ["VAL", "CF1"], ["VR"])
+    vts(T.CF[:, 2:3], T.PC[:, 1:2], 64.0, None, A.mult, None, ["PC1"], ["CF2"])
+    vts(T.JV[:, 0:64], T.VR[:, :], 6, None, A.arith_shift_right, None, ["VR"], ["JV0"])
+    vts(T.JV[:, 64:128], T.VR[:, :], 63, None, A.bitwise_and, None, ["VR"], ["JV1"])
+    vts(T.PL[:, :], T.VAL[:, 0:64], T.CF[:, 2:3], None, A.add, None, ["VAL", "CF2"], ["PL"])
+    vcopy(T.SV[:, :], T.JV[:, :], ["JV0", "JV1"], ["SV"])
+    dma("Y", T.R0[11:128:16, :], T.SV[:, 0:64], ["SV"], ["R04"], "dself")
+    dma("S", T.R0[12:128:16, :], T.SV[:, 64:128], ["SV"], ["R05"], "dself")
+    add("V", lambda: V.memset(T.R[:, :], 0.0), w=rk)
+    vcopy(T.CF[:, 3:4], T.PC[:, 0:1], ["PC0"], ["CF3"])
+    vcopy(T.CF[:, 4:5], T.PC[:, 2:3], ["PC2"], ["CF4"])
+    vts(T.CF[:, 5:6], T.PC[:, 2:3], 16.0, 15.0, A.mult, A.add, ["PC2"], ["CF5"])
+    vts(T.PC[:, 3:4], T.PC[:, 2:3], 7.0, None, A.add, None, ["PC2"], ["PC3"])
+    vts(T.HI[:, :], T.IN[:, 0:128], 6, None, A.arith_shift_right, None, ["IN0", "INl"], ["HI"])
+    vts(T.LO[:, :], T.IN[:, 0:128], 63, None, A.bitwise_and, None, ["IN0", "INl"], ["LO"])
+    vcopy(T.S0[:, 0:128], T.HI[:, :], ["HI"], ["S0a"])
+    vcopy(T.S0[:, 128:256], T.LO[:, :], ["LO"], ["S0b"])
+    for p, lane in enumerate([0, 13, 3, 14]):
+        dma("YS"[p % 2], T.R0[lane:128:16, :], T.S0[:, p * 64:(p + 1) * 64], ["S0" + "ab"[p // 2]], ["R0%d" % p], "dfirst")
+    send(xown(0), "aX0", "lO", ["Xa0", "Xb0", "S0b"])
+    arrival("aX0", ["Xr0"])
+    act(T.XV[:, :], xown(0), AF.Identity, 0.0, ["Xa0", "Xb0"], ["XV"])
+    vcopy(T.CL[:, 0:128], T.IN[:, 64:192], ["IN0"], ["CL0"])
+    vcopy(T.KL[:, 0:64], T.IN[:, 0:64], ["INl"], ["KLb"])
+    vts(T.OH[:, :], T.VAL[:, 0:16], T.CF[:, 0:1], None, A.is_equal, None, ["VAL", "CF0"], ["OH"])
+    vts(T.ID[:, :], T.VAL[:, 0:128], T.CF[:, 3:4], None, A.is_equal, None, ["VAL", "CF3"], ["ID"])
+    vts(T.PC[:, 4:5], T.PC[:, 3:4], 7, None, A.bitwise_and, None, ["PC3"], ["PC4"])
+    add("V", lambda: V.memset(T.MAT[:, :], 0.0), w=["MAT"])
+    cols = {}
+
+    def col(name):
+        if name not in cols:
+            cols[name] = len(cols)
+        return T.WC[:, cols[name]:cols[name] + 1]
+
+    def oh(l):
+        return T.OH[:, l:l + 1]
+
+    for name, a, b in [("03", 0, 3), ("36", 3, 6), ("68", 6, 8), ("8b", 8, 11), ("6a", 6, 10), ("13", 1, 3), ("46", 4, 6)]:
+        add("V", lambda o=col(name), a=a, b=b: V.tensor_reduce(o, T.OH[:, a:b], AxisListType.X, A.add), r=["OH"], w=["c" + name])
+    vcopy(col("gs"), T.PC[:, 4:5], ["PC4"], ["cgs"])
+    vts(col("a1"), oh(11), 64.0, oh(12), A.mult, A.add, ["OH"], ["ca1"])
+    vts(col("wc"), oh(13), 64.0, oh(14), A.mult, A.add, ["OH"], ["cwc"])
+    vts(col("eh"), col("68"), -64.0, col("03"), A.mult, A.add, ["c68", "c03"], ["ceh"])
+    vts(col("el"), col("68"), -64.0, col("36"), A.mult, A.add, ["c68", "c36"], ["cel"])
+    vts(col("wa"), col("8b"), 4096.0, col("a1"), A.mult, A.add, ["c8b", "ca1"], ["cwa"])
+    vts(col("k0"), oh(0), oh(3), None, A.subtract, None, ["OH"], ["ck0"])
+    vts(col("k1"), oh(1), 64.0, oh(2), A.mult, A.add, ["OH"], ["ck1"])
+    vts(col("wl"), col("eh"), 64.0, col("el"), A.mult, A.add, ["ceh", "cel"], ["cwl"])
+    vts(T.GM[:, 0:8], T.VAL[:, 0:8], T.CF[:, 4:5], None, A.is_equal, None, ["VAL", "CF4"], ["GM0"])
+    vts(T.GM[:, 8:16], T.VAL[:, 0:8], col("gs"), None, A.is_equal, None, ["VAL", "cgs"], ["GM1"])
+    vts(T.GM[:, 16:24], T.VAL[:, 0:8], T.CF[:, 4:5], -1.0, A.is_equal, A.mult, ["VAL", "CF4"], ["GM2"])
+    vts(T.GM[:, 24:32], T.VAL[:, 0:8], T.CF[:, 4:5], 128.0, A.is_equal, A.mult, ["VAL", "CF4"], ["GM3"])
+    vts(col("d1"), oh(13), col("eh"), None, A.subtract, None, ["OH", "ceh"], ["cd1"])
+    vts(col("d4"), oh(14), col("el"), None, A.subtract, None, ["OH", "cel"], ["cd4"])
+    for z, c in [("ZA", "wa"), ("ZC", "wc"), ("ZL", "wl")]:
+        vts(T[z][:, :], T.VAL[:, :], T.CF[:, 5:6], col(c), A.is_equal, A.mult, ["VAL", "CF5", "c" + c], [z])
+    vts(col("wk"), col("k0"), 4096.0, col("k1"), A.mult, A.subtract, ["ck0", "ck1"], ["cwk"])
+    vts(col("bk"), col("k0"), -256.0, None, A.mult, None, ["ck0"], ["cbk"])
+    vts(col("rd"), col("13"), col("46"), None, A.add, None, ["c13", "c46"], ["crd"])
+    vts(col("th"), oh(2), oh(5), THETA, A.add, A.mult, ["OH"], ["cth"])
+    vts(col("f2"), col("6a"), -2.0, None, A.mult, None, ["c6a"], ["cf2"])
+    vts(col("f5"), col("6a"), -5.0, None, A.mult, None, ["c6a"], ["cf5"])
+    vts(col("sb"), col("th"), -1.0, -0.5, A.mult, A.add, ["cth"], ["csb"])
+    vts(col("b1"), col("rd"), -320.0, col("f2"), A.mult, A.add, ["crd", "cf2"], ["cb1"])
+    vts(col("b0"), col("rd"), -704.0, col("f5"), A.mult, A.add, ["crd", "cf5"], ["cb0"])
+    for h, (a, b) in enumerate(hv):
+        gather("VS"[h], T.TA[:, own + a:own + b], T.R0[:, :], T.PL[:, a // 16:b // 16], r0k + ["PL"],
+               [["To00"], ["To01", "To02"]][h])
+    send(T.TA[:, own:own + S], "aT0", "lT0", ["To00", "To01"])
+    arrival("aT0", ["Tr0"])
+    statics(0)
+    lay(0, ["To00", "To01"])
+    dma("Y", T.U[:, :], T.u[:, :], [], ["U"], "ldu")
+    dma("Y", T.IN[:, 192:448], T.cand[:, 128:384], [], ["IN"], "ldc")
+
+    def entries(table):
+        for m, l, c, kind in table:
+            base = MATS.index(m) * 128
+            out, gm = T.MAT[:, base + l:base + 128:16], T.GM[:, 8 * kind:8 * kind + 8]
+            key = "m%s%d" % (m, l)
+            matkeys.setdefault(m, []).append(key)
+            sc, r = (1.0, []) if c is None else (oh(c), ["OH"]) if isinstance(c, int) else (col(c), ["c" + c])
+            add("S", lambda out=out, gm=gm, sc=sc: SC.activation(out, gm, AF.Identity, scale=sc),
+                r=r + ["MAT", "GM%d" % kind], w=[key])
+
+    entries([("BP", 0, None, 0), ("BP", 3, None, 2), ("BM", 0, None, 2), ("BM", 3, None, 0), ("MM", 1, 2, 0), ("MM", 2, 3, 0),
+             ("Be", 2, "eh", 0), ("Be", 5, "el", 0), ("Br", 13, 13, 0), ("Br", 14, 14, 0)])
+    second = [("Bt", 0, "eh", 0), ("Bt", 1, "d1", 0), ("Bt", 2, "eh", 2), ("Bt", 3, "el", 0), ("Bt", 4, "d4", 0),
+              ("Bt", 5, "el", 2), ("Bt", 10, "8b", 0), ("Bt", 11, 11, 0), ("Bt", 12, 12, 0),
+              ("Ao", 0, "wk", 0), ("Ao", 1, "wk", 0), ("Ao", 2, "wk", 0), ("Ao", 3, "wk", 2)]
+    third = [("Ab", 0, "wk", 2), ("Ab", 3, "wk", 0), ("Ab", 4, "wk", 0), ("Ab", 5, "wk", 0),
+             ("Ad", 1, "wk", 2), ("Ae", 4, "wk", 2),
+             ("Bs", 1, "03", 3), ("Bs", 4, "03", 3), ("Bs", 2, "36", 3), ("Bs", 5, "36", 3),
+             ("Bs", 6, "03", 0), ("Bs", 7, "36", 0), ("Bs", 8, "03", 1), ("Bs", 9, "36", 1)]
+
+    for t in range(RO):
+        first = t == 0
+        u, un = t % 2, (t + 1) % 2
+        tn = "TA" if un == 0 else "TZ"
+        tw = TT[u][:, :]
+        tk = ["To%d0" % u, "To%d1" % u, "To%d2" % u, "Tr%d" % u]
+        xw = T.XT[:, 0:(t + 1) * W]
+        xk = xkeys(t)
+        xvk = ["XV"]
+        lists = {"AC": (T.AC, 0, "AC"), "AB": (T.AB, 0, "AB"), "AD": (T.AD, 0, "AD")}
+        if first:
+            lists = {"AC": (T.CL, 0, "CL0"), "AB": (T.KL, 0, "KLb"), "AD": (T.KL, 64, "KLd")}
+
+        def xv(a, b):
+            return T.XV[:, a:b]
+
+        def off(name, a, b):
+            buf, o, _ = lists[name]
+            return buf[:, o + a // 16:o + b // 16]
+
+        def gmax(m, other, a, b, r, key):
+            vtt(T[m][:, a:b], xw.indirect(off("AC", a, b)), other, A.max, xk + [lists["AC"][2]] + r, [key])
+
+        def bmax(m, other, a, b, r, key):
+            h = a // 512
+            vtt(T[m][:, a:b], T[PB[h]][:, a - 512 * h:b - 512 * h], other, A.max, [PB[h]] + r, [key])
+
+        def xgather(buf, name, h):
+            a, b = hv[h]
+            gather("S", T[buf][:, a:b], xw, off(name, a, b), xk + [lists[name][2]], ["%s%d" % (buf, h)])
+            if buf == "XB":
+                mms(PB[h], 512, [("ID", T.XB[:, a:b])], True, True, ["XB%d" % h])
+
+        def look(buf, lst, o, key, cut=512):
+            for h, (a, b) in enumerate([(0, cut), (cut, S)]):
+                gather("VS"[h], T[buf][:, a:b], tw, lst[:, o + a // 16:o + b // 16], tk + [key], ["%s%d" % (buf, h)])
+
+        def send_x():
+            send(xown(t + 1), "aX%d" % (t + 1), "lO", ["Xa%d" % (t + 1), "Xb%d" % (t + 1), "Tr%d" % u])
+            arrival("aX%d" % (t + 1), ["Xr%d" % (t + 1)])
+
+        tc, tb = ["TC0", "TC1"], ["TB0", "TB1"]
+        m3 = ["M3%d" % c for c in range(4)]
+        if first:
+            for h, (a, b) in enumerate(hv):
+                gmax("M3", xv(a, b), a, b, xvk, m3[2 * h])
+                xgather("XB", "AB", h)
+            for h, (a, b) in enumerate(hv):
+                bmax("M1", xv(a, b), a, b, xvk, "M1%d" % h)
+            m3 = [m3[0], m3[0], m3[2], m3[2]]
+            entries(second)
+        elif t + 1 < RO:
+            send_x()
+        look("TC", T.CL, t * 64, "CL0" if t < 2 else "CL")
+        look("TB", T.KL, 0, "KLb")
+        conv("G1", "ZL", "TC", 0, tc)
+        if not first:
+            conv("G0", "ZA", "TC", 0, tc)
+        vcopy(T.KL[:, 64:128], T.G1[:, 0:64], ["G1"], ["KLd"])
+        if first:
+            gather("V", T.RS[:, 0:512], T.R[:, :], T.PL[:, 0:32], rk + ["PL"], ["RS0"])
+            xgather("XD", "AD", 0)
+            xgather("XD", "AD", 1)
+            conv("G0", "ZC", "TB", 0, tb)
+        else:
+            look("TD", T.KL, 64, "KLd", cut=TDCUT)
+            vcopy(T.AC[:, :], T.G0[:, 0:64], ["G0"], ["AC"])
+            conv("C2", "ZA", "TB", 0, tb)
+            conv("G1", "ZA", "TD", 0, ["TD0", "TD1"])
+            gmax("M3", xv(0, 256), 0, 256, xvk, m3[0])
+            vcopy(T.AB[:, :], T.C2[:, 0:64], ["C2"], ["AB"])
+            xgather("XB", "AB", 0)
+            gmax("M3", xv(256, 512), 256, 512, xvk, m3[1])
+            gmax("M3", xv(512, 768), 512, 768, xvk, m3[2])
+            vcopy(T.AD[:, :], T.G1[:, 0:64], ["G1"], ["AD"])
+            xgather("XD", "AD", 0)
+            conv("G0", "ZC", "TB", 0, tb)
+            gmax("M3", xv(768, S), 768, S, xvk, m3[3])
+            bmax("M1", xv(0, 512), 0, 512, xvk, "M10")
+        mms("F0", 512, [("BM", T.M3[:, 0:512]), ("BP", T.M1[:, 0:512])], True, False, m3[0:2] + ["M10"])
+        if first:
+            gather("S", T.RS[:, 512:S], T.R[:, :], T.PL[:, 32:64], rk + ["PL"], ["RS1"])
+        mms("F0", 512, [("MM", T.RS[:, 0:512])], False, False, ["RS0"])
+        if not first:
+            xgather("XB", "AB", 1)
+            xgather("XD", "AD", 1)
+        for c, (a, b) in enumerate(CHUNKS):
+            h = a // 512
+            if c == 1:
+                if not first:
+                    bmax("M1", xv(512, S), 512, S, xvk, "M11")
+                for c2 in (1, 2):
+                    a2, b2 = CHUNKS[c2]
+                    mms(FB[c2], b2 - a2, [("BM", T.M3[:, a2:b2]), ("MM", T.RS[:, a2:b2]), ("BP", T.M1[:, a2:b2])], True, False,
+                        [m3[c2 + 1], "RS1", "M11"])
+            gmax("M2", T.XD[:, a:b], a, b, ["XD%d" % h], "M2%d" % c)
+            mms(FB[c], b - a, [("BP", T.M2[:, a:b])], False, False, ["M2%d" % c])
+            bmax("M4", T.XD[:, a:b], a, b, ["XD%d" % h], "M4%d" % c)
+            mms(FB[c], b - a, [("BM", T.M4[:, a:b])], False, True, ["M4%d" % c])
+            ko = T.KK[:, own + a:own + b]
+            if c < 2:
+                act(ko, T[FB[c]][:, 0:b - a], AF.Relu, col("bk"), [FB[c], "cbk"], ["Ko%d" % c])
+            else:
+                vcopy(T.LCB[:, :], T.G0[:, 0:64], ["G0"], ["LCB"])
+                vts(ko, T[FB[c]][:, 0:b - a], col("bk"), 0.0, A.add, A.max, [FB[c], "cbk"], ["Ko%d" % c])
+            if c == 0:
+                send(ko, "aK%d" % t, "lK0", ["Ko0"])
+        send(T.KK[:, own + 512:own + S], "aK%d" % t, "lK1", ["Ko1", "Ko2"])
+        arrival("aK%d" % t, ["Kr"], calls=2)
+        kk = ["Ko0", "Ko1", "Ko2"]
+        look("TE", T.LCB, 0, "LCB")
+        if first:
+            build(1)
+            send_x()
+            entries(third)
+        conv("C0", "ZL", "TE", 0, ["TE0", "TE1"])
+        vcopy(T.KL[:, 128:192], T.C0[:, 0:64], ["C0"], ["KLe"])
+        for c, (a, b) in enumerate(CHUNKS):
+            mms(FB[c], b - a, [("Ao", T.KK[:, own + a:own + b])], True, False, ["Ko%d" % c])
+        for c, (a, b) in enumerate(CHUNKS):
+            h = a // 512
+            terms = [("Bt", TT[u][:, own + a:own + b]), ("Be", T.TE[:, a:b])]
+            if t + 1 < RO:
+                terms += [("Br", T.RS[:, a:b])]
+            mms(GB[c], b - a, terms, True, False, ["TE%d" % h, "To%d%d" % (u, c), "RS%d" % h])
+        if first:
+            vcopy(T.CL[:, 128:384], T.IN[:, 192:448], ["IN"], ["CL"])
+        if t + 1 < RO:
+            statics(t + 1)
+            lay(t + 1, ["Kr"])
+        kw = T.KK[:, :]
+        kr = kk + ["Kr"]
+        for qu, j, h in [("V", 0, 0), ("S", 1, 0), ("V", 2, 0), ("S", 1, 1), ("V", 0, 1), ("S", 2, 1)]:
+            a, b = hv[h]
+            gather(qu, T.GK[:, j * S + a:j * S + b], kw, T.KL[:, j * 64 + a // 16:j * 64 + b // 16],
+                   kr + ["KL" + "bde"[j]], ["GK%d%d" % (j, h)])
+            if h == 0:
+                mms("F0", 512, [("A" + "bde"[j], T.GK[:, j * S:j * S + 512])], False, j == 2, ["GK%d0" % j])
+            elif j == 1:
+                for c in (1, 2):
+                    a, b = CHUNKS[c]
+                    mms(FB[c], b - a, [("Ad", T.GK[:, S + a:S + b])], False, False, ["GK11"])
+        for c in (1, 2):
+            a, b = CHUNKS[c]
+            mms(FB[c], b - a, [("Ab", T.GK[:, a:b]), ("Ae", T.GK[:, 2 * S + a:2 * S + b])], False, True, ["GK01", "GK21"])
+        to = ["To%d%d" % (un, c) for c in range(3)]
+        vts(T.SN[:, 0:512], T.F0[:, :], col("th"), 2.0, A.is_gt, A.mult, ["F0", "cth"], ["SN0"])
+        for c in (1, 2):
+            a, b = CHUNKS[c]
+            act(T.SN[:, a:b], T[FB[c]][:, 0:b - a], AF.Sign, col("sb"), [FB[c], "csb"], ["SN%d" % c])
+        for c, (a, b) in enumerate(CHUNKS):
+            mms(GB[c], b - a, [("Bs", T.SN[:, a:b])], False, True, ["SN%d" % c])
+        vts(TT[un][:, own:own + 512], T.G0[:, :], col("b0"), 0.0, A.add, A.max, ["G0", "cb0"], [to[0]])
+        for c in (1, 2):
+            a, b = CHUNKS[c]
+            act(TT[un][:, own + a:own + b], T[GB[c]][:, 0:b - a], AF.Relu, col("b1"), [GB[c], "cb1"], [to[c]])
+        if t + 1 == RO:
+            conv("C0", "ZL", tn, own, to)
+            vcopy(T.Y[:, :], T.C0[:, 0:64], ["C0"], ["Y"])
+            dma("Y", T.ylink[:, :], T.Y[:, :], ["Y"], ["y"], "out")
+            break
+        send(TT[un][:, own:own + S], "aT%d" % (t + 1), "lT%d" % un, to)
+        arrival("aT%d" % (t + 1), ["Tr%d" % un])
+        conv("F2", "ZA", tn, own, to)
+        conv("C0", "ZL", tn, own, to)
+        gather("S", T.RS[:, :], T.R[:, :], T.PL[:, :], rk + ["PL"], ["RS0", "RS1"])
+        vcopy(T.AV[:, :], T.F2[:, 0:64], ["F2"], ["AV"])
+        vcopy(T.KL[:, 0:64], T.C0[:, 0:64], ["C0"], ["KLb"])
+        gather("S", T.XV[:, :], T.XT[:, 0:(t + 2) * W], T.AV[:, :], xkeys(t + 1) + ["AV"], ["XV"])
+        if t + 2 < RO:
+            build(t + 2)
+
+    emit({"G": g, "V": V, "S": SC, "P": PE, "Y": SY}, T)

@@ -2,36 +2,47 @@ from concourse.bass import DstId, RemoteDMATransfer
 from concourse.mybir import AluOpType as A, ActivationFunctionType as AF, AxisListType
 
 RO, S, W, N = 6, 1024, 4096, 4
+H = S // 2
 BF, F32, I32, U16 = "bfloat16", "float32", "int32", "uint16"
-THETA = -256.0 * 4096.0
-CHUNKS = [(0, 512), (512, 768), (768, 1024)]
-TDCUT = 384
-MATS = ["BP", "BM", "MM", "Ao", "Ab", "Ad", "Ae", "Bs", "Be", "Bt", "Br"]
+CHUNKS = {"A": (0, 512), "B": (512, 768), "C": (768, 1024), "D": (512, 1024)}
+CUT = 512
+MATS = ["BP", "BM", "MM", "Kd", "Ao", "Ab", "Ad", "Ae", "Bc", "Bt", "Bs"]
+
+GAIN0 = ("m3:512:1024 xb:D:S pb:B m3:0:512 xb:A:S m1:B tc n4:C s:3:B pb:A n1:C s:3:A s:3:C cd s:5:C m1:A r1:C:S s:5:A kd "
+         "xd:A:S s:1:C s:5:B rs s:0:A m4:A m2:A xd:B:S s:1:A s:4:A s:2:A xd:C:S s:0:B s:0:C m2:B m2:C d4:C s:1:B r4:C:V "
+         "ko:A:S send0 s:4:C m4:B s:4:B s:2:C s:2:B ko:C:V ko:B:V send1")
+GAIN = ("tc lay cd xb:A:S s:5:A kd m3:0:512 xd:A:S xb:D:S pb:A m1:A s:5:C xd:B:S xd:C:S s:5:B m2:A s:3:A s:1:A pb:B m4:A "
+        "m3:512:1024 n1:C s:2:A s:4:A m1:B r1:C:S ko:A:S send0 n4:C s:3:B m2:B d4:C s:1:C s:3:C s:1:B m4:B r4:C:S s:2:B "
+        "s:4:B ko:B:S s:4:C m2:C s:2:C ko:C:V send1")
+DECIDE = ("V:b:0:256 S:b:256:512 df V:b:512:768 S:b:768:1024 ce V:d:0:512 S:d:512:1024 le V:e:0:256 S:e:256:512 "
+          "V:e:512:768 S:e:768:1024 s:0 o:0:S s:1 o:1:V")
 
 SCRATCH = {
-    "XT": ("sbuf", [128, RO * W], BF), "TA": ("sbuf", [128, W], BF), "TZ": ("sbuf", [128, W], BF), "KK": ("sbuf", [128, W], BF),
-    "U": ("sbuf", [128, S], BF), "SG": ("sbuf", [128, S], BF), "SN": ("sbuf", [128, S], BF),
-    "TC": ("sbuf", [128, S], BF), "TB": ("sbuf", [128, S], BF), "TD": ("sbuf", [128, S], BF), "TE": ("sbuf", [128, S], BF),
-    "XV": ("sbuf", [128, S], BF), "XB": ("sbuf", [128, S], BF), "XD": ("sbuf", [128, S], BF),
+    "XX": ("sbuf", [128, 2 * (S + W)], BF), "KK": ("sbuf", [128, W], BF),
+    "T0": ("sbuf", [128, W], BF), "TA": ("sbuf", [128, W // 2], BF), "TZ": ("sbuf", [128, W // 2], BF),
+    "U": ("sbuf", [128, S], BF), "SG": ("sbuf", [128, S], BF), "SN": ("sbuf", [128, H], BF),
+    "TC": ("sbuf", [128, S], BF), "MK": ("sbuf", [128, S], BF), "XV": ("sbuf", [128, S], BF), "XB": ("sbuf", [128, S], BF), "XD": ("sbuf", [128, S], BF),
     "M1": ("sbuf", [128, S], BF), "M2": ("sbuf", [128, S], BF), "M3": ("sbuf", [128, S], BF), "M4": ("sbuf", [128, S], BF),
     "GK": ("sbuf", [128, 3 * S], BF),
-    "R0": ("sbuf", [128, S], BF), "R": ("sbuf", [128, S], BF), "RS": ("sbuf", [128, S], BF),
-    "IN": ("sbuf", [128, 7 * 64], I32), "HI": ("sbuf", [128, 128], I32), "LO": ("sbuf", [128, 128], I32),
-    "S0": ("sbuf", [128, 256], BF), "SV": ("sbuf", [128, 128], BF), "SP": ("sbuf", [128, 256], BF),
-    "CL": ("sbuf", [128, RO * 64], U16), "KL": ("sbuf", [128, 192], U16), "PL": ("sbuf", [128, 64], U16),
-    "LCB": ("sbuf", [128, 64], U16),
-    "AV": ("sbuf", [128, 64], U16), "AB": ("sbuf", [128, 64], U16), "AC": ("sbuf", [128, 64], U16), "AD": ("sbuf", [128, 64], U16),
-    "Y": ("sbuf", [128, 64], F32), "MN": ("sbuf", [128, 64], I32), "J": ("sbuf", [128, 256], I32), "JV": ("sbuf", [128, 128], I32),
-    "VAL": ("sbuf", [128, 144], F32), "PC": ("sbuf", [128, 8], I32), "CF": ("sbuf", [128, 8], F32),
-    "OH": ("sbuf", [128, 16], F32), "GM": ("sbuf", [128, 32], F32), "WC": ("sbuf", [128, 32], F32), "VR": ("sbuf", [128, 64], I32),
-    "ZL": ("sbuf", [128, 144], BF), "ZA": ("sbuf", [128, 144], BF), "ZC": ("sbuf", [128, 144], BF),
-    "MAT": ("sbuf", [128, len(MATS) * 128], BF), "ID": ("sbuf", [128, 128], BF),
+    "R0": ("sbuf", [128, S], BF), "R": ("sbuf", [128, 2 * S], BF), "RA": ("sbuf", [128, S], BF), "RZ": ("sbuf", [128, S], BF),
+    "IN": ("sbuf", [128, 7 * 64], I32), "HL": ("sbuf", [128, 320], I32),
+    "S0": ("sbuf", [128, 128], BF), "SV": ("sbuf", [128, 128], BF), "SP": ("sbuf", [128, 2, 320], BF),
+    "CL": ("sbuf", [128, 384], U16), "CH": ("sbuf", [128, 384], U16), "KL": ("sbuf", [128, 192], U16),
+    "PL": ("sbuf", [128, 64], U16), "AV": ("sbuf", [128, 64], U16),
+    "Y": ("sbuf", [128, 64], F32), "MN": ("sbuf", [128, 64], I32), "J": ("sbuf", [128, 320], I32), "JV": ("sbuf", [128, 128], I32),
+    "VAL": ("sbuf", [128, 144], F32), "V8": ("sbuf", [128, 128], F32), "PC": ("sbuf", [128, 8], I32), "CF": ("sbuf", [128, 16], F32),
+    "OH": ("sbuf", [128, 16], F32), "O8": ("sbuf", [128, 8], F32), "GM": ("sbuf", [128, 48], F32), "WC": ("sbuf", [128, 32], F32),
+    "VR": ("sbuf", [128, 64], I32),
+    "ZL": ("sbuf", [128, 144], BF), "ZE": ("sbuf", [128, 144], BF), "ZF": ("sbuf", [128, 144], BF),
+    "ZV0": ("sbuf", [128, 144], BF), "ZV1": ("sbuf", [128, 144], BF),
+    "MAT": ("sbuf", [128, len(MATS) * 128], BF), "ID": ("sbuf", [128, 128], BF), "NI": ("sbuf", [128, 128], BF),
+    "Mk": ("sbuf", [128, 128], BF), "Ma": ("sbuf", [128, 128], BF), "Mb": ("sbuf", [128, 128], BF),
     "F0": ("psum", [128, 512], F32), "F1": ("psum", [128, 512], F32), "F2": ("psum", [128, 512], F32),
-    "G0": ("psum", [128, 512], F32), "G1": ("psum", [128, 512], F32),
-    "C0": ("psum", [128, 512], F32), "C1": ("psum", [128, 512], F32), "C2": ("psum", [128, 512], F32),
+    "P0": ("psum", [128, 512], F32), "P1": ("psum", [128, 512], F32), "P2": ("psum", [128, 512], F32),
+    "C0": ("psum", [128, 512], F32), "C1": ("psum", [128, 512], F32),
 }
 PSUM = [k for k, v in SCRATCH.items() if v[0] == "psum"]
-SEMAPHORES = (["sV", "sS", "sP", "sG", "ldl", "ldc", "ldx", "ldu", "dself", "dfirst", "out", "lK0", "lK1", "lT0", "lT1", "lO"]
+SEMAPHORES = (["sV", "sS", "sP", "sG", "ldl", "ldc", "ldx", "ldu", "dfirst", "out", "lK0", "lK1", "lT0", "lT1", "lTf", "lX0", "lX1"]
               + ["%s%d" % (n, t) for n in ("aX", "aK", "aT", "dR") for t in range(RO)])
 
 
@@ -130,8 +141,11 @@ def rank_program(g, core, T, topo):
     def vtt(out, a, b, op, r, w):
         add("V", lambda: V.tensor_tensor(out, a, b, op), r=r, w=w)
 
-    def act(out, in_, func, bias, r, w):
-        add("S", lambda: SC.activation(out, in_, func, bias=bias), r=r, w=w)
+    def relu(qu, out, in_, bias, r, w):
+        if qu == "V":
+            vts(out, in_, bias, 0.0, A.add, A.max, r, w)
+        else:
+            add("S", lambda: SC.activation(out, in_, AF.Relu, bias=bias), r=r, w=w)
 
     def gather(qu, out, win, off, r, w):
         if qu == "V":
@@ -146,100 +160,135 @@ def rank_program(g, core, T, topo):
             return ins
         add("P", fn, r=r + [z], w=[bank])
 
-    matkeys = {"ID": ["ID"]}
+    def conv2(bank, z, src, r, start=True):
+        def fn():
+            for m in range(8):
+                ins = PE.matmul(T[bank][:, 0:64], T[z][:, 14 - 2 * m:142 - 2 * m], T[src][:, q * H + m:(q + 1) * H:8],
+                                start and m == 0, m == 7)
+            return ins
+        add("P", fn, r=r + [z], w=[bank], acc=not start)
 
-    def mat(l):
+    matkeys = {"ID": ["ID"], "NI": ["NI"], "Mk": ["Mk"]}
+
+    def mat(l, up=0):
         if l in MATS:
             m = MATS.index(l)
-            return T.MAT[:, m * 128:(m + 1) * 128]
+            return T.MAT[:, m * 128 - up:(m + 1) * 128 - up]
         return T[l][:, :]
 
-    def mms(bank, n, terms, start, stop, r):
+    def mms(bank, n, terms, start, stop, r, o=0):
         def fn():
-            for j, (l, x) in enumerate(terms):
-                ins = PE.matmul(T[bank][:, 0:n], mat(l), x, start and j == 0, stop and j == len(terms) - 1)
+            for j, (l, x, up) in enumerate(terms):
+                ins = PE.matmul(T[bank][:, o:o + n], mat(l, up), x, start and j == 0, stop and j == len(terms) - 1)
             return ins
-        add("P", fn, r=r + [k for l, _ in terms for k in matkeys[l]], w=[bank], acc=not start)
+        add("P", fn, r=r + [k for l, _, _ in terms for k in matkeys[l]], w=[bank], acc=not start)
+
+    def pairs(l, buf, a, b):
+        return [(l, buf[:, a:b:2], 0), (l, buf[:, a + 1:b:2], 8)]
 
     own = q * S
     hv = [(0, 512), (512, S)]
-    FB, GB, BB, PB = ["F0", "F1", "F2"], ["G0", "G1", "C2"], ["C1", "F1"], ["C0", "C1"]
-    TT = [T.TA, T.TZ]
+    FB = {"A": "F0", "B": "F1", "C": "F2"}
+    R1B, R4B = {"C": "P1", "D": "P2"}, {"B": "P1", "C": "C1"}
+    BB, DB, GB = ["C0", "C1"], ["F0", "F1"], ["P0", "P1"]
+    PART = [(0, CUT), (CUT, S)]
+    TT, RR = [T.TA, T.TZ], [T.RA, T.RZ]
+    XAT, NXAT = [S, S + W], [0, S + 2 * W]
+
+    def keys(name, a, b):
+        return ["%s%d" % (name, k) for k in range(a // 128, (b + 127) // 128)]
 
     def xown(n, a=0, b=S):
-        return T.XT[:, n * W + own + a:n * W + own + b]
+        return T.XX[:, XAT[n % 2] + own + a:XAT[n % 2] + own + b]
 
-    def xkeys(n):
-        return ["X%s%d" % (s, m) for m in range(n + 1) for s in ("a", "b", "r")]
+    def xk(n, a=0, b=S):
+        return keys("X%d" % (n % 2), a, b)
 
     def build(n):
         for h, (a, b) in enumerate(hv):
-            mms(BB[h], 512, [("ID", xown(n - 1, a, b)), ("ID", T.U[:, a:b])], True, True, ["X%s%d" % ("ab"[h], n - 1), "U"])
+            mms(BB[h], 512, [("ID", xown(n, a, b), 0), ("ID", T.U[:, a:b], 0)], True, True, xk(n, a, b) + ["U"])
         for h, (a, b) in enumerate(hv):
             vts(T.SG[:, a:b], T[BB[h]][:, :], 32.0, -32.0, A.is_ge, A.mult, [BB[h]], ["SG%d" % h])
-        for h, (a, b) in enumerate(hv):
-            vtt(xown(n, a, b), T[BB[h]][:, :], T.SG[:, a:b], A.add, [BB[h], "SG%d" % h], ["X%s%d" % ("ab"[h], n)])
+            vtt(T.XX[:, NXAT[n % 2] + a:NXAT[n % 2] + b], T[BB[h]][:, :], T.SG[:, a:b], A.add, [BB[h], "SG%d" % h],
+                ["N%d%d" % (n % 2, h)])
 
     def cand(t):
         return T.IN[:, 64 + t * 64:128 + t * 64]
 
     def statics(t):
-        k = "IN0" if t == 0 else "IN"
+        k = "IN0" if t < 2 else "IN"
         vtt(T.MN[:, :], cand(t), T.VR[:, :], A.min, [k, "VR"], ["MN"])
-        n = 128
-        if t + 1 < RO:
-            vts(T.J[:, 128:192], cand(t + 1), 6, None, A.arith_shift_right, None, [k], ["J2"])
-            vts(T.J[:, 192:256], cand(t + 1), 63, None, A.bitwise_and, None, [k], ["J3"])
-            n = 256
+        vts(T.J[:, 128:192], cand(t), 6, None, A.arith_shift_right, None, [k], ["J2"])
+        vts(T.J[:, 192:256], cand(t), 1, 31, A.arith_shift_right, A.bitwise_and, [k], ["J3"])
+        vts(T.J[:, 256:320], cand(t), 1, None, A.bitwise_and, None, [k], ["J4"])
         vts(T.J[:, 0:64], T.MN[:, :], 6, None, A.arith_shift_right, None, ["MN"], ["J0"])
         vts(T.J[:, 64:128], T.MN[:, :], 63, None, A.bitwise_and, None, ["MN"], ["J1"])
-        vcopy(T.SP[:, 0:n], T.J[:, 0:n], ["J0", "J1", "J2", "J3"], ["SP"])
+        vcopy(T.SP[:, t % 2, :], T.J[:, :], ["J%d" % p for p in range(5)], ["SP%d" % (t % 2)])
+
+    def rk(t):
+        return ["R%d%d" % (t % 2, p) for p in range(5)]
 
     def lay(t, extra):
-        for p, lane in enumerate([2, 3, 13, 14][:4 if t + 1 < RO else 2]):
-            dma("Y", T.R[lane:128:16, :], T.SP[:, p * 64:(p + 1) * 64], ["SP"] + extra, ["R%d" % p], "dR%d" % t)
+        for p, lane in enumerate([2, 3, 13, 14, 15]):
+            dma("Y", T.R[lane:128:16, t % 2 * S:(t % 2 + 1) * S], T.SP[:, t % 2, p * 64:(p + 1) * 64], ["SP%d" % (t % 2)] + extra,
+                [rk(t)[p]], "dR%d" % t)
 
-    rk = ["R%d" % p for p in range(4)]
+    def order_lanes(t, cut=0):
+        for qu, a, b in [("V", 0, cut), ("S", cut, S)]:
+            if a < b:
+                gather(qu, RR[t % 2][:, a:b], T.R[:, t % 2 * S:(t % 2 + 1) * S], T.PL[:, a // 16:b // 16], rk(t) + ["PL"],
+                       keys("RS%d" % (t % 2), a, b))
+
+    def open_sums(t):
+        add("S", lambda: SC.activation(T.XV[:, :], xown(t), AF.Copy), r=xk(t), w=["XV"])
+        for c in "ABC" if t else "":
+            a, b = CHUNKS[c]
+            mms(FB[c], b - a, [("MM", RR[t % 2][:, a:b], 0)], True, False, keys("RS%d" % (t % 2), a, b))
+        for c in R1B:
+            if "n1:" + c in (GAIN if t else GAIN0).split():
+                a, b = CHUNKS[c]
+                mms(R1B[c], b - a, [("ID", xown(t, a, b), 0)], True, False, xk(t, a, b))
 
     dma("Y", T.IN[:, 0:64], T.link[:, :], [], ["INl"], "ldl")
-    dma("S", T.IN[:, 64:192], T.cand[:, 0:128], [], ["IN0"], "ldl")
-    dma("Y", xown(0), T.x[:, :], [], ["Xa0", "Xb0"], "ldx")
+    dma("Y", xown(0), T.x[:, :], [], xk(0), "ldx")
+    dma("Y", T.IN[:, 64:192], T.cand[:, 0:128], [], ["IN0"], "ldc")
     add("G", lambda: g.iota(T.PC[:, 0:1], [[1, 1]], 0, 1), w=["PC0"])
     add("G", lambda: g.iota(T.VAL[:, :], [[1, 144]], 0, 0, allow_small_or_imprecise_dtypes=True), w=["VAL"])
-    r0k = ["R0%d" % p for p in range(6)]
-    add("V", lambda: V.memset(T.R0[:, :], 0.0), w=r0k)
-    vts(T.PC[:, 1:2], T.PC[:, 0:1], 15, None, A.bitwise_and, None, ["PC0"], ["PC1"])
-    vts(T.PC[:, 2:3], T.PC[:, 0:1], 4, None, A.arith_shift_right, None, ["PC0"], ["PC2"])
-    vts(T.CF[:, 1:2], T.PC[:, 1:2], float(own), None, A.add, None, ["PC1"], ["CF1"])
-    vcopy(T.CF[:, 0:1], T.PC[:, 1:2], ["PC1"], ["CF0"])
-    vts(T.VR[:, :], T.VAL[:, 0:64], 16.0, T.CF[:, 1:2], A.mult, A.add, ["VAL", "CF1"], ["VR"])
-    vts(T.CF[:, 2:3], T.PC[:, 1:2], 64.0, None, A.mult, None, ["PC1"], ["CF2"])
-    vts(T.JV[:, 0:64], T.VR[:, :], 6, None, A.arith_shift_right, None, ["VR"], ["JV0"])
-    vts(T.JV[:, 64:128], T.VR[:, :], 63, None, A.bitwise_and, None, ["VR"], ["JV1"])
-    vts(T.PL[:, :], T.VAL[:, 0:64], T.CF[:, 2:3], None, A.add, None, ["VAL", "CF2"], ["PL"])
-    vcopy(T.SV[:, :], T.JV[:, :], ["JV0", "JV1"], ["SV"])
-    dma("Y", T.R0[11:128:16, :], T.SV[:, 0:64], ["SV"], ["R04"], "dself")
-    dma("S", T.R0[12:128:16, :], T.SV[:, 64:128], ["SV"], ["R05"], "dself")
-    add("V", lambda: V.memset(T.R[:, :], 0.0), w=rk)
-    vcopy(T.CF[:, 3:4], T.PC[:, 0:1], ["PC0"], ["CF3"])
-    vcopy(T.CF[:, 4:5], T.PC[:, 2:3], ["PC2"], ["CF4"])
-    vts(T.CF[:, 5:6], T.PC[:, 2:3], 16.0, 15.0, A.mult, A.add, ["PC2"], ["CF5"])
-    vts(T.PC[:, 3:4], T.PC[:, 2:3], 7.0, None, A.add, None, ["PC2"], ["PC3"])
-    vts(T.HI[:, :], T.IN[:, 0:128], 6, None, A.arith_shift_right, None, ["IN0", "INl"], ["HI"])
-    vts(T.LO[:, :], T.IN[:, 0:128], 63, None, A.bitwise_and, None, ["IN0", "INl"], ["LO"])
-    vcopy(T.S0[:, 0:128], T.HI[:, :], ["HI"], ["S0a"])
-    vcopy(T.S0[:, 128:256], T.LO[:, :], ["LO"], ["S0b"])
-    for p, lane in enumerate([0, 13, 3, 14]):
-        dma("YS"[p % 2], T.R0[lane:128:16, :], T.S0[:, p * 64:(p + 1) * 64], ["S0" + "ab"[p // 2]], ["R0%d" % p], "dfirst")
-    send(xown(0), "aX0", "lO", ["Xa0", "Xb0", "S0b"])
-    arrival("aX0", ["Xr0"])
-    act(T.XV[:, :], xown(0), AF.Identity, 0.0, ["Xa0", "Xb0"], ["XV"])
-    vcopy(T.CL[:, 0:128], T.IN[:, 64:192], ["IN0"], ["CL0"])
-    vcopy(T.KL[:, 0:64], T.IN[:, 0:64], ["INl"], ["KLb"])
-    vts(T.OH[:, :], T.VAL[:, 0:16], T.CF[:, 0:1], None, A.is_equal, None, ["VAL", "CF0"], ["OH"])
-    vts(T.ID[:, :], T.VAL[:, 0:128], T.CF[:, 3:4], None, A.is_equal, None, ["VAL", "CF3"], ["ID"])
-    vts(T.PC[:, 4:5], T.PC[:, 3:4], 7, None, A.bitwise_and, None, ["PC3"], ["PC4"])
+    add("G", lambda: g.iota(T.V8[:, :], [[1, 16], [0, 8]], 0, 0, allow_small_or_imprecise_dtypes=True), w=["V8"])
+    add("V", lambda: V.memset(T.R0[:, :], 0.0), w=["Rf0", "Rf1"])
+
+    def cf(j):
+        return T.CF[:, j:j + 1]
+
+    def pc(j):
+        return T.PC[:, j:j + 1]
+
+    vts(pc(1), pc(0), 15, None, A.bitwise_and, None, ["PC0"], ["PC1"])
+    vts(pc(2), pc(0), 4, None, A.arith_shift_right, None, ["PC0"], ["PC2"])
+    vts(pc(3), pc(0), 3, None, A.arith_shift_right, None, ["PC0"], ["PC3"])
+    vts(pc(4), pc(0), 7, None, A.bitwise_and, None, ["PC0"], ["PC4"])
+    vts(pc(5), pc(0), 3, 1, A.arith_shift_right, A.bitwise_and, ["PC0"], ["PC5"])
+    vts(pc(6), pc(0), 112.0, None, A.add, None, ["PC0"], ["PC6"])
+    vcopy(T.CF[:, 0:6], T.PC[:, 0:6], ["PC%d" % j for j in range(6)], ["CF"])
+    vts(pc(7), pc(6), 112, None, A.bitwise_and, None, ["PC6"], ["PC7"])
+    vts(cf(6), cf(1), 64.0, None, A.mult, None, ["CF"], ["CF6"])
+    vts(cf(7), cf(1), float(own), None, A.add, None, ["CF"], ["CF7"])
+    vts(T.OH[:, :], T.VAL[:, 0:16], cf(1), None, A.is_equal, None, ["VAL", "CF"], ["OH"])
+    vts(T.O8[:, :], T.VAL[:, 0:8], cf(4), None, A.is_equal, None, ["VAL", "CF"], ["O8"])
+    vts(T.PL[:, :], T.VAL[:, 0:64], cf(6), None, A.add, None, ["VAL", "CF6"], ["PL"])
+    vts(T.VR[:, :], T.VAL[:, 0:64], 16.0, cf(7), A.mult, A.add, ["VAL", "CF7"], ["VR"])
+    vts(T.GM[:, 0:8], T.VAL[:, 0:8], cf(2), None, A.is_equal, None, ["VAL", "CF"], ["GM0"])
+    vts(T.GM[:, 8:16], T.VAL[:, 0:8], cf(2), -1.0, A.is_equal, A.mult, ["VAL", "CF"], ["GM1"])
     add("V", lambda: V.memset(T.MAT[:, :], 0.0), w=["MAT"])
+    vts(T.HL[:, 0:64], T.IN[:, 0:64], 6, None, A.arith_shift_right, None, ["INl"], ["HI"])
+    vts(T.HL[:, 64:128], T.IN[:, 0:64], 63, None, A.bitwise_and, None, ["INl"], ["LO"])
+    vcopy(T.S0[:, :], T.HL[:, 0:128], ["HI", "LO"], ["S0"])
+    for p, lane in enumerate([0, 3]):
+        dma("YS"[p], T.R0[lane:128:16, :], T.S0[:, p * 64:(p + 1) * 64], ["S0"], ["Rf%d" % p], "dfirst")
+    vcopy(T.KL[:, 0:64], T.IN[:, 0:64], ["INl"], ["KLb"])
+    send(xown(0), "aX0", "lX0", xk(0) + ["KLb"])
+    arrival("aX0", ["Xr0"])
+    add("V", lambda: V.memset(T.R[:, :], 0.0), w=rk(0) + rk(1))
     cols = {}
 
     def col(name):
@@ -250,234 +299,248 @@ def rank_program(g, core, T, topo):
     def oh(l):
         return T.OH[:, l:l + 1]
 
-    for name, a, b in [("03", 0, 3), ("36", 3, 6), ("68", 6, 8), ("8b", 8, 11), ("6a", 6, 10), ("13", 1, 3), ("46", 4, 6)]:
-        add("V", lambda o=col(name), a=a, b=b: V.tensor_reduce(o, T.OH[:, a:b], AxisListType.X, A.add), r=["OH"], w=["c" + name])
-    vcopy(col("gs"), T.PC[:, 4:5], ["PC4"], ["cgs"])
-    vts(col("a1"), oh(11), 64.0, oh(12), A.mult, A.add, ["OH"], ["ca1"])
-    vts(col("wc"), oh(13), 64.0, oh(14), A.mult, A.add, ["OH"], ["cwc"])
-    vts(col("eh"), col("68"), -64.0, col("03"), A.mult, A.add, ["c68", "c03"], ["ceh"])
-    vts(col("el"), col("68"), -64.0, col("36"), A.mult, A.add, ["c68", "c36"], ["cel"])
-    vts(col("wa"), col("8b"), 4096.0, col("a1"), A.mult, A.add, ["c8b", "ca1"], ["cwa"])
-    vts(col("k0"), oh(0), oh(3), None, A.subtract, None, ["OH"], ["ck0"])
-    vts(col("k1"), oh(1), 64.0, oh(2), A.mult, A.add, ["OH"], ["ck1"])
-    vts(col("wl"), col("eh"), 64.0, col("el"), A.mult, A.add, ["ceh", "cel"], ["cwl"])
-    vts(T.GM[:, 0:8], T.VAL[:, 0:8], T.CF[:, 4:5], None, A.is_equal, None, ["VAL", "CF4"], ["GM0"])
-    vts(T.GM[:, 8:16], T.VAL[:, 0:8], col("gs"), None, A.is_equal, None, ["VAL", "cgs"], ["GM1"])
-    vts(T.GM[:, 16:24], T.VAL[:, 0:8], T.CF[:, 4:5], -1.0, A.is_equal, A.mult, ["VAL", "CF4"], ["GM2"])
-    vts(T.GM[:, 24:32], T.VAL[:, 0:8], T.CF[:, 4:5], 128.0, A.is_equal, A.mult, ["VAL", "CF4"], ["GM3"])
-    vts(col("d1"), oh(13), col("eh"), None, A.subtract, None, ["OH", "ceh"], ["cd1"])
-    vts(col("d4"), oh(14), col("el"), None, A.subtract, None, ["OH", "cel"], ["cd4"])
-    for z, c in [("ZA", "wa"), ("ZC", "wc"), ("ZL", "wl")]:
-        vts(T[z][:, :], T.VAL[:, :], T.CF[:, 5:6], col(c), A.is_equal, A.mult, ["VAL", "CF5", "c" + c], [z])
-    vts(col("wk"), col("k0"), 4096.0, col("k1"), A.mult, A.subtract, ["ck0", "ck1"], ["cwk"])
-    vts(col("bk"), col("k0"), -256.0, None, A.mult, None, ["ck0"], ["cbk"])
-    vts(col("rd"), col("13"), col("46"), None, A.add, None, ["c13", "c46"], ["crd"])
-    vts(col("th"), oh(2), oh(5), THETA, A.add, A.mult, ["OH"], ["cth"])
-    vts(col("f2"), col("6a"), -2.0, None, A.mult, None, ["c6a"], ["cf2"])
-    vts(col("f5"), col("6a"), -5.0, None, A.mult, None, ["c6a"], ["cf5"])
-    vts(col("sb"), col("th"), -1.0, -0.5, A.mult, A.add, ["cth"], ["csb"])
-    vts(col("b1"), col("rd"), -320.0, col("f2"), A.mult, A.add, ["crd", "cf2"], ["cb1"])
-    vts(col("b0"), col("rd"), -704.0, col("f5"), A.mult, A.add, ["crd", "cf5"], ["cb0"])
-    for h, (a, b) in enumerate(hv):
-        gather("VS"[h], T.TA[:, own + a:own + b], T.R0[:, :], T.PL[:, a // 16:b // 16], r0k + ["PL"],
-               [["To00"], ["To01", "To02"]][h])
-    send(T.TA[:, own:own + S], "aT0", "lT0", ["To00", "To01"])
-    arrival("aT0", ["Tr0"])
-    statics(0)
-    lay(0, ["To00", "To01"])
-    dma("Y", T.U[:, :], T.u[:, :], [], ["U"], "ldu")
-    dma("Y", T.IN[:, 192:448], T.cand[:, 128:384], [], ["IN"], "ldc")
+    def o8(l):
+        return T.O8[:, l:l + 1]
 
-    def entries(table):
+    def lanes(name, src, a, b, step=1):
+        add("V", lambda: V.tensor_reduce(col(name), T[src][:, a:b:step], AxisListType.X, A.add), r=[src], w=["c" + name])
+
+    def axpy(name, x, a, y, r):
+        vts(col(name), x, a, y, A.mult, A.add, r, ["c" + name])
+
+    def entries(qu, table):
         for m, l, c, kind in table:
             base = MATS.index(m) * 128
-            out, gm = T.MAT[:, base + l:base + 128:16], T.GM[:, 8 * kind:8 * kind + 8]
+            if kind < 2:
+                out, gm = T.MAT[:, base + l:base + 128:16], T.GM[:, 8 * kind:8 * kind + 8]
+            else:
+                out, gm = T.MAT[:, base + l:base + 128:8], T.GM[:, 16 * kind - 16:16 * kind]
             key = "m%s%d" % (m, l)
             matkeys.setdefault(m, []).append(key)
             sc, r = (1.0, []) if c is None else (oh(c), ["OH"]) if isinstance(c, int) else (col(c), ["c" + c])
-            add("S", lambda out=out, gm=gm, sc=sc: SC.activation(out, gm, AF.Identity, scale=sc),
-                r=r + ["MAT", "GM%d" % kind], w=[key])
+            r = r + ["MAT", "GM%d" % kind]
+            if qu == "V":
+                vts(out, gm, sc, None, A.mult, None, r, [key])
+            else:
+                add("S", lambda out=out, gm=gm, sc=sc: SC.activation(out, gm, AF.Identity, scale=sc), r=r, w=[key])
 
-    entries([("BP", 0, None, 0), ("BP", 3, None, 2), ("BM", 0, None, 2), ("BM", 3, None, 0), ("MM", 1, 2, 0), ("MM", 2, 3, 0),
-             ("Be", 2, "eh", 0), ("Be", 5, "el", 0), ("Br", 13, 13, 0), ("Br", 14, 14, 0)])
-    second = [("Bt", 0, "eh", 0), ("Bt", 1, "d1", 0), ("Bt", 2, "eh", 2), ("Bt", 3, "el", 0), ("Bt", 4, "d4", 0),
-              ("Bt", 5, "el", 2), ("Bt", 10, "8b", 0), ("Bt", 11, 11, 0), ("Bt", 12, 12, 0),
-              ("Ao", 0, "wk", 0), ("Ao", 1, "wk", 0), ("Ao", 2, "wk", 0), ("Ao", 3, "wk", 2)]
-    third = [("Ab", 0, "wk", 2), ("Ab", 3, "wk", 0), ("Ab", 4, "wk", 0), ("Ab", 5, "wk", 0),
-             ("Ad", 1, "wk", 2), ("Ae", 4, "wk", 2),
-             ("Bs", 1, "03", 3), ("Bs", 4, "03", 3), ("Bs", 2, "36", 3), ("Bs", 5, "36", 3),
-             ("Bs", 6, "03", 0), ("Bs", 7, "36", 0), ("Bs", 8, "03", 1), ("Bs", 9, "36", 1)]
+    entries("S", [("BP", 0, None, 0), ("BP", 3, None, 1), ("BM", 0, None, 1), ("BM", 3, None, 0), ("MM", 1, 2, 0), ("MM", 2, 3, 0),
+                  ("Bc", 1, 13, 0), ("Ab", 6, 4, 0), ("Ab", 7, 5, 0)])
+    vts(T.GM[:, 16:32], T.VAL[:, 0:16], cf(3), None, A.is_equal, None, ["VAL", "CF"], ["GM2"])
+    vts(T.GM[:, 32:48], T.VAL[:, 0:16], cf(3), -1.0, A.is_equal, A.mult, ["VAL", "CF"], ["GM3"])
+    for name, a, b in [("03", 0, 3), ("36", 3, 6), ("68", 6, 8)]:
+        lanes(name, "O8", a, b)
+    vts(col("k0"), oh(0), oh(3), None, A.subtract, None, ["OH"], ["ck0"])
+    axpy("k1", oh(1), 64.0, oh(2), ["OH"])
+    axpy("eh", col("68"), -64.0, col("03"), ["c68", "c03"])
+    axpy("el", col("68"), -64.0, col("36"), ["c68", "c36"])
+    axpy("cm", oh(14), 2.0, oh(15), ["OH"])
+    vts(col("wk"), col("k0"), 4096.0, col("k1"), A.mult, A.subtract, ["ck0", "ck1"], ["cwk"])
+    vts(T.ID[:, :], T.VAL[:, 0:128], cf(0), None, A.is_equal, None, ["VAL", "CF"], ["ID"])
+    vts(T.NI[:, :], T.VAL[:, 0:128], cf(0), -1.0, A.is_equal, A.mult, ["VAL", "CF"], ["NI"])
+    entries("S", [("Kd", 4, "eh", 0), ("Kd", 5, "el", 0), ("Bc", 4, "cm", 0),
+                  ("Bt", 0, "eh", 2), ("Bt", 1, "eh", 3), ("Bt", 2, "eh", 3), ("Bt", 3, "el", 2), ("Bt", 4, "el", 3), ("Bt", 5, "el", 3)])
+    axpy("wt", oh(6), 256.0 * 4096.0, col("wk"), ["OH", "cwk"])
+    axpy("wl", col("eh"), 64.0, col("el"), ["ceh", "cel"])
+    axpy("bk", col("k0"), -256.0, oh(6), ["ck0", "OH"])
+    vts(cf(8), cf(2), 16.0, 15.0, A.mult, A.add, ["CF"], ["CF8"])
+    vcopy(T.CL[:, 0:128], T.IN[:, 64:192], ["IN0"], ["CL0"])
+    vts(T.ZL[:, :], T.VAL[:, :], cf(8), col("wl"), A.is_equal, A.mult, ["VAL", "CF8", "cwl"], ["ZL"])
+    for h, (a, b) in enumerate(hv):
+        gather("VS"[h], T.T0[:, own + a:own + b], T.R0[:, :], T.PL[:, a // 16:b // 16], ["Rf0", "Rf1", "PL"], keys("Tf", a, b))
+    send(T.T0[:, own:own + S], "aT0", "lTf", keys("Tf", 0, S))
+    arrival("aT0", ["Tr0"])
+    open_sums(0)
+    entries("S", [("Ao", 0, "wk", 0), ("Ao", 1, "wk", 0), ("Ao", 2, "wt", 0), ("Ao", 3, "wk", 1),
+                  ("Ab", 0, "wk", 1), ("Ab", 3, "wk", 0), ("Ab", 4, "wk", 0), ("Ab", 5, "wt", 0), ("Ad", 1, "wk", 1), ("Ae", 4, "wk", 1)])
+    lanes("14", "O8", 1, 6, 3)
+    lanes("25", "O8", 2, 6, 3)
+    lanes("mb", "OH", 0, 8)
+    vts(col("g1"), col("03"), 128.0, None, A.mult, None, ["c03"], ["cg1"])
+    axpy("g2", col("36"), 128.0, o8(6), ["c36", "O8"])
+    axpy("g5", col("36"), 128.0, o8(7), ["c36", "O8"])
+    axpy("we", oh(4), 64.0, oh(5), ["OH"])
+    vts(col("cap"), col("68"), 63.0, 1.0, A.mult, A.add, ["c68"], ["ccap"])
+    vts(col("f2"), col("68"), -2.0, None, A.mult, None, ["c68"], ["cf2"])
+    vts(col("rd"), col("14"), col("25"), -320.0, A.add, A.mult, ["c14", "c25"], ["crd"])
+    vts(col("w0"), col("68"), float(NXAT[0] - XAT[0] - own), None, A.mult, None, ["c68"], ["cw0"])
+    vts(col("w1"), col("68"), float(NXAT[1] - XAT[1] - own), None, A.mult, None, ["c68"], ["cw1"])
+    vts(cf(9), cf(5), cf(8), -1.0, A.add, A.add, ["CF", "CF8"], ["CF9"])
+    vts(cf(10), pc(7), cf(5), 14.0, A.add, A.add, ["PC7", "CF"], ["CF10"])
+    vts(cf(11), cf(2), 2.0, None, A.mult, None, ["CF"], ["CF11"])
+    vts(cf(12), cf(2), 2.0, 1.0, A.mult, A.add, ["CF"], ["CF12"])
+    vts(col("bt"), col("rd"), col("f2"), None, A.add, None, ["crd", "cf2"], ["cbt"])
+    entries("S", [("Bs", 1, "g1", 2), ("Bs", 4, "g1", 2), ("Bs", 2, "g2", 2), ("Bs", 5, "g5", 2), ("Bs", 6, "03", 2), ("Bs", 7, "36", 2)])
+    for z, c, at in [("ZE", "we", 8), ("ZF", "wl", 9), ("ZV0", "w0", 10), ("ZV1", "w1", 10)]:
+        vts(T[z][:, :], T.VAL[:, :], cf(at), col(c), A.is_equal, A.mult, ["VAL", "CF%d" % at, "c" + c], [z])
+    vts(T.JV[:, 0:64], T.VR[:, :], 4032, None, A.bitwise_and, None, ["VR"], ["JV0"])
+    vts(T.JV[:, 64:128], T.VR[:, :], 63, None, A.bitwise_and, None, ["VR"], ["JV1"])
+    vts(T.Ma[:, :], T.V8[:, :], cf(11), oh(15), A.is_equal, A.mult, ["V8", "CF11", "OH"], ["Ma"])
+    vts(T.Mb[:, :], T.V8[:, :], cf(12), oh(15), A.is_equal, A.mult, ["V8", "CF12", "OH"], ["Mb"])
+    vcopy(T.SV[:, :], T.JV[:, :], ["JV0", "JV1"], ["SV"])
+    vtt(T.Mk[:, :], T.Mb[:, :], T.Ma[:, :], A.subtract, ["Ma", "Mb"], ["Mk"])
+    statics(0)
+    lay(0, [])
+    statics(1)
+    lay(1, [])
+    dma("Y", T.U[:, :], T.u[:, :], [], ["U"], "ldu")
+    dma("Y", T.IN[:, 192:448], T.cand[:, 128:384], [], ["IN"], "ldu")
 
     for t in range(RO):
-        first = t == 0
+        first, last = t == 0, t + 1 == RO
         u, un = t % 2, (t + 1) % 2
         tn = "TA" if un == 0 else "TZ"
-        tw = TT[u][:, :]
-        tk = ["To%d0" % u, "To%d1" % u, "To%d2" % u, "Tr%d" % u]
-        xw = T.XT[:, 0:(t + 1) * W]
-        xk = xkeys(t)
-        xvk = ["XV"]
-        lists = {"AC": (T.AC, 0, "AC"), "AB": (T.AB, 0, "AB"), "AD": (T.AD, 0, "AD")}
-        if first:
-            lists = {"AC": (T.CL, 0, "CL0"), "AB": (T.KL, 0, "KLb"), "AD": (T.KL, 64, "KLd")}
+        xw = T.XX[:, XAT[u]:XAT[u] + W]
+        xr = xk(t) + ["Xr%d" % u]
+        ck = "CL0" if t < 2 else "CL"
+        todo = {c: 6 if first else 5 for c in "ABC"}
 
-        def xv(a, b):
-            return T.XV[:, a:b]
-
-        def off(name, a, b):
-            buf, o, _ = lists[name]
-            return buf[:, o + a // 16:o + b // 16]
-
-        def gmax(m, other, a, b, r, key):
-            vtt(T[m][:, a:b], xw.indirect(off("AC", a, b)), other, A.max, xk + [lists["AC"][2]] + r, [key])
-
-        def bmax(m, other, a, b, r, key):
-            h = a // 512
-            vtt(T[m][:, a:b], T[PB[h]][:, a - 512 * h:b - 512 * h], other, A.max, [PB[h]] + r, [key])
-
-        def xgather(buf, name, h):
-            a, b = hv[h]
-            gather("S", T[buf][:, a:b], xw, off(name, a, b), xk + [lists[name][2]], ["%s%d" % (buf, h)])
-            if buf == "XB":
-                mms(PB[h], 512, [("ID", T.XB[:, a:b])], True, True, ["XB%d" % h])
-
-        def look(buf, lst, o, key, cut=512):
-            for h, (a, b) in enumerate([(0, cut), (cut, S)]):
-                gather("VS"[h], T[buf][:, a:b], tw, lst[:, o + a // 16:o + b // 16], tk + [key], ["%s%d" % (buf, h)])
-
-        def send_x():
-            send(xown(t + 1), "aX%d" % (t + 1), "lO", ["Xa%d" % (t + 1), "Xb%d" % (t + 1), "Tr%d" % u])
-            arrival("aX%d" % (t + 1), ["Xr%d" % (t + 1)])
-
-        tc, tb = ["TC0", "TC1"], ["TB0", "TB1"]
-        m3 = ["M3%d" % c for c in range(4)]
-        if first:
-            for h, (a, b) in enumerate(hv):
-                gmax("M3", xv(a, b), a, b, xvk, m3[2 * h])
-                xgather("XB", "AB", h)
-            for h, (a, b) in enumerate(hv):
-                bmax("M1", xv(a, b), a, b, xvk, "M1%d" % h)
-            m3 = [m3[0], m3[0], m3[2], m3[2]]
-            entries(second)
-        elif t + 1 < RO:
-            send_x()
-        look("TC", T.CL, t * 64, "CL0" if t < 2 else "CL")
-        look("TB", T.KL, 0, "KLb")
-        conv("G1", "ZL", "TC", 0, tc)
-        if not first:
-            conv("G0", "ZA", "TC", 0, tc)
-        vcopy(T.KL[:, 64:128], T.G1[:, 0:64], ["G1"], ["KLd"])
-        if first:
-            gather("V", T.RS[:, 0:512], T.R[:, :], T.PL[:, 0:32], rk + ["PL"], ["RS0"])
-            xgather("XD", "AD", 0)
-            xgather("XD", "AD", 1)
-            conv("G0", "ZC", "TB", 0, tb)
-        else:
-            look("TD", T.KL, 64, "KLd", cut=TDCUT)
-            vcopy(T.AC[:, :], T.G0[:, 0:64], ["G0"], ["AC"])
-            conv("C2", "ZA", "TB", 0, tb)
-            conv("G1", "ZA", "TD", 0, ["TD0", "TD1"])
-            gmax("M3", xv(0, 256), 0, 256, xvk, m3[0])
-            vcopy(T.AB[:, :], T.C2[:, 0:64], ["C2"], ["AB"])
-            xgather("XB", "AB", 0)
-            gmax("M3", xv(256, 512), 256, 512, xvk, m3[1])
-            gmax("M3", xv(512, 768), 512, 768, xvk, m3[2])
-            vcopy(T.AD[:, :], T.G1[:, 0:64], ["G1"], ["AD"])
-            xgather("XD", "AD", 0)
-            conv("G0", "ZC", "TB", 0, tb)
-            gmax("M3", xv(768, S), 768, S, xvk, m3[3])
-            bmax("M1", xv(0, 512), 0, 512, xvk, "M10")
-        mms("F0", 512, [("BM", T.M3[:, 0:512]), ("BP", T.M1[:, 0:512])], True, False, m3[0:2] + ["M10"])
-        if first:
-            gather("S", T.RS[:, 512:S], T.R[:, :], T.PL[:, 32:64], rk + ["PL"], ["RS1"])
-        mms("F0", 512, [("MM", T.RS[:, 0:512])], False, False, ["RS0"])
-        if not first:
-            xgather("XB", "AB", 1)
-            xgather("XD", "AD", 1)
-        for c, (a, b) in enumerate(CHUNKS):
-            h = a // 512
-            if c == 1:
-                if not first:
-                    bmax("M1", xv(512, S), 512, S, xvk, "M11")
-                for c2 in (1, 2):
-                    a2, b2 = CHUNKS[c2]
-                    mms(FB[c2], b2 - a2, [("BM", T.M3[:, a2:b2]), ("MM", T.RS[:, a2:b2]), ("BP", T.M1[:, a2:b2])], True, False,
-                        [m3[c2 + 1], "RS1", "M11"])
-            gmax("M2", T.XD[:, a:b], a, b, ["XD%d" % h], "M2%d" % c)
-            mms(FB[c], b - a, [("BP", T.M2[:, a:b])], False, False, ["M2%d" % c])
-            bmax("M4", T.XD[:, a:b], a, b, ["XD%d" % h], "M4%d" % c)
-            mms(FB[c], b - a, [("BM", T.M4[:, a:b])], False, True, ["M4%d" % c])
-            ko = T.KK[:, own + a:own + b]
-            if c < 2:
-                act(ko, T[FB[c]][:, 0:b - a], AF.Relu, col("bk"), [FB[c], "cbk"], ["Ko%d" % c])
+        def look():
+            if first:
+                for h, (a, b) in enumerate(hv):
+                    gather("VS"[h], T.TC[:, a:b], T.T0[:, :], T.CL[:, a // 16:b // 16], keys("Tf", 0, S) + ["Tr0", ck], keys("TC", a, b))
             else:
-                vcopy(T.LCB[:, :], T.G0[:, 0:64], ["G0"], ["LCB"])
-                vts(ko, T[FB[c]][:, 0:b - a], col("bk"), 0.0, A.add, A.max, [FB[c], "cbk"], ["Ko%d" % c])
-            if c == 0:
-                send(ko, "aK%d" % t, "lK0", ["Ko0"])
-        send(T.KK[:, own + 512:own + S], "aK%d" % t, "lK1", ["Ko1", "Ko2"])
+                vtt(T.TC[:, :], TT[u][:, :].indirect(T.CH[:, t * 64:t * 64 + 64]), T.MK[:, :], A.mult,
+                    ["To%d0" % u, "To%d1" % u, "Tr%d" % u, "CH", "MK0", "MK1"], keys("TC", 0, S))
+
+        def gmax(m, other, r, a, b):
+            vtt(T[m][:, a:b], xw.indirect(T.CL[:, t * 64 + a // 16:t * 64 + b // 16]), other, A.max, xr + [ck] + r, keys(m, a, b))
+
+        def summed(term, c):
+            a, b = CHUNKS[c]
+            l, buf, k = {"0": ("MM", RR[u], "RS%d" % u), "1": ("BP", T.M1, "M1"), "2": ("BP", T.M2, "M2"),
+                         "3": ("BM", T.M3, "M3"), "4": ("BM", T.M4, "M4"), "5": ("Kd", T.TC, "TC")}[term]
+            todo[c] -= 1
+            mms(FB[c], b - a, [(l, buf[:, a:b], 0)], todo[c] == 5, todo[c] == 0, keys(k, a, b))
+
+        def feat(buf, j, c, qu):
+            a, b = CHUNKS[c]
+            gather(qu, T[buf][:, a:b], xw, T.KL[:, j * 64 + a // 16:j * 64 + b // 16], xr + ["KL" + "bd"[j]], keys(buf, a, b))
+
+        def psum(bank, l, buf, c, start, stop):
+            a, b = CHUNKS[c]
+            mms(bank, b - a, [(l, T[buf][:, a:b], 0)], start, stop, keys(buf, a, b))
+
+        def bmax(m, c):
+            a, b = CHUNKS[c]
+            bank, o = ("P0", 0) if c == "A" else ("P2", 512)
+            other, r = (xown(t, a, b), xk(t, a, b)) if m == "M1" else (T.XD[:, a:b], keys("XD", a, b))
+            vtt(T[m][:, a:b], T[bank][:, a - o:b - o], other, A.max, [bank] + r, keys(m, a, b))
+
+        def over(m, bank, c, qu):
+            a, b = CHUNKS[c]
+            relu(qu, T[m][:, a:b], T[bank][:, 0:b - a], 0.0, [bank], keys(m, a, b))
+
+        def ko(c, qu):
+            a, b = CHUNKS[c]
+            relu(qu, T.KK[:, own + a:own + b], T[FB[c]][:, 0:b - a], col("bk"), [FB[c], "cbk"], keys("Ko", a, b))
+
+        def m2(c):
+            a, b = CHUNKS[c]
+            gmax("M2", T.XD[:, a:b], keys("XD", a, b), a, b)
+
+        steps = {
+            "tc": look, "cd": lambda: conv("C0", "ZL", "TC", 0, keys("TC", 0, S)),
+            "kd": lambda: vcopy(T.KL[:, 64:128], T.C0[:, 0:64], ["C0"], ["KLd"]),
+            "m3": lambda a, b: gmax("M3", T.XV[:, int(a):int(b)], ["XV"], int(a), int(b)), "m2": m2,
+            "xb": lambda c, qu: feat("XB", 0, c, qu), "xd": lambda c, qu: feat("XD", 1, c, qu),
+            "pb": lambda c: psum("P0" if c == "A" else "P2", "ID", "XB", c, True, True),
+            "n1": lambda c: psum(R1B[c], "NI", "XB", c, False, True),
+            "n4": lambda c: psum(R4B[c], "NI", "XB", c, True, False), "d4": lambda c: psum(R4B[c], "ID", "XD", c, False, True),
+            "m1": lambda c: bmax("M1", c), "m4": lambda c: bmax("M4", c),
+            "r1": lambda c, qu: over("M1", R1B[c], c, qu), "r4": lambda c, qu: over("M4", R4B[c], c, qu),
+            "s": summed, "ko": ko, "rs": lambda: order_lanes(0, 512),
+            "lay": lambda: last or lay(t + 1, ["Xr%d" % u]),
+            "send0": lambda: send(T.KK[:, own:own + 512], "aK%d" % t, "lK0", keys("Ko", 0, 512)),
+            "send1": lambda: send(T.KK[:, own + 512:own + S], "aK%d" % t, "lK1", keys("Ko", 512, S)),
+        }
+        for step in (GAIN0 if first else GAIN).split():
+            name, *args = step.split(":")
+            steps[name](*args)
         arrival("aK%d" % t, ["Kr"], calls=2)
-        kk = ["Ko0", "Ko1", "Ko2"]
-        look("TE", T.LCB, 0, "LCB")
-        if first:
-            build(1)
-            send_x()
-            entries(third)
-        conv("C0", "ZL", "TE", 0, ["TE0", "TE1"])
-        vcopy(T.KL[:, 128:192], T.C0[:, 0:64], ["C0"], ["KLe"])
-        for c, (a, b) in enumerate(CHUNKS):
-            mms(FB[c], b - a, [("Ao", T.KK[:, own + a:own + b])], True, False, ["Ko%d" % c])
-        for c, (a, b) in enumerate(CHUNKS):
-            h = a // 512
-            terms = [("Bt", TT[u][:, own + a:own + b]), ("Be", T.TE[:, a:b])]
-            if t + 1 < RO:
-                terms += [("Br", T.RS[:, a:b])]
-            mms(GB[c], b - a, terms, True, False, ["TE%d" % h, "To%d%d" % (u, c), "RS%d" % h])
-        if first:
-            vcopy(T.CL[:, 128:384], T.IN[:, 192:448], ["IN"], ["CL"])
-        if t + 1 < RO:
-            statics(t + 1)
-            lay(t + 1, ["Kr"])
-        kw = T.KK[:, :]
-        kr = kk + ["Kr"]
-        for qu, j, h in [("V", 0, 0), ("S", 1, 0), ("V", 2, 0), ("S", 1, 1), ("V", 0, 1), ("S", 2, 1)]:
-            a, b = hv[h]
-            gather(qu, T.GK[:, j * S + a:j * S + b], kw, T.KL[:, j * 64 + a // 16:j * 64 + b // 16],
-                   kr + ["KL" + "bde"[j]], ["GK%d%d" % (j, h)])
-            if h == 0:
-                mms("F0", 512, [("A" + "bde"[j], T.GK[:, j * S:j * S + 512])], False, j == 2, ["GK%d0" % j])
-            elif j == 1:
-                for c in (1, 2):
-                    a, b = CHUNKS[c]
-                    mms(FB[c], b - a, [("Ad", T.GK[:, S + a:S + b])], False, False, ["GK11"])
-        for c in (1, 2):
-            a, b = CHUNKS[c]
-            mms(FB[c], b - a, [("Ab", T.GK[:, a:b]), ("Ae", T.GK[:, 2 * S + a:2 * S + b])], False, True, ["GK01", "GK21"])
-        to = ["To%d%d" % (un, c) for c in range(3)]
-        vts(T.SN[:, 0:512], T.F0[:, :], col("th"), 2.0, A.is_gt, A.mult, ["F0", "cth"], ["SN0"])
-        for c in (1, 2):
-            a, b = CHUNKS[c]
-            act(T.SN[:, a:b], T[FB[c]][:, 0:b - a], AF.Sign, col("sb"), [FB[c], "csb"], ["SN%d" % c])
-        for c, (a, b) in enumerate(CHUNKS):
-            mms(GB[c], b - a, [("Bs", T.SN[:, a:b])], False, True, ["SN%d" % c])
-        vts(TT[un][:, own:own + 512], T.G0[:, :], col("b0"), 0.0, A.add, A.max, ["G0", "cb0"], [to[0]])
-        for c in (1, 2):
-            a, b = CHUNKS[c]
-            act(TT[un][:, own + a:own + b], T[GB[c]][:, 0:b - a], AF.Relu, col("b1"), [GB[c], "cb1"], [to[c]])
-        if t + 1 == RO:
-            conv("C0", "ZL", tn, own, to)
+        if not last:
+            build(t)
+            order_lanes(t + 1)
+        for h, (a, b) in enumerate(PART):
+            mms(DB[h], (b - a) // 2, pairs("Ao", T.KK, own + a, own + b), True, False, keys("Ko", a, b))
+        for h, (a, b) in enumerate(PART):
+            if first:
+                terms, r = pairs("Bt", T.T0, own + a, own + b), keys("Tf", a, b)
+            else:
+                terms, r = [("Bt", TT[u][:, (own + a) // 2:(own + b) // 2], 0)], ["To%d%d" % (u, h)]
+            mms(GB[h], (b - a) // 2, terms + pairs("Bc", RR[u], a, b), True, False, r + keys("RS%d" % u, a, b))
+        if not last:
+            mms("P2", 64, [("ID", T.SV[:, 0:64], 0), ("ID", T.SV[:, 64:128], 0)], True, False, ["SV"])
+        kr = keys("Ko", 0, S) + ["Kr"]
+        left = [3 * (b - a) for a, b in PART]
+        waiting = []
+
+        def differences():
+            for j, a, b in waiting:
+                for h, (c, d) in enumerate(PART):
+                    lo, hi = max(a, c), min(b, d)
+                    if lo < hi:
+                        left[h] -= hi - lo
+                        mms(DB[h], (hi - lo) // 2, pairs("A" + "bde"[j], T.GK, j * S + lo, j * S + hi), False, left[h] == 0,
+                            keys("GK%d" % j, lo, hi), o=(lo - c) // 2)
+            waiting.clear()
+
+        listed = False
+        for step in DECIDE.split():
+            name, *args = step.split(":")
+            if name in "VS":
+                j, a, b = "bde".index(args[0]), int(args[1]), int(args[2])
+                gather(name, T.GK[:, j * S + a:j * S + b], T.KK[:, :], T.KL[:, j * 64 + a // 16:j * 64 + b // 16],
+                       kr + ["KL" + args[0]], keys("GK%d" % j, a, b))
+                waiting.append((j, a, b))
+                if listed:
+                    differences()
+            elif name == "ce":
+                conv("F2", "ZE", "GK", 0, keys("GK0", 0, S))
+                listed = True
+                differences()
+            elif name == "df":
+                differences()
+            elif name == "le":
+                vcopy(T.KL[:, 128:192], T.F2[:, 0:64], ["F2"], ["KLe"])
+            elif name == "s":
+                h = int(args[0])
+                a, b = PART[h]
+                sn = T.SN[:, a // 2:b // 2]
+                vts(sn, T[DB[h]][:, 0:(b - a) // 2], 0.0, col("cap"), A.max, A.min, [DB[h], "ccap"], ["SN%d" % h])
+                mms(GB[h], (b - a) // 2, [("Bs", sn, 0)], False, True, ["SN%d" % h])
+            elif name == "o":
+                h = int(args[0])
+                a, b = PART[h]
+                relu(args[1], TT[un][:, (own + a) // 2:(own + b) // 2], T[GB[h]][:, 0:(b - a) // 2], col("bt"),
+                     [GB[h], "cbt"], ["To%d%d" % (un, h)])
+        to = ["To%d0" % un, "To%d1" % un]
+        if last:
+            conv2("C0", "ZF", tn, to)
             vcopy(T.Y[:, :], T.C0[:, 0:64], ["C0"], ["Y"])
             dma("Y", T.ylink[:, :], T.Y[:, :], ["Y"], ["y"], "out")
             break
-        send(TT[un][:, own:own + S], "aT%d" % (t + 1), "lT%d" % un, to)
+        send(TT[un][:, q * H:(q + 1) * H], "aT%d" % (t + 1), "lT%d" % un, to)
         arrival("aT%d" % (t + 1), ["Tr%d" % un])
-        conv("F2", "ZA", tn, own, to)
-        conv("C0", "ZL", tn, own, to)
-        gather("S", T.RS[:, :], T.R[:, :], T.PL[:, :], rk + ["PL"], ["RS0", "RS1"])
-        vcopy(T.AV[:, :], T.F2[:, 0:64], ["F2"], ["AV"])
-        vcopy(T.KL[:, 0:64], T.C0[:, 0:64], ["C0"], ["KLb"])
-        gather("S", T.XV[:, :], T.XT[:, 0:(t + 2) * W], T.AV[:, :], xkeys(t + 1) + ["AV"], ["XV"])
+        conv2("P2", "ZV%d" % u, tn, to, start=False)
+        lo = min(XAT[u], NXAT[u])
+        vts(T.AV[:, :], T.P2[:, 0:64], float(XAT[u] - lo), None, A.add, None, ["P2"], ["AV"])
+        for h, (a, b) in enumerate(hv):
+            gather("VS"[h], xown(t + 1, a, b), T.XX[:, lo:lo + S + W], T.AV[:, a // 16:b // 16],
+                   xr + ["N%d0" % u, "N%d1" % u, "AV"], xk(t + 1, a, b))
+        send(xown(t + 1), "aX%d" % (t + 1), "lX%d" % un, xk(t + 1))
+        arrival("aX%d" % (t + 1), ["Xr%d" % un])
+        conv2("F2", "ZF", tn, to)
+        for h, (a, b) in enumerate(hv):
+            mms(BB[h], 512, [("Mk", RR[un][:, a:b], 0)], True, True, keys("RS%d" % un, a, b))
+            relu("S", T.MK[:, a:b], T[BB[h]][:, :], col("mb"), [BB[h], "cmb"], ["MK%d" % h])
+        vcopy(T.KL[:, 0:64], T.F2[:, 0:64], ["F2"], ["KLb"])
+        if first:
+            vts(T.HL[:, :], T.IN[:, 128:448], 1, None, A.arith_shift_right, None, ["IN0", "IN"], ["HI", "LO"])
+            vcopy(T.CH[:, 64:384], T.HL[:, :], ["HI", "LO"], ["CH"])
+            vcopy(T.CL[:, 128:384], T.IN[:, 192:448], ["IN"], ["CL"])
         if t + 2 < RO:
-            build(t + 2)
+            statics(t + 2)
+        open_sums(t + 1)
 
     emit({"G": g, "V": V, "S": SC, "P": PE, "Y": SY}, T)

@@ -5,45 +5,45 @@ RO, S, W, N = 6, 1024, 4096, 4
 H = S // 2
 BF, F32, I32, U16 = "bfloat16", "float32", "int32", "uint16"
 CHUNKS = {"A": (0, 512), "B": (512, 768), "C": (768, 1024), "D": (512, 1024)}
-CUT = 512
-MATS = ["BP", "BM", "MM", "Kd", "Ao", "Ab", "Ad", "Ae", "Bc", "Bt", "Bs"]
+PART = [(0, 512), (512, 768), (768, 1024)]
+MATS = ["BP", "BM", "MM", "Kg", "M0", "Kh", "Kl", "Ao", "Ab", "Ad", "Ae", "Bc", "Bt", "Bs"]
 
-GAIN0 = ("m3:512:1024 xb:D:S pb:B m3:0:512 xb:A:S m1:B tc n4:C s:3:B pb:A n1:C s:3:A s:3:C cd s:5:C m1:A r1:C:S s:5:A kd "
-         "xd:A:S s:1:C s:5:B rs s:0:A m4:A m2:A xd:B:S s:1:A s:4:A s:2:A xd:C:S s:0:B s:0:C m2:B m2:C d4:C s:1:B r4:C:V "
-         "ko:A:S send0 s:4:C m4:B s:4:B s:2:C s:2:B ko:C:V ko:B:V send1")
-GAIN = ("tc lay cd xb:A:S s:5:A kd m3:0:512 xd:A:S xb:D:S pb:A m1:A s:5:C xd:B:S xd:C:S s:5:B m2:A s:3:A s:1:A pb:B m4:A "
-        "m3:512:1024 n1:C s:2:A s:4:A m1:B r1:C:S ko:A:S send0 n4:C s:3:B m2:B d4:C s:1:C s:3:C s:1:B m4:B r4:C:S s:2:B "
-        "s:4:B ko:B:S s:4:C m2:C s:2:C ko:C:V send1")
-DECIDE = ("V:b:0:256 S:b:256:512 df V:b:512:768 S:b:768:1024 ce V:d:0:512 S:d:512:1024 le V:e:0:256 S:e:256:512 "
-          "V:e:512:768 S:e:768:1024 s:0 o:0:S s:1 o:1:V")
+GAIN = ("kd xb:A m3:A xd:A xb:D pb:A s:5:A s:5:B s:5:C m1:A xd:B xd:C m2:A s:3:A s:1:A pb:B m4:A m3:D n1 s:2:A s:4:A m1:B "
+        "r1 ko:A:S k:A n4 s:3:B m2:B d4 s:1:C s:3:C s:1:B m4:B r4 s:2:B s:4:B ko:B:S s:4:C m2:C s:2:C ko:C:V k:D")
+GAIN0 = ("m3:A kd xb:A xb:D xd:A pb:A m1:A rs:256 s:3:A s:5:A m2:A m4:A n1 m3:D n4 s:1:A pb:B xd:B s:5:C s:2:A s:0:A s:4:A "
+         "m4:B m1:B s:0:C r1 s:5:B s:3:B s:0:B m2:B xd:C d4 s:4:B s:1:B s:1:C ko:A:S k:A s:3:C s:2:B r4 s:4:C m2:C s:2:C "
+         "ko:B:S ko:C:V k:D")
+DECIDE = ("V:b:0 p:b:0 V:b:2 V:d:0 S:b:1 p:b:1 S:b:3 ce V:d:3 p:b:3 p:d:0 S:d:2 le p:b:2 S:d:1 V:e:0 S:e:1 p:d:3 p:d:1 "
+          "p:e:0 p:e:1 V:e:2 p:d:2 s:0 p:e:2 S:e:3 s:1 p:e:3 bs:0 bs:1 s:2 o:1:V bs:2 o:2:V o:0:S")
 
 SCRATCH = {
     "XX": ("sbuf", [128, 2 * (S + W)], BF), "KK": ("sbuf", [128, W], BF),
-    "T0": ("sbuf", [128, W], BF), "TA": ("sbuf", [128, W // 2], BF), "TZ": ("sbuf", [128, W // 2], BF),
+    "TA": ("sbuf", [128, W // 2], BF), "TZ": ("sbuf", [128, W // 2], BF),
     "U": ("sbuf", [128, S], BF), "SG": ("sbuf", [128, S], BF), "SN": ("sbuf", [128, H], BF),
-    "TC": ("sbuf", [128, S], BF), "MK": ("sbuf", [128, S], BF), "XV": ("sbuf", [128, S], BF), "XB": ("sbuf", [128, S], BF), "XD": ("sbuf", [128, S], BF),
+    "TC": ("sbuf", [128, S], BF), "MK": ("sbuf", [128, S], BF), "T0": ("sbuf", [128, S], BF),
+    "XV": ("sbuf", [128, S], BF), "XB": ("sbuf", [128, S], BF), "XD": ("sbuf", [128, S], BF),
     "M1": ("sbuf", [128, S], BF), "M2": ("sbuf", [128, S], BF), "M3": ("sbuf", [128, S], BF), "M4": ("sbuf", [128, S], BF),
     "GK": ("sbuf", [128, 3 * S], BF),
-    "R0": ("sbuf", [128, S], BF), "R": ("sbuf", [128, 2 * S], BF), "RA": ("sbuf", [128, S], BF), "RZ": ("sbuf", [128, S], BF),
-    "IN": ("sbuf", [128, 7 * 64], I32), "HL": ("sbuf", [128, 320], I32),
-    "S0": ("sbuf", [128, 128], BF), "SV": ("sbuf", [128, 128], BF), "SP": ("sbuf", [128, 2, 320], BF),
-    "CL": ("sbuf", [128, 384], U16), "CH": ("sbuf", [128, 384], U16), "KL": ("sbuf", [128, 192], U16),
-    "PL": ("sbuf", [128, 64], U16), "AV": ("sbuf", [128, 64], U16),
-    "Y": ("sbuf", [128, 64], F32), "MN": ("sbuf", [128, 64], I32), "J": ("sbuf", [128, 320], I32), "JV": ("sbuf", [128, 128], I32),
-    "VAL": ("sbuf", [128, 144], F32), "V8": ("sbuf", [128, 128], F32), "PC": ("sbuf", [128, 8], I32), "CF": ("sbuf", [128, 16], F32),
-    "OH": ("sbuf", [128, 16], F32), "O8": ("sbuf", [128, 8], F32), "GM": ("sbuf", [128, 48], F32), "WC": ("sbuf", [128, 32], F32),
-    "VR": ("sbuf", [128, 64], I32),
-    "ZL": ("sbuf", [128, 144], BF), "ZE": ("sbuf", [128, 144], BF), "ZF": ("sbuf", [128, 144], BF),
-    "ZV0": ("sbuf", [128, 144], BF), "ZV1": ("sbuf", [128, 144], BF),
+    "R0": ("sbuf", [128, S], BF), "R": ("sbuf", [128, S], BF), "RA": ("sbuf", [128, S], BF), "RZ": ("sbuf", [128, S], BF),
+    "IN": ("sbuf", [128, 7 * 64], I32), "HL": ("sbuf", [128, 640], I32),
+    "S0": ("sbuf", [128, N * 128], BF), "SV": ("sbuf", [128, 128], BF), "SP": ("sbuf", [128, 5, 384], BF),
+    "CL": ("sbuf", [128, 384], U16), "CH": ("sbuf", [128, 384], U16), "CS": ("sbuf", [128, 64], U16),
+    "KL": ("sbuf", [128, 192], U16), "PL": ("sbuf", [128, 64], U16), "AV": ("sbuf", [128, 64], U16),
+    "Y": ("sbuf", [128, 64], F32), "MN": ("sbuf", [128, 192], I32), "J": ("sbuf", [128, 5, 192], I32), "JV": ("sbuf", [128, 256], I32),
+    "VAL": ("sbuf", [128, 144], F32), "PC": ("sbuf", [128, 8], I32), "CF": ("sbuf", [128, 16], F32),
+    "OH": ("sbuf", [128, 16], F32), "O8": ("sbuf", [128, 8], F32), "GM": ("sbuf", [128, 48], F32), "WC": ("sbuf", [128, 48], F32),
+    "VR": ("sbuf", [128, 64], I32), "MT": ("sbuf", [128, 16], BF),
+    "ZL": ("sbuf", [128, 144], BF), "ZD": ("sbuf", [128, 144], BF), "ZE": ("sbuf", [128, 144], BF),
+    "ZF": ("sbuf", [128, 144], BF), "ZV0": ("sbuf", [128, 144], BF), "ZV1": ("sbuf", [128, 144], BF),
     "MAT": ("sbuf", [128, len(MATS) * 128], BF), "ID": ("sbuf", [128, 128], BF), "NI": ("sbuf", [128, 128], BF),
-    "Mk": ("sbuf", [128, 128], BF), "Ma": ("sbuf", [128, 128], BF), "Mb": ("sbuf", [128, 128], BF),
+    "DL": ("sbuf", [128, 128], F32), "Z6": ("sbuf", [128, 144], BF), "Z1": ("sbuf", [128, 144], BF),
     "F0": ("psum", [128, 512], F32), "F1": ("psum", [128, 512], F32), "F2": ("psum", [128, 512], F32),
     "P0": ("psum", [128, 512], F32), "P1": ("psum", [128, 512], F32), "P2": ("psum", [128, 512], F32),
     "C0": ("psum", [128, 512], F32), "C1": ("psum", [128, 512], F32),
 }
 PSUM = [k for k, v in SCRATCH.items() if v[0] == "psum"]
-SEMAPHORES = (["sV", "sS", "sP", "sG", "ldl", "ldc", "ldx", "ldu", "dfirst", "out", "lK0", "lK1", "lT0", "lT1", "lTf", "lX0", "lX1"]
-              + ["%s%d" % (n, t) for n in ("aX", "aK", "aT", "dR") for t in range(RO)])
+SEMAPHORES = (["sV", "sS", "sP", "sG", "ldl", "ldc", "ldx", "ldu", "dfirst", "out", "lT0", "lT1", "lTf", "lX0", "lX1",
+               "lKA", "lKD", "ldv"] + ["%s%d" % (n, t) for n in ("aX", "aK", "aT", "dR", "dU", "dX", "dS") for t in range(RO)])
 
 
 def make_plan():
@@ -153,22 +153,23 @@ def rank_program(g, core, T, topo):
         else:
             add("S", lambda: SC.activation(out, win.indirect(off), AF.Copy), r=r, w=w)
 
-    def conv(bank, z, src, a, r):
+    def conv(bank, z, src, a, r, start=True, stop=True):
         def fn():
             for i in range(16):
-                ins = PE.matmul(T[bank][:, 0:64], T[z][:, 15 - i:143 - i], T[src][:, a + i:a + S:16], i == 0, i == 15)
+                ins = PE.matmul(T[bank][:, 0:64], T[z][:, 15 - i:143 - i], T[src][:, a + i:a + S:16],
+                                start and i == 0, stop and i == 15)
             return ins
-        add("P", fn, r=r + [z], w=[bank])
+        add("P", fn, r=r + [z], w=[bank], acc=not start)
 
-    def conv2(bank, z, src, r, start=True):
+    def conv2(bank, z, src, r, start=True, rank=q):
         def fn():
             for m in range(8):
-                ins = PE.matmul(T[bank][:, 0:64], T[z][:, 14 - 2 * m:142 - 2 * m], T[src][:, q * H + m:(q + 1) * H:8],
+                ins = PE.matmul(T[bank][:, 0:64], T[z][:, 14 - 2 * m:142 - 2 * m], T[src][:, rank * H + m:(rank + 1) * H:8],
                                 start and m == 0, m == 7)
             return ins
         add("P", fn, r=r + [z], w=[bank], acc=not start)
 
-    matkeys = {"ID": ["ID"], "NI": ["NI"], "Mk": ["Mk"]}
+    matkeys = {"ID": ["ID"], "NI": ["NI"]}
 
     def mat(l, up=0):
         if l in MATS:
@@ -189,9 +190,8 @@ def rank_program(g, core, T, topo):
     own = q * S
     hv = [(0, 512), (512, S)]
     FB = {"A": "F0", "B": "F1", "C": "F2"}
-    R1B, R4B = {"C": "P1", "D": "P2"}, {"B": "P1", "C": "C1"}
-    BB, DB, GB = ["C0", "C1"], ["F0", "F1"], ["P0", "P1"]
-    PART = [(0, CUT), (CUT, S)]
+    PB = {"A": "P0", "B": "P2"}
+    DB, GB = ["F0", "F1", "C0"], ["P0", "P1", "C1"]
     TT, RR = [T.TA, T.TZ], [T.RA, T.RZ]
     XAT, NXAT = [S, S + W], [0, S + 2 * W]
 
@@ -204,58 +204,92 @@ def rank_program(g, core, T, topo):
     def xk(n, a=0, b=S):
         return keys("X%d" % (n % 2), a, b)
 
-    def build(n):
-        for h, (a, b) in enumerate(hv):
-            mms(BB[h], 512, [("ID", xown(n, a, b), 0), ("ID", T.U[:, a:b], 0)], True, True, xk(n, a, b) + ["U"])
-        for h, (a, b) in enumerate(hv):
-            vts(T.SG[:, a:b], T[BB[h]][:, :], 32.0, -32.0, A.is_ge, A.mult, [BB[h]], ["SG%d" % h])
-            vtt(T.XX[:, NXAT[n % 2] + a:NXAT[n % 2] + b], T[BB[h]][:, :], T.SG[:, a:b], A.add, [BB[h], "SG%d" % h],
-                ["N%d%d" % (n % 2, h)])
+    def nx(n):
+        return T.XX[:, NXAT[n % 2]:NXAT[n % 2] + S]
+
+    def drift_u(n, extra):
+        dma("Y", nx(n), T.U[:, :], ["U"] + extra, ["N%d" % (n % 2)], "dU%d" % n)
+
+    def drift_x(n):
+        add("G", lambda: g.dma_start(nx(n), xown(n), accum_op=A.add), r=xk(n) + ["N%d" % (n % 2)], w=["N%d" % (n % 2)],
+            sem="dX%d" % n, inc=16, whole=True)
+
+    def drift_over(n):
+        vts(T.SG[:, :], nx(n), 32.0, -32.0, A.is_ge, A.mult, ["N%d" % (n % 2)], ["SG"])
+        add("G", lambda: g.dma_start(nx(n), T.SG[:, :], accum_op=A.add), r=["SG", "N%d" % (n % 2)], w=["N%d" % (n % 2)],
+            sem="dS%d" % n, inc=16, whole=True)
 
     def cand(t):
         return T.IN[:, 64 + t * 64:128 + t * 64]
 
-    def statics(t):
-        k = "IN0" if t < 2 else "IN"
-        vtt(T.MN[:, :], cand(t), T.VR[:, :], A.min, [k, "VR"], ["MN"])
-        vts(T.J[:, 128:192], cand(t), 6, None, A.arith_shift_right, None, [k], ["J2"])
-        vts(T.J[:, 192:256], cand(t), 1, 31, A.arith_shift_right, A.bitwise_and, [k], ["J3"])
-        vts(T.J[:, 256:320], cand(t), 1, None, A.bitwise_and, None, [k], ["J4"])
-        vts(T.J[:, 0:64], T.MN[:, :], 6, None, A.arith_shift_right, None, ["MN"], ["J0"])
-        vts(T.J[:, 64:128], T.MN[:, :], 63, None, A.bitwise_and, None, ["MN"], ["J1"])
-        vcopy(T.SP[:, t % 2, :], T.J[:, :], ["J%d" % p for p in range(5)], ["SP%d" % (t % 2)])
+    def statics(t0, t1):
+        a, b, n = 64 * t0, 64 * t1, 64 * (t1 - t0)
+        c, k, rounds = T.IN[:, 64 + a:64 + b], ["IN0", "IN"][:1 + (t1 > 2)], range(t0, t1)
+        for t in rounds:
+            vtt(T.MN[:, 64 * t - a:64 * t - a + 64], cand(t), T.VR[:, :], A.min, k + ["VR"], ["MN%d" % (t - t0)])
+        vts(T.J[:, 2, 0:n], c, 6, None, A.arith_shift_right, None, k, ["J2"])
+        vts(T.J[:, 3, 0:n], c, 1, 31, A.arith_shift_right, A.bitwise_and, k, ["J3"])
+        vts(T.J[:, 4, 0:n], c, 1, None, A.bitwise_and, None, k, ["J4"])
+        mn = ["MN%d" % (t - t0) for t in rounds]
+        vts(T.J[:, 0, 0:n], T.MN[:, 0:n], 6, None, A.arith_shift_right, None, mn, ["J0"])
+        vts(T.J[:, 1, 0:n], T.MN[:, 0:n], 63, None, A.bitwise_and, None, mn, ["J1"])
+        if t0:
+            vts(T.HL[:, 0:n], c, 1, None, A.arith_shift_right, None, k, ["HI", "LO"])
+        vcopy(T.CL[:, a:b], c, k, ["CL%d" % t for t in rounds])
+        vcopy(T.SP[:, :, a:b], T.J[:, :, 0:n], ["J%d" % p for p in range(5)], ["SP%d" % t for t in rounds])
+        if t0:
+            vcopy(T.CH[:, a:b], T.HL[:, 0:n], ["HI", "LO"], ["CH%d" % t for t in rounds])
 
-    def rk(t):
-        return ["R%d%d" % (t % 2, p) for p in range(5)]
+    rk = ["R%d" % p for p in range(5)]
 
     def lay(t, extra):
         for p, lane in enumerate([2, 3, 13, 14, 15]):
-            dma("Y", T.R[lane:128:16, t % 2 * S:(t % 2 + 1) * S], T.SP[:, t % 2, p * 64:(p + 1) * 64], ["SP%d" % (t % 2)] + extra,
-                [rk(t)[p]], "dR%d" % t)
+            dma("Y", T.R[lane:128:16, :], T.SP[:, p, t * 64:t * 64 + 64], ["SP%d" % t] + extra, [rk[p]], "dR%d" % t)
 
     def order_lanes(t, cut=0):
         for qu, a, b in [("V", 0, cut), ("S", cut, S)]:
             if a < b:
-                gather(qu, RR[t % 2][:, a:b], T.R[:, t % 2 * S:(t % 2 + 1) * S], T.PL[:, a // 16:b // 16], rk(t) + ["PL"],
-                       keys("RS%d" % (t % 2), a, b))
+                gather(qu, RR[t % 2][:, a:b], T.R[:, :], T.PL[:, a // 16:b // 16], rk + ["PL"], keys("RS%d" % (t % 2), a, b))
+
+    def partners_of_c(t):
+        u = t % 2
+        if t:
+            for h, (a, b) in enumerate(hv):
+                gather("VS"[h], T.TC[:, a:b], TT[u][:, :], T.CH[:, t * 64 + a // 16:t * 64 + b // 16],
+                       ["To%d%d" % (u, k) for k in range(len(PART))] + ["Tr%d" % u, "CH%d" % t], keys("TC", a, b))
+            conv("C1", "ZD", "TC", 0, keys("TC", 0, S))
+        else:
+            for m, k, z, a0 in [("TC", "TC", "Z6", 0), ("GK", "GK0", "Z1", 64)]:
+                vtt(T[m][:, 0:S], T.S0[:, a0:a0 + 448].indirect(T.CH[:, 0:64]), T.MK[:, :], A.mult, ["S0", "Tr0", "CH0", "MK"],
+                    keys(k, 0, S))
+                conv("C0", z, m, 0, keys(k, 0, S), a0 == 0, a0 > 0)
+            return
+        conv("C0", "ZL", "TC", 0, keys("TC", 0, S))
+
+    def list_of_d(t):
+        if t:
+            vtt(T.DL[:, 0:64], T.C1[:, 0:64], T.SP[:, 4, t * 64:t * 64 + 64], A.mult, ["C1", "SP%d" % t], ["DL0"])
+            vtt(T.DL[:, 64:128], T.C0[:, 0:64], T.DL[:, 0:64], A.add, ["C0", "DL0"], ["DL1"])
+            vcopy(T.KL[:, 64:128], T.DL[:, 64:128], ["DL1"], ["KLd"])
+        else:
+            vcopy(T.KL[:, 64:128], T.C0[:, 0:64], ["C0"], ["KLd"])
 
     def open_sums(t):
-        add("S", lambda: SC.activation(T.XV[:, :], xown(t), AF.Copy), r=xk(t), w=["XV"])
         for c in "ABC" if t else "":
             a, b = CHUNKS[c]
             mms(FB[c], b - a, [("MM", RR[t % 2][:, a:b], 0)], True, False, keys("RS%d" % (t % 2), a, b))
-        for c in R1B:
-            if "n1:" + c in (GAIN if t else GAIN0).split():
-                a, b = CHUNKS[c]
-                mms(R1B[c], b - a, [("ID", xown(t, a, b), 0)], True, False, xk(t, a, b))
+        a, b = CHUNKS["C"]
+        mms("P1", b - a, [("ID", xown(t, a, b), 0)], True, False, xk(t, a, b))
 
     dma("Y", T.IN[:, 0:64], T.link[:, :], [], ["INl"], "ldl")
     dma("Y", xown(0), T.x[:, :], [], xk(0), "ldx")
     dma("Y", T.IN[:, 64:192], T.cand[:, 0:128], [], ["IN0"], "ldc")
+    dma("Y", T.XV[:, :], T.x[:, :], [], ["XV"], "ldv")
+    dma("Y", T.U[:, :], T.u[:, :], [], ["U"], "ldu")
+    dma("Y", T.IN[:, 192:448], T.cand[:, 128:384], [], ["IN"], "ldu")
     add("G", lambda: g.iota(T.PC[:, 0:1], [[1, 1]], 0, 1), w=["PC0"])
     add("G", lambda: g.iota(T.VAL[:, :], [[1, 144]], 0, 0, allow_small_or_imprecise_dtypes=True), w=["VAL"])
-    add("G", lambda: g.iota(T.V8[:, :], [[1, 16], [0, 8]], 0, 0, allow_small_or_imprecise_dtypes=True), w=["V8"])
-    add("V", lambda: V.memset(T.R0[:, :], 0.0), w=["Rf0", "Rf1"])
+    add("G", lambda: g.iota(T.R0[:, :], [[0, S]], 0, 0, allow_small_or_imprecise_dtypes=True), w=["Rf0", "Rf1"])
 
     def cf(j):
         return T.CF[:, j:j + 1]
@@ -282,13 +316,17 @@ def rank_program(g, core, T, topo):
     add("V", lambda: V.memset(T.MAT[:, :], 0.0), w=["MAT"])
     vts(T.HL[:, 0:64], T.IN[:, 0:64], 6, None, A.arith_shift_right, None, ["INl"], ["HI"])
     vts(T.HL[:, 64:128], T.IN[:, 0:64], 63, None, A.bitwise_and, None, ["INl"], ["LO"])
-    vcopy(T.S0[:, :], T.HL[:, 0:128], ["HI", "LO"], ["S0"])
+    vcopy(T.S0[:, q * 128:q * 128 + 128], T.HL[:, 0:128], ["HI", "LO"], ["S0"])
     for p, lane in enumerate([0, 3]):
-        dma("YS"[p], T.R0[lane:128:16, :], T.S0[:, p * 64:(p + 1) * 64], ["S0"], ["Rf%d" % p], "dfirst")
+        dma("YS"[p], T.R0[lane:128:16, :], T.S0[:, q * 128 + p * 64:q * 128 + p * 64 + 64], ["S0"], ["Rf%d" % p], "dfirst")
     vcopy(T.KL[:, 0:64], T.IN[:, 0:64], ["INl"], ["KLb"])
-    send(xown(0), "aX0", "lX0", xk(0) + ["KLb"])
+    send(T.S0[:, q * 128:q * 128 + 128], "aT0", "lTf", ["S0", "KLb"])
+    arrival("aT0", ["Tr0"])
+    send(xown(0), "aX0", "lX0", xk(0))
     arrival("aX0", ["Xr0"])
-    add("V", lambda: V.memset(T.R[:, :], 0.0), w=rk(0) + rk(1))
+    add("G", lambda: g.iota(T.R[:, :], [[0, S]], 0, 0, allow_small_or_imprecise_dtypes=True), w=rk)
+    drift_u(0, ["Tr0"])
+    drift_x(0)
     cols = {}
 
     def col(name):
@@ -313,6 +351,8 @@ def rank_program(g, core, T, topo):
             base = MATS.index(m) * 128
             if kind < 2:
                 out, gm = T.MAT[:, base + l:base + 128:16], T.GM[:, 8 * kind:8 * kind + 8]
+            elif kind > 3:
+                out, gm, kind = T.MAT[:, base + l:base + 128:16], T.GM[:, 12 + kind:32:2], 2
             else:
                 out, gm = T.MAT[:, base + l:base + 128:8], T.GM[:, 16 * kind - 16:16 * kind]
             key = "m%s%d" % (m, l)
@@ -324,8 +364,9 @@ def rank_program(g, core, T, topo):
             else:
                 add("S", lambda out=out, gm=gm, sc=sc: SC.activation(out, gm, AF.Identity, scale=sc), r=r, w=[key])
 
-    entries("S", [("BP", 0, None, 0), ("BP", 3, None, 1), ("BM", 0, None, 1), ("BM", 3, None, 0), ("MM", 1, 2, 0), ("MM", 2, 3, 0),
-                  ("Bc", 1, 13, 0), ("Ab", 6, 4, 0), ("Ab", 7, 5, 0)])
+    entries("S", [("BP", 0, None, 0), ("BP", 3, None, 1), ("BM", 0, None, 1), ("BM", 3, None, 0), ("M0", 1, 2, 0), ("M0", 2, 3, 0),
+                  ("Bc", 1, 13, 0), ("Kh", 4, None, 0), ("Kl", 7, None, 0)])
+    vts(T.MT[:, :], T.VAL[:, 0:16], cf(1), None, A.is_equal, None, ["VAL", "CF"], ["MT"])
     vts(T.GM[:, 16:32], T.VAL[:, 0:16], cf(3), None, A.is_equal, None, ["VAL", "CF"], ["GM2"])
     vts(T.GM[:, 32:48], T.VAL[:, 0:16], cf(3), -1.0, A.is_equal, A.mult, ["VAL", "CF"], ["GM3"])
     for name, a, b in [("03", 0, 3), ("36", 3, 6), ("68", 6, 8)]:
@@ -334,57 +375,70 @@ def rank_program(g, core, T, topo):
     axpy("k1", oh(1), 64.0, oh(2), ["OH"])
     axpy("eh", col("68"), -64.0, col("03"), ["c68", "c03"])
     axpy("el", col("68"), -64.0, col("36"), ["c68", "c36"])
-    axpy("cm", oh(14), 2.0, oh(15), ["OH"])
     vts(col("wk"), col("k0"), 4096.0, col("k1"), A.mult, A.subtract, ["ck0", "ck1"], ["cwk"])
+    vts(T.JV[:, 0:64], cand(0), 4, None, A.arith_shift_right, None, ["IN0"], ["JV0"])
+    vts(T.JV[:, 64:128], cand(0), 4, 192, A.arith_shift_right, A.bitwise_and, ["IN0"], ["JV1"])
+    vts(T.JV[:, 128:192], cand(0), 15, None, A.bitwise_and, None, ["IN0"], ["JV2"])
+    vtt(T.JV[:, 192:256], T.JV[:, 0:64], T.JV[:, 64:128], A.add, ["JV0", "JV1"], ["JV3"])
+    vcopy(T.CS[:, 0:64], T.JV[:, 128:192], ["JV2"], ["CS0"])
+    vcopy(T.CH[:, 0:64], T.JV[:, 192:256], ["JV3"], ["CH0"])
+    gather("S", T.MK[:, :], T.MT[:, :], T.CS[:, :], ["MT", "CS0"], ["MK"])
     vts(T.ID[:, :], T.VAL[:, 0:128], cf(0), None, A.is_equal, None, ["VAL", "CF"], ["ID"])
     vts(T.NI[:, :], T.VAL[:, 0:128], cf(0), -1.0, A.is_equal, A.mult, ["VAL", "CF"], ["NI"])
-    entries("S", [("Kd", 4, "eh", 0), ("Kd", 5, "el", 0), ("Bc", 4, "cm", 0),
-                  ("Bt", 0, "eh", 2), ("Bt", 1, "eh", 3), ("Bt", 2, "eh", 3), ("Bt", 3, "el", 2), ("Bt", 4, "el", 3), ("Bt", 5, "el", 3)])
+    entries("S", [("Bt", 0, "eh", 2), ("Bt", 1, "eh", 3), ("Bt", 2, "eh", 3), ("Bt", 3, "el", 2), ("Bt", 4, "el", 3), ("Bt", 5, "el", 3)])
     axpy("wt", oh(6), 256.0 * 4096.0, col("wk"), ["OH", "cwk"])
     axpy("wl", col("eh"), 64.0, col("el"), ["ceh", "cel"])
-    axpy("bk", col("k0"), -256.0, oh(6), ["ck0", "OH"])
+    axpy("b0", col("k0"), -256.0, oh(6), ["ck0", "OH"])
+    lanes("59", "OH", 5, 9, 3)
+    lanes("45", "OH", 4, 6)
+    lanes("89", "OH", 7, 9)
     vts(cf(8), cf(2), 16.0, 15.0, A.mult, A.add, ["CF"], ["CF8"])
-    vcopy(T.CL[:, 0:128], T.IN[:, 64:192], ["IN0"], ["CL0"])
-    vts(T.ZL[:, :], T.VAL[:, :], cf(8), col("wl"), A.is_equal, A.mult, ["VAL", "CF8", "cwl"], ["ZL"])
-    for h, (a, b) in enumerate(hv):
-        gather("VS"[h], T.T0[:, own + a:own + b], T.R0[:, :], T.PL[:, a // 16:b // 16], ["Rf0", "Rf1", "PL"], keys("Tf", a, b))
-    send(T.T0[:, own:own + S], "aT0", "lTf", keys("Tf", 0, S))
-    arrival("aT0", ["Tr0"])
+    axpy("bk", col("59"), -128.0, col("b0"), ["c59", "cb0"])
+    vts(T.Z6[:, :], T.VAL[:, :], cf(8), 64.0, A.is_equal, A.mult, ["VAL", "CF8"], ["Z6"])
+    vts(T.Z1[:, :], T.VAL[:, :], cf(8), None, A.is_equal, None, ["VAL", "CF8"], ["Z1"])
     open_sums(0)
     entries("S", [("Ao", 0, "wk", 0), ("Ao", 1, "wk", 0), ("Ao", 2, "wt", 0), ("Ao", 3, "wk", 1),
                   ("Ab", 0, "wk", 1), ("Ab", 3, "wk", 0), ("Ab", 4, "wk", 0), ("Ab", 5, "wt", 0), ("Ad", 1, "wk", 1), ("Ae", 4, "wk", 1)])
-    lanes("14", "O8", 1, 6, 3)
-    lanes("25", "O8", 2, 6, 3)
-    lanes("mb", "OH", 0, 8)
+    axpy("cm", oh(14), 2.0, oh(15), ["OH"])
+    axpy("we", col("45"), 64.0, col("89"), ["c45", "c89"])
+    lanes("ol", "O8", 0, 6, 3)
     vts(col("g1"), col("03"), 128.0, None, A.mult, None, ["c03"], ["cg1"])
     axpy("g2", col("36"), 128.0, o8(6), ["c36", "O8"])
     axpy("g5", col("36"), 128.0, o8(7), ["c36", "O8"])
-    axpy("we", oh(4), 64.0, oh(5), ["OH"])
     vts(col("cap"), col("68"), 63.0, 1.0, A.mult, A.add, ["c68"], ["ccap"])
-    vts(col("f2"), col("68"), -2.0, None, A.mult, None, ["c68"], ["cf2"])
-    vts(col("rd"), col("14"), col("25"), -320.0, A.add, A.mult, ["c14", "c25"], ["crd"])
+    vts(col("f2"), col("68"), 318.0, -320.0, A.mult, A.add, ["c68"], ["cf2"])
     vts(col("w0"), col("68"), float(NXAT[0] - XAT[0] - own), None, A.mult, None, ["c68"], ["cw0"])
-    vts(col("w1"), col("68"), float(NXAT[1] - XAT[1] - own), None, A.mult, None, ["c68"], ["cw1"])
     vts(cf(9), cf(5), cf(8), -1.0, A.add, A.add, ["CF", "CF8"], ["CF9"])
     vts(cf(10), pc(7), cf(5), 14.0, A.add, A.add, ["PC7", "CF"], ["CF10"])
-    vts(cf(11), cf(2), 2.0, None, A.mult, None, ["CF"], ["CF11"])
-    vts(cf(12), cf(2), 2.0, 1.0, A.mult, A.add, ["CF"], ["CF12"])
-    vts(col("bt"), col("rd"), col("f2"), None, A.add, None, ["crd", "cf2"], ["cbt"])
-    entries("S", [("Bs", 1, "g1", 2), ("Bs", 4, "g1", 2), ("Bs", 2, "g2", 2), ("Bs", 5, "g5", 2), ("Bs", 6, "03", 2), ("Bs", 7, "36", 2)])
-    for z, c, at in [("ZE", "we", 8), ("ZF", "wl", 9), ("ZV0", "w0", 10), ("ZV1", "w1", 10)]:
-        vts(T[z][:, :], T.VAL[:, :], cf(at), col(c), A.is_equal, A.mult, ["VAL", "CF%d" % at, "c" + c], [z])
-    vts(T.JV[:, 0:64], T.VR[:, :], 4032, None, A.bitwise_and, None, ["VR"], ["JV0"])
-    vts(T.JV[:, 64:128], T.VR[:, :], 63, None, A.bitwise_and, None, ["VR"], ["JV1"])
-    vts(T.Ma[:, :], T.V8[:, :], cf(11), oh(15), A.is_equal, A.mult, ["V8", "CF11", "OH"], ["Ma"])
-    vts(T.Mb[:, :], T.V8[:, :], cf(12), oh(15), A.is_equal, A.mult, ["V8", "CF12", "OH"], ["Mb"])
-    vcopy(T.SV[:, :], T.JV[:, :], ["JV0", "JV1"], ["SV"])
-    vtt(T.Mk[:, :], T.Mb[:, :], T.Ma[:, :], A.subtract, ["Ma", "Mb"], ["Mk"])
-    statics(0)
-    lay(0, [])
-    statics(1)
-    lay(1, [])
-    dma("Y", T.U[:, :], T.u[:, :], [], ["U"], "ldu")
-    dma("Y", T.IN[:, 192:448], T.cand[:, 128:384], [], ["IN"], "ldu")
+    axpy("bt", col("ol"), 320.0, col("f2"), ["col", "cf2"])
+    entries("S", [("Bc", 4, "cm", 0), ("Ab", 6, "45", 0), ("Ab", 7, "89", 0),
+                  ("Kg", 4, "eh", 4), ("Kg", 5, "eh", 5), ("Kg", 7, "el", 4), ("Kg", 8, "el", 5)])
+    statics(0, 1)
+    lay(0, ["Tr0"])
+
+    def weights(table):
+        for z, c, at in table:
+            vts(T[z][:, :], T.VAL[:, :], cf(at), col(c), A.is_equal, A.mult, ["VAL", "CF%d" % at, "c" + c], [z])
+
+    partners_of_c(0)
+
+    def late_constants():
+        gather("S", T.T0[:, :], T.R0[:, :], T.PL[:, :], ["Rf0", "Rf1", "PL"], ["Tf"])
+        entries("S", [("Bs", 1, "g1", 2), ("Bs", 4, "g1", 2), ("Bs", 2, "g2", 2), ("Bs", 5, "g5", 2), ("Bs", 6, "03", 2),
+                      ("Bs", 7, "36", 2), ("MM", 1, 2, 0), ("MM", 2, 3, 0)])
+        vts(T.JV[:, 0:64], T.VR[:, :], 4032, None, A.bitwise_and, None, ["VR"], ["JV0"])
+        vts(T.JV[:, 64:128], T.VR[:, :], 63, None, A.bitwise_and, None, ["VR"], ["JV1"])
+        weights([("ZE", "we", 8), ("ZF", "wl", 9), ("ZV0", "w0", 10)])
+        vcopy(T.SV[:, :], T.JV[:, 0:128], ["JV0", "JV1"], ["SV"])
+
+    def last_constants():
+        vts(col("wo"), col("wl"), cf(5), None, A.mult, None, ["cwl", "CF"], ["cwo"])
+        vts(col("sl"), oh(15), 128.0, None, A.mult, None, ["OH"], ["csl"])
+        vts(col("wv"), col("wl"), col("wo"), None, A.subtract, None, ["cwl", "cwo"], ["cwv"])
+        vts(col("w1"), col("68"), float(NXAT[1] - XAT[1] - own), None, A.mult, None, ["c68"], ["cw1"])
+        vts(col("wd"), col("wo"), col("wv"), None, A.subtract, None, ["cwo", "cwv"], ["cwd"])
+        entries("V", [("MM", 4, "sl", 1), ("MM", 5, "sl", 0), ("MM", 7, "sl", 1), ("MM", 8, "sl", 0)])
+        weights([("ZD", "wd", 8), ("ZL", "wv", 8), ("ZV1", "w1", 10)])
 
     for t in range(RO):
         first, last = t == 0, t + 1 == RO
@@ -392,30 +446,27 @@ def rank_program(g, core, T, topo):
         tn = "TA" if un == 0 else "TZ"
         xw = T.XX[:, XAT[u]:XAT[u] + W]
         xr = xk(t) + ["Xr%d" % u]
-        ck = "CL0" if t < 2 else "CL"
+        ck = "CL%d" % t
         todo = {c: 6 if first else 5 for c in "ABC"}
 
-        def look():
-            if first:
-                for h, (a, b) in enumerate(hv):
-                    gather("VS"[h], T.TC[:, a:b], T.T0[:, :], T.CL[:, a // 16:b // 16], keys("Tf", 0, S) + ["Tr0", ck], keys("TC", a, b))
-            else:
-                vtt(T.TC[:, :], TT[u][:, :].indirect(T.CH[:, t * 64:t * 64 + 64]), T.MK[:, :], A.mult,
-                    ["To%d0" % u, "To%d1" % u, "Tr%d" % u, "CH", "MK0", "MK1"], keys("TC", 0, S))
-
-        def gmax(m, other, r, a, b):
-            vtt(T[m][:, a:b], xw.indirect(T.CL[:, t * 64 + a // 16:t * 64 + b // 16]), other, A.max, xr + [ck] + r, keys(m, a, b))
+        def gmax(m, other, c):
+            a, b = CHUNKS[c]
+            vtt(T[m][:, a:b], xw.indirect(T.CL[:, t * 64 + a // 16:t * 64 + b // 16]), T[other][:, a:b], A.max,
+                xr + [ck] + (["XV"] if other == "XV" else keys(other, a, b)), keys(m, a, b))
 
         def summed(term, c):
             a, b = CHUNKS[c]
-            l, buf, k = {"0": ("MM", RR[u], "RS%d" % u), "1": ("BP", T.M1, "M1"), "2": ("BP", T.M2, "M2"),
-                         "3": ("BM", T.M3, "M3"), "4": ("BM", T.M4, "M4"), "5": ("Kd", T.TC, "TC")}[term]
+            l, buf, k = {"0": ("M0", RR[u], "RS%d" % u), "1": ("BP", T.M1, "M1"), "2": ("BP", T.M2, "M2"),
+                         "3": ("BM", T.M3, "M3"), "4": ("BM", T.M4, "M4"), "5": ("Kg", T.TC, "TC")}[term]
             todo[c] -= 1
-            mms(FB[c], b - a, [(l, buf[:, a:b], 0)], todo[c] == 5, todo[c] == 0, keys(k, a, b))
+            terms, r = [(l, buf[:, a:b], 0)], keys(k, a, b)
+            if first and term == "5":
+                terms, r = [("Kh", T.TC[:, a:b], 0), ("Kl", T.GK[:, a:b], 0)], r + keys("GK0", a, b)
+            mms(FB[c], b - a, terms, todo[c] == 5, todo[c] == 0, r)
 
-        def feat(buf, j, c, qu):
+        def feat(buf, j, c):
             a, b = CHUNKS[c]
-            gather(qu, T[buf][:, a:b], xw, T.KL[:, j * 64 + a // 16:j * 64 + b // 16], xr + ["KL" + "bd"[j]], keys(buf, a, b))
+            gather("S", T[buf][:, a:b], xw, T.KL[:, j * 64 + a // 16:j * 64 + b // 16], xr + ["KL" + "bd"[j]], keys(buf, a, b))
 
         def psum(bank, l, buf, c, start, stop):
             a, b = CHUNKS[c]
@@ -423,49 +474,53 @@ def rank_program(g, core, T, topo):
 
         def bmax(m, c):
             a, b = CHUNKS[c]
-            bank, o = ("P0", 0) if c == "A" else ("P2", 512)
             other, r = (xown(t, a, b), xk(t, a, b)) if m == "M1" else (T.XD[:, a:b], keys("XD", a, b))
-            vtt(T[m][:, a:b], T[bank][:, a - o:b - o], other, A.max, [bank] + r, keys(m, a, b))
+            vtt(T[m][:, a:b], T[PB[c]][:, 0:b - a], other, A.max, [PB[c]] + r, keys(m, a, b))
 
-        def over(m, bank, c, qu):
-            a, b = CHUNKS[c]
-            relu(qu, T[m][:, a:b], T[bank][:, 0:b - a], 0.0, [bank], keys(m, a, b))
+        def over(m, bank):
+            a, b = CHUNKS["C"]
+            relu("S", T[m][:, a:b], T[bank][:, 0:b - a], 0.0, [bank], keys(m, a, b))
 
         def ko(c, qu):
             a, b = CHUNKS[c]
             relu(qu, T.KK[:, own + a:own + b], T[FB[c]][:, 0:b - a], col("bk"), [FB[c], "cbk"], keys("Ko", a, b))
 
-        def m2(c):
+        def keys_out(c):
             a, b = CHUNKS[c]
-            gmax("M2", T.XD[:, a:b], keys("XD", a, b), a, b)
+            send(T.KK[:, own + a:own + b], "aK%d" % t, "lK" + c, keys("Ko", a, b))
 
         steps = {
-            "tc": look, "cd": lambda: conv("C0", "ZL", "TC", 0, keys("TC", 0, S)),
-            "kd": lambda: vcopy(T.KL[:, 64:128], T.C0[:, 0:64], ["C0"], ["KLd"]),
-            "m3": lambda a, b: gmax("M3", T.XV[:, int(a):int(b)], ["XV"], int(a), int(b)), "m2": m2,
-            "xb": lambda c, qu: feat("XB", 0, c, qu), "xd": lambda c, qu: feat("XD", 1, c, qu),
-            "pb": lambda c: psum("P0" if c == "A" else "P2", "ID", "XB", c, True, True),
-            "n1": lambda c: psum(R1B[c], "NI", "XB", c, False, True),
-            "n4": lambda c: psum(R4B[c], "NI", "XB", c, True, False), "d4": lambda c: psum(R4B[c], "ID", "XD", c, False, True),
+            "m3": lambda c: gmax("M3", "XV", c), "m2": lambda c: gmax("M2", "XD", c),
+            "xb": lambda c: feat("XB", 0, c), "xd": lambda c: feat("XD", 1, c),
+            "pb": lambda c: psum(PB[c], "ID", "XB", c, True, True), "n1": lambda: psum("P1", "NI", "XB", "C", False, True),
+            "n4": lambda: psum("C1", "NI", "XB", "C", True, False), "d4": lambda: psum("C1", "ID", "XD", "C", False, True),
             "m1": lambda c: bmax("M1", c), "m4": lambda c: bmax("M4", c),
-            "r1": lambda c, qu: over("M1", R1B[c], c, qu), "r4": lambda c, qu: over("M4", R4B[c], c, qu),
-            "s": summed, "ko": ko, "rs": lambda: order_lanes(0, 512),
-            "lay": lambda: last or lay(t + 1, ["Xr%d" % u]),
-            "send0": lambda: send(T.KK[:, own:own + 512], "aK%d" % t, "lK0", keys("Ko", 0, 512)),
-            "send1": lambda: send(T.KK[:, own + 512:own + S], "aK%d" % t, "lK1", keys("Ko", 512, S)),
+            "r1": lambda: over("M1", "P1"), "r4": lambda: over("M4", "C1"),
+            "kd": lambda: list_of_d(t), "s": summed, "ko": ko, "k": keys_out, "rs": lambda cut: order_lanes(0, int(cut)),
         }
+        if not first and not last:
+            lay(t + 1, ["Xr%d" % u])
+        if t + 2 < RO:
+            drift_u(t + 1, ["Xr%d" % u])
         for step in (GAIN0 if first else GAIN).split():
             name, *args = step.split(":")
             steps[name](*args)
         arrival("aK%d" % t, ["Kr"], calls=2)
         if not last:
-            build(t)
+            drift_over(t)
+        if first:
+            late_constants()
+            statics(1, 2)
+            lay(1, ["Kr"])
+        elif not last:
             order_lanes(t + 1)
+            if t + 2 < RO:
+                statics(t + 2, t + 3)
         for h, (a, b) in enumerate(PART):
             mms(DB[h], (b - a) // 2, pairs("Ao", T.KK, own + a, own + b), True, False, keys("Ko", a, b))
         for h, (a, b) in enumerate(PART):
             if first:
-                terms, r = pairs("Bt", T.T0, own + a, own + b), keys("Tf", a, b)
+                terms, r = pairs("Bt", T.T0, a, b), ["Tf"]
             else:
                 terms, r = [("Bt", TT[u][:, (own + a) // 2:(own + b) // 2], 0)], ["To%d%d" % (u, h)]
             mms(GB[h], (b - a) // 2, terms + pairs("Bc", RR[u], a, b), True, False, r + keys("RS%d" % u, a, b))
@@ -473,48 +528,33 @@ def rank_program(g, core, T, topo):
             mms("P2", 64, [("ID", T.SV[:, 0:64], 0), ("ID", T.SV[:, 64:128], 0)], True, False, ["SV"])
         kr = keys("Ko", 0, S) + ["Kr"]
         left = [3 * (b - a) for a, b in PART]
-        waiting = []
-
-        def differences():
-            for j, a, b in waiting:
-                for h, (c, d) in enumerate(PART):
-                    lo, hi = max(a, c), min(b, d)
-                    if lo < hi:
-                        left[h] -= hi - lo
-                        mms(DB[h], (hi - lo) // 2, pairs("A" + "bde"[j], T.GK, j * S + lo, j * S + hi), False, left[h] == 0,
-                            keys("GK%d" % j, lo, hi), o=(lo - c) // 2)
-            waiting.clear()
-
-        listed = False
         for step in DECIDE.split():
             name, *args = step.split(":")
-            if name in "VS":
-                j, a, b = "bde".index(args[0]), int(args[1]), int(args[2])
-                gather(name, T.GK[:, j * S + a:j * S + b], T.KK[:, :], T.KL[:, j * 64 + a // 16:j * 64 + b // 16],
-                       kr + ["KL" + args[0]], keys("GK%d" % j, a, b))
-                waiting.append((j, a, b))
-                if listed:
-                    differences()
+            if name in "VSp":
+                j, a = "bde".index(args[0]), 256 * int(args[1])
+                gk, gks = j * S + a, keys("GK%d" % j, a, a + 256)
+                if name == "p":
+                    h = [a < b for _, b in PART].index(True)
+                    left[h] -= 256
+                    mms(DB[h], 128, pairs("A" + args[0], T.GK, gk, gk + 256), False, left[h] == 0, gks, o=(a - PART[h][0]) // 2)
+                else:
+                    gather(name, T.GK[:, gk:gk + 256], T.KK[:, :], T.KL[:, gk // 16:gk // 16 + 16], kr + ["KL" + args[0]], gks)
             elif name == "ce":
                 conv("F2", "ZE", "GK", 0, keys("GK0", 0, S))
-                listed = True
-                differences()
-            elif name == "df":
-                differences()
             elif name == "le":
                 vcopy(T.KL[:, 128:192], T.F2[:, 0:64], ["F2"], ["KLe"])
-            elif name == "s":
+            else:
                 h = int(args[0])
                 a, b = PART[h]
                 sn = T.SN[:, a // 2:b // 2]
-                vts(sn, T[DB[h]][:, 0:(b - a) // 2], 0.0, col("cap"), A.max, A.min, [DB[h], "ccap"], ["SN%d" % h])
-                mms(GB[h], (b - a) // 2, [("Bs", sn, 0)], False, True, ["SN%d" % h])
-            elif name == "o":
-                h = int(args[0])
-                a, b = PART[h]
-                relu(args[1], TT[un][:, (own + a) // 2:(own + b) // 2], T[GB[h]][:, 0:(b - a) // 2], col("bt"),
-                     [GB[h], "cbt"], ["To%d%d" % (un, h)])
-        to = ["To%d0" % un, "To%d1" % un]
+                if name == "s":
+                    vts(sn, T[DB[h]][:, 0:(b - a) // 2], 0.0, col("cap"), A.max, A.min, [DB[h], "ccap"], ["SN%d" % h])
+                elif name == "bs":
+                    mms(GB[h], (b - a) // 2, [("Bs", sn, 0)], False, True, ["SN%d" % h])
+                else:
+                    relu(args[1], TT[un][:, (own + a) // 2:(own + b) // 2], T[GB[h]][:, 0:(b - a) // 2], col("bt"),
+                         [GB[h], "cbt"], ["To%d%d" % (un, h)])
+        to = ["To%d%d" % (un, h) for h in range(len(PART))]
         if last:
             conv2("C0", "ZF", tn, to)
             vcopy(T.Y[:, :], T.C0[:, 0:64], ["C0"], ["Y"])
@@ -527,20 +567,20 @@ def rank_program(g, core, T, topo):
         vts(T.AV[:, :], T.P2[:, 0:64], float(XAT[u] - lo), None, A.add, None, ["P2"], ["AV"])
         for h, (a, b) in enumerate(hv):
             gather("VS"[h], xown(t + 1, a, b), T.XX[:, lo:lo + S + W], T.AV[:, a // 16:b // 16],
-                   xr + ["N%d0" % u, "N%d1" % u, "AV"], xk(t + 1, a, b))
+                   xr + ["N%d" % u, "AV"], xk(t + 1, a, b))
         send(xown(t + 1), "aX%d" % (t + 1), "lX%d" % un, xk(t + 1))
         arrival("aX%d" % (t + 1), ["Xr%d" % un])
+        if t + 2 < RO:
+            drift_x(t + 1)
         conv2("F2", "ZF", tn, to)
-        for h, (a, b) in enumerate(hv):
-            mms(BB[h], 512, [("Mk", RR[un][:, a:b], 0)], True, True, keys("RS%d" % un, a, b))
-            relu("S", T.MK[:, a:b], T[BB[h]][:, :], col("mb"), [BB[h], "cmb"], ["MK%d" % h])
         vcopy(T.KL[:, 0:64], T.F2[:, 0:64], ["F2"], ["KLb"])
         if first:
-            vts(T.HL[:, :], T.IN[:, 128:448], 1, None, A.arith_shift_right, None, ["IN0", "IN"], ["HI", "LO"])
-            vcopy(T.CH[:, 64:384], T.HL[:, :], ["HI", "LO"], ["CH"])
-            vcopy(T.CL[:, 128:384], T.IN[:, 192:448], ["IN"], ["CL"])
-        if t + 2 < RO:
-            statics(t + 2)
+            order_lanes(1)
+            last_constants()
         open_sums(t + 1)
+        partners_of_c(t + 1)
+        add("S", lambda n=t + 1: SC.activation(T.XV[:, :], xown(n), AF.Copy), r=xk(t + 1), w=["XV"])
+        if first:
+            statics(2, 3)
 
     emit({"G": g, "V": V, "S": SC, "P": PE, "Y": SY}, T)

@@ -1,49 +1,49 @@
 from concourse.bass import DstId, RemoteDMATransfer
-from concourse.mybir import AluOpType as A, ActivationFunctionType as AF, AxisListType
+from concourse.mybir import AluOpType as A, ActivationFunctionType as AF
 
 RO, S, W, N = 6, 1024, 4096, 4
-H = S // 2
+Q4 = S // 4
 BF, F32, I32, U16 = "bfloat16", "float32", "int32", "uint16"
-CHUNKS = {"A": (0, 512), "B": (512, 768), "C": (768, 1024), "D": (512, 1024)}
-PART = [(0, 512), (512, 768), (768, 1024)]
-MATS = ["BP", "BM", "MM", "Kg", "M0", "Kh", "Kl", "Ao", "Ab", "Ad", "Ae", "Bc", "Bt", "Bs"]
+CHUNKS = {"A": (0, 448), "B": (448, 704), "C": (704, 1024), "D": (448, 1024), "a": (0, 256), "b": (256, 448)}
+DIFF = "C"
+MATS = ["BP", "BM", "Kg"]
+ZERO_GAIN = -256.0 * 4096.0
 
-GAIN = ("kd xb:A m3:A xd:A xb:D pb:A s:5:A s:5:B s:5:C m1:A xd:B xd:C m2:A s:3:A s:1:A pb:B m4:A m3:D n1 s:2:A s:4:A m1:B "
-        "r1 ko:A:S k:A n4 s:3:B m2:B d4 s:1:C s:3:C s:1:B m4:B r4 s:2:B s:4:B ko:B:S s:4:C m2:C s:2:C ko:C:V k:D")
-GAIN0 = ("m3:A kd xb:A xb:D xd:A pb:A m1:A rs:256 s:3:A s:5:A m2:A m4:A n1 m3:D n4 s:1:A pb:B xd:B s:5:C s:2:A s:0:A s:4:A "
-         "m4:B m1:B s:0:C r1 s:5:B s:3:B s:0:B m2:B xd:C d4 s:4:B s:1:B s:1:C ko:A:S k:A s:3:C s:2:B r4 s:4:C m2:C s:2:C "
-         "ko:B:S ko:C:V k:D")
-DECIDE = ("V:b:0 p:b:0 V:b:2 V:d:0 S:b:1 p:b:1 S:b:3 ce V:d:3 p:b:3 p:d:0 S:d:2 le p:b:2 S:d:1 V:e:0 S:e:1 p:d:3 p:d:1 "
-          "p:e:0 p:e:1 V:e:2 p:d:2 s:0 p:e:2 S:e:3 s:1 p:e:3 bs:0 bs:1 s:2 o:1:V bs:2 o:2:V o:0:S")
+TAIL = ("xd:C xd:B n1 pb:B m4:A s:2:A n4 s:4:A m3:C r1 ko:A:S k:A d4 m1:B s:3:C s:1:C r4 m2:C s:1:B m4:B s:2:C s:4:C m2:B "
+        "ko:C:S s:4:B s:2:B ko:B:V k:D")
+GAIN = ("xb:A m3:a s:5:A pb:A kd xd:A m3:b m3:B xb:D m1:A s:5:B s:3:A m2:A s:5:C s:3:B m4:A s:1:A m3:C xd:B xd:C n1 pb:B "
+        "s:2:A m1:B r1 s:4:A n4 d4 ko:A:S s:1:C s:3:C m2:C r4 m4:B k:A s:1:B m2:B s:2:C s:4:B s:4:C ko:C:S s:2:B ko:B:V k:D")
+GAIN0 = "xb:A m3:A pb:A tc xb:D m3:B m1:A kd xd:A s:3:A s:5:A s:1:A s:3:B s:5:B s:5:C m2:A " + TAIL
+CUT_C = 768
+CUT_D, CUT_E, CUT_X = 352, 640, 352
+BIG = 2.0 ** 23
 
 SCRATCH = {
-    "XX": ("sbuf", [128, 2 * (S + W)], BF), "KK": ("sbuf", [128, W], BF),
-    "TA": ("sbuf", [128, W // 2], BF), "TZ": ("sbuf", [128, W // 2], BF),
-    "U": ("sbuf", [128, S], BF), "SG": ("sbuf", [128, S], BF), "SN": ("sbuf", [128, H], BF),
-    "TC": ("sbuf", [128, S], BF), "MK": ("sbuf", [128, S], BF), "T0": ("sbuf", [128, S], BF),
+    "XX": ("sbuf", [128, 2 * (S + W)], BF), "KK": ("sbuf", [128, W], BF), "TT": ("sbuf", [128, W // 4], BF),
+    "SG": ("sbuf", [128, S], BF), "TC": ("sbuf", [128, S], BF), "MK": ("sbuf", [128, S], BF),
     "XV": ("sbuf", [128, S], BF), "XB": ("sbuf", [128, S], BF), "XD": ("sbuf", [128, S], BF),
     "M1": ("sbuf", [128, S], BF), "M2": ("sbuf", [128, S], BF), "M3": ("sbuf", [128, S], BF), "M4": ("sbuf", [128, S], BF),
-    "GK": ("sbuf", [128, 3 * S], BF),
-    "R0": ("sbuf", [128, S], BF), "R": ("sbuf", [128, S], BF), "RA": ("sbuf", [128, S], BF), "RZ": ("sbuf", [128, S], BF),
-    "IN": ("sbuf", [128, 7 * 64], I32), "HL": ("sbuf", [128, 640], I32),
-    "S0": ("sbuf", [128, N * 128], BF), "SV": ("sbuf", [128, 128], BF), "SP": ("sbuf", [128, 5, 384], BF),
-    "CL": ("sbuf", [128, 384], U16), "CH": ("sbuf", [128, 384], U16), "CS": ("sbuf", [128, 64], U16),
-    "KL": ("sbuf", [128, 192], U16), "PL": ("sbuf", [128, 64], U16), "AV": ("sbuf", [128, 64], U16),
-    "Y": ("sbuf", [128, 64], F32), "MN": ("sbuf", [128, 192], I32), "J": ("sbuf", [128, 5, 192], I32), "JV": ("sbuf", [128, 256], I32),
-    "VAL": ("sbuf", [128, 144], F32), "PC": ("sbuf", [128, 8], I32), "CF": ("sbuf", [128, 16], F32),
-    "OH": ("sbuf", [128, 16], F32), "O8": ("sbuf", [128, 8], F32), "GM": ("sbuf", [128, 48], F32), "WC": ("sbuf", [128, 48], F32),
-    "VR": ("sbuf", [128, 64], I32), "MT": ("sbuf", [128, 16], BF),
-    "ZL": ("sbuf", [128, 144], BF), "ZD": ("sbuf", [128, 144], BF), "ZE": ("sbuf", [128, 144], BF),
-    "ZF": ("sbuf", [128, 144], BF), "ZV0": ("sbuf", [128, 144], BF), "ZV1": ("sbuf", [128, 144], BF),
-    "MAT": ("sbuf", [128, len(MATS) * 128], BF), "ID": ("sbuf", [128, 128], BF), "NI": ("sbuf", [128, 128], BF),
-    "DL": ("sbuf", [128, 128], F32), "Z6": ("sbuf", [128, 144], BF), "Z1": ("sbuf", [128, 144], BF),
+    "GB": ("sbuf", [128, S], BF), "GZ": ("sbuf", [128, S], BF),
+    "IN": ("sbuf", [128, 7 * 64], I32), "J": ("sbuf", [128, 320], I32), "JY": ("sbuf", [128, 192], I32),
+    "BL": ("sbuf", [128, 128], BF), "MP": ("sbuf", [128, RO * 128], BF), "SV": ("sbuf", [128, 128], BF),
+    "DP": ("sbuf", [128, 256], BF), "PP": ("sbuf", [128, 256], BF), "FL": ("sbuf", [128, 256], BF),
+    "GD": ("sbuf", [128, S], BF), "N32": ("sbuf", [128, 128], F32),
+    "CL": ("sbuf", [128, RO * 64], U16), "CU": ("sbuf", [128, RO * 128], U16),
+    "KL": ("sbuf", [128, 256], U16), "ZP": ("sbuf", [128, 4, 144], BF), "AV": ("sbuf", [128, 64], U16), "L": ("sbuf", [128, 11, 64], F32),
+    "VAL": ("sbuf", [128, 152], F32), "PC": ("sbuf", [128, 8], I32), "CF": ("sbuf", [128, 16], F32),
+    "OH": ("sbuf", [128, 16], F32), "O4": ("sbuf", [128, 4], F32), "GM": ("sbuf", [128, 16], F32), "WC": ("sbuf", [128, 16], F32),
+    "VR": ("sbuf", [128, 64], I32), "MT": ("sbuf", [128, 16], BF), "ZS": ("sbuf", [128, 4, 152], BF), "ZZ": ("sbuf", [128, Q4], BF),
+    "ZD": ("sbuf", [128, 144], BF), "ZE": ("sbuf", [128, 144], BF), "ZK": ("sbuf", [128, 144], BF),
+    "MAT": ("sbuf", [128, len(MATS) * 128], BF), "ID": ("sbuf", [128, 152], BF), "Z1": ("sbuf", [128, 144], BF), "NI": ("sbuf", [128, 128], BF),
+    "I64": ("sbuf", [128, 128], BF), "SH0": ("sbuf", [128, 128], BF), "SH1": ("sbuf", [128, 128], BF),
     "F0": ("psum", [128, 512], F32), "F1": ("psum", [128, 512], F32), "F2": ("psum", [128, 512], F32),
     "P0": ("psum", [128, 512], F32), "P1": ("psum", [128, 512], F32), "P2": ("psum", [128, 512], F32),
     "C0": ("psum", [128, 512], F32), "C1": ("psum", [128, 512], F32),
 }
 PSUM = [k for k, v in SCRATCH.items() if v[0] == "psum"]
-SEMAPHORES = (["sV", "sS", "sP", "sG", "ldl", "ldc", "ldx", "ldu", "dfirst", "out", "lT0", "lT1", "lTf", "lX0", "lX1",
-               "lKA", "lKD", "ldv"] + ["%s%d" % (n, t) for n in ("aX", "aK", "aT", "dR", "dU", "dX", "dS") for t in range(RO)])
+SEMAPHORES = (["sV", "sS", "sP", "sG", "ldl", "ldc", "ldx", "ldu", "out", "lT", "lX0", "lX1", "lKA", "lKD", "ldv"]
+              + ["%s%d" % (n, t) for n in ("aX", "aK", "aT", "dU", "dX", "dS") for t in range(RO)])
+LISTS = ["KP", "NO", "KA", "KB", "B", "DC", "DE", "TA", "TB", "YA", "Y"]
 
 
 def make_plan():
@@ -125,9 +125,8 @@ def rank_program(g, core, T, topo):
     def arrival(sem, keys, calls=1):
         add("X", None, w=keys, sem=sem, inc=nen * len(peers) * calls)
 
-    def dma(qu, out, in_, r, w, sem):
-        e = SY if qu == "Y" else SC
-        add(qu, lambda: e.dma_start(out, in_), r=r, w=w, sem=sem, inc=16, whole=True)
+    def dma(out, in_, r, w, sem):
+        add("Y", lambda: SY.dma_start(out, in_), r=r, w=w, sem=sem, inc=16, whole=True)
 
     def vcopy(out, in_, r, w):
         add("V", lambda: V.tensor_copy(out, in_), r=r, w=w)
@@ -161,42 +160,52 @@ def rank_program(g, core, T, topo):
             return ins
         add("P", fn, r=r + [z], w=[bank], acc=not start)
 
-    def conv2(bank, z, src, r, start=True, rank=q):
+    def conv_half(bank, z, src, h, start, stop):
         def fn():
             for m in range(8):
-                ins = PE.matmul(T[bank][:, 0:64], T[z][:, 14 - 2 * m:142 - 2 * m], T[src][:, rank * H + m:(rank + 1) * H:8],
-                                start and m == 0, m == 7)
+                i = 8 * h + m
+                ins = PE.matmul(T[bank][:, 0:64], T[z][:, 15 - i:143 - i], T[src][:, 512 * h + m:512 * h + 512:8],
+                                start and i == 0, stop and i == 15)
             return ins
-        add("P", fn, r=r + [z], w=[bank], acc=not start)
+        add("P", fn, r=keys(src, 512 * h, 512 * h + 512) + [z], w=[bank], acc=h == 1 or not start)
 
-    matkeys = {"ID": ["ID"], "NI": ["NI"]}
+    def spread(lists, r, stop):
+        def fn():
+            todo = [(x, p, a) for x, p in lists for a in range(4)]
+            for n, (x, p, a) in enumerate(todo):
+                o = 12 + 4 * a - 4 * p
+                ins = PE.matmul(T.P0[:, a:Q4:4], T.ZS[:, a, o:o + 128], x, False, stop and n == len(todo) - 1)
+            return ins
+        add("P", fn, r=r + ["ZS%d" % a for a in range(4)], w=["P0"], acc=True)
 
-    def mat(l, up=0):
+    matkeys = {m: [m] for m in ("ID", "NI", "I64", "N32", "SH0", "SH1")}
+    matkeys.update({"ZZ": ["ZZ"], "LO": ["ZP2"]})
+
+    def mat(l):
         if l in MATS:
             m = MATS.index(l)
-            return T.MAT[:, m * 128 - up:(m + 1) * 128 - up]
-        return T[l][:, :]
+            return T.MAT[:, m * 128:(m + 1) * 128]
+        if l == "LO":
+            return T.ZP[:, 2, 8:136]
+        return T.ID[:, 12:140] if l == "ID" else T[l][:, 0:128]
 
-    def mms(bank, n, terms, start, stop, r, o=0):
+    def mms(bank, n, terms, start, stop, r):
         def fn():
-            for j, (l, x, up) in enumerate(terms):
-                ins = PE.matmul(T[bank][:, o:o + n], mat(l, up), x, start and j == 0, stop and j == len(terms) - 1)
+            for j, (l, x) in enumerate(terms):
+                ins = PE.matmul(T[bank][:, 0:n], mat(l), x, start and j == 0, stop and j == len(terms) - 1)
             return ins
-        add("P", fn, r=r + [k for l, _, _ in terms for k in matkeys[l]], w=[bank], acc=not start)
-
-    def pairs(l, buf, a, b):
-        return [(l, buf[:, a:b:2], 0), (l, buf[:, a + 1:b:2], 8)]
+        add("P", fn, r=r + [k for l, _ in terms for k in matkeys[l]], w=[bank], acc=not start)
 
     own = q * S
-    hv = [(0, 512), (512, S)]
     FB = {"A": "F0", "B": "F1", "C": "F2"}
     PB = {"A": "P0", "B": "P2"}
-    DB, GB = ["F0", "F1", "C0"], ["P0", "P1", "C1"]
-    TT, RR = [T.TA, T.TZ], [T.RA, T.RZ]
     XAT, NXAT = [S, S + W], [0, S + 2 * W]
 
-    def keys(name, a, b):
-        return ["%s%d" % (name, k) for k in range(a // 128, (b + 127) // 128)]
+    def keys(name, a=0, b=S):
+        return ["%s_%d" % (name, k) for k in range(a // 32, (b + 31) // 32)]
+
+    def lst(name):
+        return T.L[:, LISTS.index(name), :]
 
     def xown(n, a=0, b=S):
         return T.XX[:, XAT[n % 2] + own + a:XAT[n % 2] + own + b]
@@ -208,11 +217,11 @@ def rank_program(g, core, T, topo):
         return T.XX[:, NXAT[n % 2]:NXAT[n % 2] + S]
 
     def drift_u(n, extra):
-        dma("Y", nx(n), T.U[:, :], ["U"] + extra, ["N%d" % (n % 2)], "dU%d" % n)
+        dma(nx(n), T.u[:, :], extra, ["N%d" % (n % 2)], "dU%d" % n)
 
-    def drift_x(n):
-        add("G", lambda: g.dma_start(nx(n), xown(n), accum_op=A.add), r=xk(n) + ["N%d" % (n % 2)], w=["N%d" % (n % 2)],
-            sem="dX%d" % n, inc=16, whole=True)
+    def drift_x(n, extra):
+        add("G", lambda: g.dma_start(nx(n), xown(n), accum_op=A.add), r=xk(n) + ["N%d" % (n % 2)] + extra,
+            w=["N%d" % (n % 2)], sem="dX%d" % n, inc=16, whole=True)
 
     def drift_over(n):
         vts(T.SG[:, :], nx(n), 32.0, -32.0, A.is_ge, A.mult, ["N%d" % (n % 2)], ["SG"])
@@ -222,74 +231,80 @@ def rank_program(g, core, T, topo):
     def cand(t):
         return T.IN[:, 64 + t * 64:128 + t * 64]
 
-    def statics(t0, t1):
-        a, b, n = 64 * t0, 64 * t1, 64 * (t1 - t0)
-        c, k, rounds = T.IN[:, 64 + a:64 + b], ["IN0", "IN"][:1 + (t1 > 2)], range(t0, t1)
-        for t in rounds:
-            vtt(T.MN[:, 64 * t - a:64 * t - a + 64], cand(t), T.VR[:, :], A.min, k + ["VR"], ["MN%d" % (t - t0)])
-        vts(T.J[:, 2, 0:n], c, 6, None, A.arith_shift_right, None, k, ["J2"])
-        vts(T.J[:, 3, 0:n], c, 1, 31, A.arith_shift_right, A.bitwise_and, k, ["J3"])
-        vts(T.J[:, 4, 0:n], c, 1, None, A.bitwise_and, None, k, ["J4"])
-        mn = ["MN%d" % (t - t0) for t in rounds]
-        vts(T.J[:, 0, 0:n], T.MN[:, 0:n], 6, None, A.arith_shift_right, None, mn, ["J0"])
-        vts(T.J[:, 1, 0:n], T.MN[:, 0:n], 63, None, A.bitwise_and, None, mn, ["J1"])
-        if t0:
-            vts(T.HL[:, 0:n], c, 1, None, A.arith_shift_right, None, k, ["HI", "LO"])
-        vcopy(T.CL[:, a:b], c, k, ["CL%d" % t for t in rounds])
-        vcopy(T.SP[:, :, a:b], T.J[:, :, 0:n], ["J%d" % p for p in range(5)], ["SP%d" % t for t in rounds])
-        if t0:
-            vcopy(T.CH[:, a:b], T.HL[:, 0:n], ["HI", "LO"], ["CH%d" % t for t in rounds])
+    def pieces(out, x, r, w):
+        vts(out[0], x, 6, None, A.arith_shift_right, None, r, [w + "h"])
+        vts(out[1], x, 63, None, A.bitwise_and, None, r, [w + "l"])
 
-    rk = ["R%d" % p for p in range(5)]
+    def minima(t, between):
+        k = ["IN0" if t < 2 else "IN"]
+        vtt(T.J[:, 0:64], cand(t), T.VR[:, :], A.min, k + ["VR"], ["J0"])
+        between()
+        pieces([T.J[:, 64:128], T.J[:, 128:192]], T.J[:, 0:64], ["J0"], "J1")
 
-    def lay(t, extra):
-        for p, lane in enumerate([2, 3, 13, 14, 15]):
-            dma("Y", T.R[lane:128:16, :], T.SP[:, p, t * 64:t * 64 + 64], ["SP%d" % t] + extra, [rk[p]], "dR%d" % t)
+    def minima_out(t):
+        vcopy(T.MP[:, 128 * t:128 * t + 128], T.J[:, 64:192], ["J1h", "J1l"], ["MP%d" % t])
 
-    def order_lanes(t, cut=0):
-        for qu, a, b in [("V", 0, cut), ("S", cut, S)]:
-            if a < b:
-                gather(qu, RR[t % 2][:, a:b], T.R[:, :], T.PL[:, a // 16:b // 16], rk + ["PL"], keys("RS%d" % (t % 2), a, b))
+    def offsets(t):
+        k = ["IN0" if t < 2 else "IN"]
+        vts(T.J[:, 192:256], cand(t), 2, None, A.arith_shift_right, None, k, ["J3"])
+        vts(T.J[:, 256:320], cand(t), 3, None, A.bitwise_and, None, k, ["J4"])
+        vcopy(T.CL[:, 64 * t:64 * t + 64], cand(t), k, ["CL%d" % t])
+        vcopy(T.CU[:, 128 * t:128 * t + 128], T.J[:, 192:320], ["J3", "J4"], ["CU%d" % t])
 
-    def partners_of_c(t):
-        u = t % 2
-        if t:
-            for h, (a, b) in enumerate(hv):
-                gather("VS"[h], T.TC[:, a:b], TT[u][:, :], T.CH[:, t * 64 + a // 16:t * 64 + b // 16],
-                       ["To%d%d" % (u, k) for k in range(len(PART))] + ["Tr%d" % u, "CH%d" % t], keys("TC", a, b))
-            conv("C1", "ZD", "TC", 0, keys("TC", 0, S))
-        else:
-            for m, k, z, a0 in [("TC", "TC", "Z6", 0), ("GK", "GK0", "Z1", 64)]:
-                vtt(T[m][:, 0:S], T.S0[:, a0:a0 + 448].indirect(T.CH[:, 0:64]), T.MK[:, :], A.mult, ["S0", "Tr0", "CH0", "MK"],
-                    keys(k, 0, S))
-                conv("C0", z, m, 0, keys(k, 0, S), a0 == 0, a0 > 0)
-            return
-        conv("C0", "ZL", "TC", 0, keys("TC", 0, S))
+    def lane_mask(t):
+        gather("S", T.MK[:, :], T.MT[:, :], T.CU[:, 128 * t + 64:128 * t + 128], ["MT", "CU%d" % t], ["MK"])
 
-    def list_of_d(t):
-        if t:
-            vtt(T.DL[:, 0:64], T.C1[:, 0:64], T.SP[:, 4, t * 64:t * 64 + 64], A.mult, ["C1", "SP%d" % t], ["DL0"])
-            vtt(T.DL[:, 64:128], T.C0[:, 0:64], T.DL[:, 0:64], A.add, ["C0", "DL0"], ["DL1"])
-            vcopy(T.KL[:, 64:128], T.DL[:, 64:128], ["DL1"], ["KLd"])
-        else:
-            vcopy(T.KL[:, 64:128], T.C0[:, 0:64], ["C0"], ["KLd"])
+    def open_table(t):
+        if t == 0:
+            mms("P0", Q4, [("ZZ", T.ZZ[:, :])], True, False, [])
+            spread([(T.BL[:, 0:64], 0), (T.BL[:, 64:128], 1)], ["BL"], False)
+        spread([(T.MP[:, 128 * t:128 * t + 64], 2), (T.MP[:, 128 * t + 64:128 * t + 128], 3)], ["MP%d" % t], t == 0)
 
-    def open_sums(t):
-        for c in "ABC" if t else "":
-            a, b = CHUNKS[c]
-            mms(FB[c], b - a, [("MM", RR[t % 2][:, a:b], 0)], True, False, keys("RS%d" % (t % 2), a, b))
-        a, b = CHUNKS["C"]
-        mms("P1", b - a, [("ID", xown(t, a, b), 0)], True, False, xk(t, a, b))
+    def table_out(t):
+        vcopy(T.TT[:, q * Q4:(q + 1) * Q4], T.P0[:, 0:Q4], ["P0"], ["To"])
+        send(T.TT[:, q * Q4:(q + 1) * Q4], "aT%d" % t, "lT", ["To"])
+        arrival("aT%d" % t, ["Tr"])
 
-    dma("Y", T.IN[:, 0:64], T.link[:, :], [], ["INl"], "ldl")
-    dma("Y", xown(0), T.x[:, :], [], xk(0), "ldx")
-    dma("Y", T.IN[:, 64:192], T.cand[:, 0:128], [], ["IN0"], "ldc")
-    dma("Y", T.XV[:, :], T.x[:, :], [], ["XV"], "ldv")
-    dma("Y", T.U[:, :], T.u[:, :], [], ["U"], "ldu")
-    dma("Y", T.IN[:, 192:448], T.cand[:, 128:384], [], ["IN"], "ldu")
+    def look_up_c(t):
+        cut = CUT_C
+        r, k = ["To", "Tr", "CU%d" % t], 128 * t + cut // 16
+        vtt(T.TC[:, 0:cut], T.TT[:, :].indirect(T.CU[:, 128 * t:k]), T.MK[:, 0:cut], A.mult, r + ["MK"], keys("TC", 0, cut))
+        if cut < S:
+            mms("C1", S - cut, [("I64", T.MK[:, cut:S])], True, False, ["MK"])
+            gather("S", T.GZ[:, cut:S], T.TT[:, :], T.CU[:, k:128 * t + 64], r, keys("GZ", cut, S))
+            mms("C1", S - cut, [("ID", T.GZ[:, cut:S])], False, True, keys("GZ", cut, S))
+            relu("S", T.TC[:, cut:S], T.C1[:, 0:S - cut], -64.0, ["C1"], keys("TC", cut, S))
+        conv("C0", "ZD", "TC", 0, keys("TC"))
+
+    def partner_lists():
+        mms("F1", 128, [("ZZ", T.ZZ[:, 0:128])], True, False, [])
+
+        def fn():
+            for p, l in enumerate(["I64", "ID"]):
+                PE.matmul(T.F1[:, 0:64], mat(l), T.BL[:, 64 * p:64 * p + 64], False, False)
+                for h in range(2):
+                    for r in range(2):
+                        o = 8 + 8 * h - 8 * r
+                        ins = PE.matmul(T.F1[:, 64 + 32 * h:96 + 32 * h], T.ZP[:, 2 * p + h, o:o + 128],
+                                        T.BL[:, 64 * p + r:64 * p + 64:2], False, p + h + r == 3)
+            return ins
+        add("P", fn, r=["BL", "ID", "I64"] + ["ZP%d" % n for n in range(4)], w=["F1"], acc=True)
+        vcopy(T.KL[:, 0:128], T.F1[:, 0:128], ["F1"], ["KLb"])
+
+    def open_diff(t):
+        a, b = CHUNKS[DIFF]
+        mms("P1", b - a, [("ID", xown(t, a, b))], True, False, xk(t, a, b))
+
+    dma(xown(0), T.x[:, :], [], xk(0), "ldx")
+    dma(T.IN[:, 0:64], T.link[:, :], [], ["INl"], "ldl")
+    dma(T.IN[:, 64:192], T.cand[:, 0:128], [], ["IN0"], "ldc")
+    dma(T.XV[:, :], T.x[:, :], [], ["XV"], "ldv")
+    drift_u(0, [])
+    dma(T.IN[:, 192:448], T.cand[:, 128:384], [], ["IN"], "ldu")
     add("G", lambda: g.iota(T.PC[:, 0:1], [[1, 1]], 0, 1), w=["PC0"])
-    add("G", lambda: g.iota(T.VAL[:, :], [[1, 144]], 0, 0, allow_small_or_imprecise_dtypes=True), w=["VAL"])
-    add("G", lambda: g.iota(T.R0[:, :], [[0, S]], 0, 0, allow_small_or_imprecise_dtypes=True), w=["Rf0", "Rf1"])
+    add("G", lambda: g.iota(T.VAL[:, :], [[1, 152]], 0, 0, allow_small_or_imprecise_dtypes=True), w=["VAL"])
+    send(xown(0), "aX0", "lX0", xk(0))
+    arrival("aX0", ["Xr0"])
 
     def cf(j):
         return T.CF[:, j:j + 1]
@@ -297,36 +312,6 @@ def rank_program(g, core, T, topo):
     def pc(j):
         return T.PC[:, j:j + 1]
 
-    vts(pc(1), pc(0), 15, None, A.bitwise_and, None, ["PC0"], ["PC1"])
-    vts(pc(2), pc(0), 4, None, A.arith_shift_right, None, ["PC0"], ["PC2"])
-    vts(pc(3), pc(0), 3, None, A.arith_shift_right, None, ["PC0"], ["PC3"])
-    vts(pc(4), pc(0), 7, None, A.bitwise_and, None, ["PC0"], ["PC4"])
-    vts(pc(5), pc(0), 3, 1, A.arith_shift_right, A.bitwise_and, ["PC0"], ["PC5"])
-    vts(pc(6), pc(0), 112.0, None, A.add, None, ["PC0"], ["PC6"])
-    vcopy(T.CF[:, 0:6], T.PC[:, 0:6], ["PC%d" % j for j in range(6)], ["CF"])
-    vts(pc(7), pc(6), 112, None, A.bitwise_and, None, ["PC6"], ["PC7"])
-    vts(cf(6), cf(1), 64.0, None, A.mult, None, ["CF"], ["CF6"])
-    vts(cf(7), cf(1), float(own), None, A.add, None, ["CF"], ["CF7"])
-    vts(T.OH[:, :], T.VAL[:, 0:16], cf(1), None, A.is_equal, None, ["VAL", "CF"], ["OH"])
-    vts(T.O8[:, :], T.VAL[:, 0:8], cf(4), None, A.is_equal, None, ["VAL", "CF"], ["O8"])
-    vts(T.PL[:, :], T.VAL[:, 0:64], cf(6), None, A.add, None, ["VAL", "CF6"], ["PL"])
-    vts(T.VR[:, :], T.VAL[:, 0:64], 16.0, cf(7), A.mult, A.add, ["VAL", "CF7"], ["VR"])
-    vts(T.GM[:, 0:8], T.VAL[:, 0:8], cf(2), None, A.is_equal, None, ["VAL", "CF"], ["GM0"])
-    vts(T.GM[:, 8:16], T.VAL[:, 0:8], cf(2), -1.0, A.is_equal, A.mult, ["VAL", "CF"], ["GM1"])
-    add("V", lambda: V.memset(T.MAT[:, :], 0.0), w=["MAT"])
-    vts(T.HL[:, 0:64], T.IN[:, 0:64], 6, None, A.arith_shift_right, None, ["INl"], ["HI"])
-    vts(T.HL[:, 64:128], T.IN[:, 0:64], 63, None, A.bitwise_and, None, ["INl"], ["LO"])
-    vcopy(T.S0[:, q * 128:q * 128 + 128], T.HL[:, 0:128], ["HI", "LO"], ["S0"])
-    for p, lane in enumerate([0, 3]):
-        dma("YS"[p], T.R0[lane:128:16, :], T.S0[:, q * 128 + p * 64:q * 128 + p * 64 + 64], ["S0"], ["Rf%d" % p], "dfirst")
-    vcopy(T.KL[:, 0:64], T.IN[:, 0:64], ["INl"], ["KLb"])
-    send(T.S0[:, q * 128:q * 128 + 128], "aT0", "lTf", ["S0", "KLb"])
-    arrival("aT0", ["Tr0"])
-    send(xown(0), "aX0", "lX0", xk(0))
-    arrival("aX0", ["Xr0"])
-    add("G", lambda: g.iota(T.R[:, :], [[0, S]], 0, 0, allow_small_or_imprecise_dtypes=True), w=rk)
-    drift_u(0, ["Tr0"])
-    drift_x(0)
     cols = {}
 
     def col(name):
@@ -337,117 +322,90 @@ def rank_program(g, core, T, topo):
     def oh(l):
         return T.OH[:, l:l + 1]
 
-    def o8(l):
-        return T.O8[:, l:l + 1]
-
-    def lanes(name, src, a, b, step=1):
-        add("V", lambda: V.tensor_reduce(col(name), T[src][:, a:b:step], AxisListType.X, A.add), r=[src], w=["c" + name])
+    def o4(l):
+        return T.O4[:, l:l + 1]
 
     def axpy(name, x, a, y, r):
         vts(col(name), x, a, y, A.mult, A.add, r, ["c" + name])
 
-    def entries(qu, table):
-        for m, l, c, kind in table:
+    def entries(table):
+        for m, l, c, neg in table:
             base = MATS.index(m) * 128
-            if kind < 2:
-                out, gm = T.MAT[:, base + l:base + 128:16], T.GM[:, 8 * kind:8 * kind + 8]
-            elif kind > 3:
-                out, gm, kind = T.MAT[:, base + l:base + 128:16], T.GM[:, 12 + kind:32:2], 2
-            else:
-                out, gm = T.MAT[:, base + l:base + 128:8], T.GM[:, 16 * kind - 16:16 * kind]
+            out, gm = T.MAT[:, base + l:base + 128:16], T.GM[:, 8 * neg:8 * neg + 8]
             key = "m%s%d" % (m, l)
             matkeys.setdefault(m, []).append(key)
-            sc, r = (1.0, []) if c is None else (oh(c), ["OH"]) if isinstance(c, int) else (col(c), ["c" + c])
-            r = r + ["MAT", "GM%d" % kind]
-            if qu == "V":
-                vts(out, gm, sc, None, A.mult, None, r, [key])
-            else:
-                add("S", lambda out=out, gm=gm, sc=sc: SC.activation(out, gm, AF.Identity, scale=sc), r=r, w=[key])
+            sc, r = (1.0, []) if c is None else (o4(c), ["O4"])
+            add("S", lambda out=out, gm=gm, sc=sc: SC.activation(out, gm, AF.Identity, scale=sc), r=r + ["MAT", "GM%d" % neg], w=[key])
 
-    entries("S", [("BP", 0, None, 0), ("BP", 3, None, 1), ("BM", 0, None, 1), ("BM", 3, None, 0), ("M0", 1, 2, 0), ("M0", 2, 3, 0),
-                  ("Bc", 1, 13, 0), ("Kh", 4, None, 0), ("Kl", 7, None, 0)])
-    vts(T.MT[:, :], T.VAL[:, 0:16], cf(1), None, A.is_equal, None, ["VAL", "CF"], ["MT"])
-    vts(T.GM[:, 16:32], T.VAL[:, 0:16], cf(3), None, A.is_equal, None, ["VAL", "CF"], ["GM2"])
-    vts(T.GM[:, 32:48], T.VAL[:, 0:16], cf(3), -1.0, A.is_equal, A.mult, ["VAL", "CF"], ["GM3"])
-    for name, a, b in [("03", 0, 3), ("36", 3, 6), ("68", 6, 8)]:
-        lanes(name, "O8", a, b)
-    vts(col("k0"), oh(0), oh(3), None, A.subtract, None, ["OH"], ["ck0"])
-    axpy("k1", oh(1), 64.0, oh(2), ["OH"])
-    axpy("eh", col("68"), -64.0, col("03"), ["c68", "c03"])
-    axpy("el", col("68"), -64.0, col("36"), ["c68", "c36"])
-    vts(col("wk"), col("k0"), 4096.0, col("k1"), A.mult, A.subtract, ["ck0", "ck1"], ["cwk"])
-    vts(T.JV[:, 0:64], cand(0), 4, None, A.arith_shift_right, None, ["IN0"], ["JV0"])
-    vts(T.JV[:, 64:128], cand(0), 4, 192, A.arith_shift_right, A.bitwise_and, ["IN0"], ["JV1"])
-    vts(T.JV[:, 128:192], cand(0), 15, None, A.bitwise_and, None, ["IN0"], ["JV2"])
-    vtt(T.JV[:, 192:256], T.JV[:, 0:64], T.JV[:, 64:128], A.add, ["JV0", "JV1"], ["JV3"])
-    vcopy(T.CS[:, 0:64], T.JV[:, 128:192], ["JV2"], ["CS0"])
-    vcopy(T.CH[:, 0:64], T.JV[:, 192:256], ["JV3"], ["CH0"])
-    gather("S", T.MK[:, :], T.MT[:, :], T.CS[:, :], ["MT", "CS0"], ["MK"])
-    vts(T.ID[:, :], T.VAL[:, 0:128], cf(0), None, A.is_equal, None, ["VAL", "CF"], ["ID"])
-    vts(T.NI[:, :], T.VAL[:, 0:128], cf(0), -1.0, A.is_equal, A.mult, ["VAL", "CF"], ["NI"])
-    entries("S", [("Bt", 0, "eh", 2), ("Bt", 1, "eh", 3), ("Bt", 2, "eh", 3), ("Bt", 3, "el", 2), ("Bt", 4, "el", 3), ("Bt", 5, "el", 3)])
-    axpy("wt", oh(6), 256.0 * 4096.0, col("wk"), ["OH", "cwk"])
-    axpy("wl", col("eh"), 64.0, col("el"), ["ceh", "cel"])
-    axpy("b0", col("k0"), -256.0, oh(6), ["ck0", "OH"])
-    lanes("59", "OH", 5, 9, 3)
-    lanes("45", "OH", 4, 6)
-    lanes("89", "OH", 7, 9)
+    def scaled(out, x, sc, r, w):
+        if isinstance(sc, str):
+            sc, r = col(sc), r + ["c" + sc]
+        add("S", lambda: SC.activation(out, x, AF.Identity, scale=sc), r=r, w=w)
+
+    add("V", lambda: V.memset(T.ZZ[:, :], 0.0), w=["ZZ"])
+    add("V", lambda: V.memset(T.MAT[:, :], 0.0), w=["MAT"])
+    vts(pc(1), pc(0), 15, None, A.bitwise_and, None, ["PC0"], ["PC1"])
+    vts(pc(2), pc(0), 4, None, A.arith_shift_right, None, ["PC0"], ["PC2"])
+    vts(pc(3), pc(0), 2, 3, A.arith_shift_right, A.bitwise_and, ["PC0"], ["PC3"])
+    vts(pc(4), pc(0), 3, None, A.bitwise_and, None, ["PC0"], ["PC4"])
+    vts(pc(5), pc(0), 112.0, None, A.add, None, ["PC0"], ["PC5"])
+    vts(cf(6), pc(0), 12.0, None, A.add, None, ["PC0"], ["CF6"])
+    vcopy(T.CF[:, 0:5], T.PC[:, 0:5], ["PC%d" % j for j in range(5)], ["CF"])
+    vts(pc(6), pc(5), 127, None, A.bitwise_and, None, ["PC5"], ["PC6"])
+    vts(T.O4[:, :], T.VAL[:, 0:4], cf(3), None, A.is_equal, None, ["VAL", "CF"], ["O4"])
+    vts(cf(7), cf(1), float(own), None, A.add, None, ["CF"], ["CF7"])
+    vts(T.GM[:, 0:8], T.VAL[:, 0:8], cf(2), None, A.is_equal, None, ["VAL", "CF"], ["GM0"])
+    vts(T.GM[:, 8:16], T.VAL[:, 0:8], cf(2), -1.0, A.is_equal, A.mult, ["VAL", "CF"], ["GM1"])
+    vts(T.VR[:, :], T.VAL[:, 0:64], 16.0, cf(7), A.mult, A.add, ["VAL", "CF7"], ["VR"])
+    vts(T.ID[:, :], T.VAL[:, :], cf(6), None, A.is_equal, None, ["VAL", "CF6"], ["ID"])
+    for a in range(4):
+        scaled(T.ZS[:, a, :], T.ID[:, :], o4(a), ["ID", "O4"], ["ZS%d" % a])
+    entries([("BP", 0, None, 0), ("BP", 1, None, 1), ("BM", 0, None, 1), ("BM", 1, None, 0),
+             ("Kg", 4, 0, 0), ("Kg", 5, 1, 0), ("Kg", 2, 2, 0), ("Kg", 3, 3, 0)])
+    vts(T.MT[:, :], T.VAL[:, 0:16], cf(4), None, A.is_equal, None, ["VAL", "CF"], ["MT"])
     vts(cf(8), cf(2), 16.0, 15.0, A.mult, A.add, ["CF"], ["CF8"])
-    axpy("bk", col("59"), -128.0, col("b0"), ["c59", "cb0"])
-    vts(T.Z6[:, :], T.VAL[:, :], cf(8), 64.0, A.is_equal, A.mult, ["VAL", "CF8"], ["Z6"])
-    vts(T.Z1[:, :], T.VAL[:, :], cf(8), None, A.is_equal, None, ["VAL", "CF8"], ["Z1"])
-    open_sums(0)
-    entries("S", [("Ao", 0, "wk", 0), ("Ao", 1, "wk", 0), ("Ao", 2, "wt", 0), ("Ao", 3, "wk", 1),
-                  ("Ab", 0, "wk", 1), ("Ab", 3, "wk", 0), ("Ab", 4, "wk", 0), ("Ab", 5, "wt", 0), ("Ad", 1, "wk", 1), ("Ae", 4, "wk", 1)])
-    axpy("cm", oh(14), 2.0, oh(15), ["OH"])
-    axpy("we", col("45"), 64.0, col("89"), ["c45", "c89"])
-    lanes("ol", "O8", 0, 6, 3)
-    vts(col("g1"), col("03"), 128.0, None, A.mult, None, ["c03"], ["cg1"])
-    axpy("g2", col("36"), 128.0, o8(6), ["c36", "O8"])
-    axpy("g5", col("36"), 128.0, o8(7), ["c36", "O8"])
-    vts(col("cap"), col("68"), 63.0, 1.0, A.mult, A.add, ["c68"], ["ccap"])
-    vts(col("f2"), col("68"), 318.0, -320.0, A.mult, A.add, ["c68"], ["cf2"])
-    vts(col("w0"), col("68"), float(NXAT[0] - XAT[0] - own), None, A.mult, None, ["c68"], ["cw0"])
-    vts(cf(9), cf(5), cf(8), -1.0, A.add, A.add, ["CF", "CF8"], ["CF9"])
-    vts(cf(10), pc(7), cf(5), 14.0, A.add, A.add, ["PC7", "CF"], ["CF10"])
-    axpy("bt", col("ol"), 320.0, col("f2"), ["col", "cf2"])
-    entries("S", [("Bc", 4, "cm", 0), ("Ab", 6, "45", 0), ("Ab", 7, "89", 0),
-                  ("Kg", 4, "eh", 4), ("Kg", 5, "eh", 5), ("Kg", 7, "el", 4), ("Kg", 8, "el", 5)])
-    statics(0, 1)
-    lay(0, ["Tr0"])
-
-    def weights(table):
-        for z, c, at in table:
-            vts(T[z][:, :], T.VAL[:, :], cf(at), col(c), A.is_equal, A.mult, ["VAL", "CF%d" % at, "c" + c], [z])
-
-    partners_of_c(0)
-
-    def late_constants():
-        gather("S", T.T0[:, :], T.R0[:, :], T.PL[:, :], ["Rf0", "Rf1", "PL"], ["Tf"])
-        entries("S", [("Bs", 1, "g1", 2), ("Bs", 4, "g1", 2), ("Bs", 2, "g2", 2), ("Bs", 5, "g5", 2), ("Bs", 6, "03", 2),
-                      ("Bs", 7, "36", 2), ("MM", 1, 2, 0), ("MM", 2, 3, 0)])
-        vts(T.JV[:, 0:64], T.VR[:, :], 4032, None, A.bitwise_and, None, ["VR"], ["JV0"])
-        vts(T.JV[:, 64:128], T.VR[:, :], 63, None, A.bitwise_and, None, ["VR"], ["JV1"])
-        weights([("ZE", "we", 8), ("ZF", "wl", 9), ("ZV0", "w0", 10)])
-        vcopy(T.SV[:, :], T.JV[:, 0:128], ["JV0", "JV1"], ["SV"])
-
-    def last_constants():
-        vts(col("wo"), col("wl"), cf(5), None, A.mult, None, ["cwl", "CF"], ["cwo"])
-        vts(col("sl"), oh(15), 128.0, None, A.mult, None, ["OH"], ["csl"])
-        vts(col("wv"), col("wl"), col("wo"), None, A.subtract, None, ["cwl", "cwo"], ["cwv"])
-        vts(col("w1"), col("68"), float(NXAT[1] - XAT[1] - own), None, A.mult, None, ["c68"], ["cw1"])
-        vts(col("wd"), col("wo"), col("wv"), None, A.subtract, None, ["cwo", "cwv"], ["cwd"])
-        entries("V", [("MM", 4, "sl", 1), ("MM", 5, "sl", 0), ("MM", 7, "sl", 1), ("MM", 8, "sl", 0)])
-        weights([("ZD", "wd", 8), ("ZL", "wv", 8), ("ZV1", "w1", 10)])
+    vcopy(cf(9), pc(6), ["PC6"], ["CF9"])
+    vts(T.OH[:, :], T.VAL[:, 0:16], cf(1), None, A.is_equal, None, ["VAL", "CF"], ["OH"])
+    axpy("wd", o4(0), 64.0, o4(1), ["O4"])
+    vts(T.Z1[:, :], T.VAL[:, 0:144], cf(8), None, A.is_equal, None, ["VAL", "CF8"], ["Z1"])
+    for m, sc in [("I64", 64.0), ("NI", -1.0)]:
+        scaled(mat(m), mat("ID"), sc, ["ID"], [m])
+    scaled(T.ZD[:, :], T.Z1[:, :], "wd", ["Z1"], ["ZD"])
+    for h in range(2):
+        vts(col("l%d" % h), o4(2 * h), o4(2 * h + 1), None, A.add, None, ["O4"], ["cl%d" % h])
+        vts(col("h%d" % h), o4(2 * h), o4(2 * h + 1), 64.0, A.add, A.mult, ["O4"], ["ch%d" % h])
+    for n, c in enumerate(["h0", "h1", "l0", "l1"]):
+        scaled(T.ZP[:, n, :], T.ID[:, 4:148], c, ["ID"], ["ZP%d" % n])
+    minima(0, lambda: pieces([T.JY[:, 64:128], T.JY[:, 128:192]], T.IN[:, 0:64], ["INl"], "JY"))
+    vcopy(T.BL[:, :], T.JY[:, 64:192], ["JYh", "JYl"], ["BL"])
+    minima_out(0)
+    open_table(0)
+    offsets(0)
+    lane_mask(0)
+    table_out(0)
+    vts(col("k0"), oh(0), oh(1), None, A.subtract, None, ["OH"], ["ck0"])
+    axpy("k1", oh(2), 64.0, oh(3), ["OH"])
+    axpy("we", oh(4), 64.0, oh(5), ["OH"])
+    vts(col("wk"), col("k0"), 4096.0, col("k1"), A.mult, A.subtract, ["ck0", "ck1"], ["cwk"])
+    vts(col("bk"), col("k0"), -256.0, None, A.mult, None, ["ck0"], ["cbk"])
+    partner_lists()
+    for z, c in [("ZK", "wk"), ("ZE", "we")]:
+        scaled(T[z][:, :], T.Z1[:, :], c, ["Z1"], [z])
+    scaled(T.N32[:, :], mat("ID"), -1.0, ["ID"], ["N32"])
+    for u in range(2):
+        vts(T["SH%d" % u][:, :], T.VAL[:, 0:128], cf(9), float(NXAT[u] - XAT[u] - own), A.is_equal, A.mult, ["VAL", "CF9"], ["SH%d" % u])
+    pieces([T.JY[:, 64:128], T.JY[:, 128:192]], T.VR[:, :], ["VR"], "JY")
+    offsets(1)
+    vcopy(T.SV[:, :], T.JY[:, 64:192], ["JYh", "JYl"], ["SV"])
+    open_diff(0)
 
     for t in range(RO):
         first, last = t == 0, t + 1 == RO
         u, un = t % 2, (t + 1) % 2
-        tn = "TA" if un == 0 else "TZ"
         xw = T.XX[:, XAT[u]:XAT[u] + W]
         xr = xk(t) + ["Xr%d" % u]
         ck = "CL%d" % t
-        todo = {c: 6 if first else 5 for c in "ABC"}
+        todo = {c: 5 for c in "ABC"}
 
         def gmax(m, other, c):
             a, b = CHUNKS[c]
@@ -456,30 +414,26 @@ def rank_program(g, core, T, topo):
 
         def summed(term, c):
             a, b = CHUNKS[c]
-            l, buf, k = {"0": ("M0", RR[u], "RS%d" % u), "1": ("BP", T.M1, "M1"), "2": ("BP", T.M2, "M2"),
-                         "3": ("BM", T.M3, "M3"), "4": ("BM", T.M4, "M4"), "5": ("Kg", T.TC, "TC")}[term]
             todo[c] -= 1
-            terms, r = [(l, buf[:, a:b], 0)], keys(k, a, b)
-            if first and term == "5":
-                terms, r = [("Kh", T.TC[:, a:b], 0), ("Kl", T.GK[:, a:b], 0)], r + keys("GK0", a, b)
-            mms(FB[c], b - a, terms, todo[c] == 5, todo[c] == 0, r)
+            l, buf = ("Kg", "TC") if term == "5" else ("BP" if term in "12" else "BM", "M" + term)
+            mms(FB[c], b - a, [(l, T[buf][:, a:b])], todo[c] == 4, todo[c] == 0, keys(buf, a, b))
 
-        def feat(buf, j, c):
+        def feat(buf, j, c, qu="S"):
             a, b = CHUNKS[c]
-            gather("S", T[buf][:, a:b], xw, T.KL[:, j * 64 + a // 16:j * 64 + b // 16], xr + ["KL" + "bd"[j]], keys(buf, a, b))
+            gather(qu, T[buf][:, a:b], xw, T.KL[:, j * 128 + a // 16:j * 128 + b // 16], xr + ["KL" + "bd"[j]], keys(buf, a, b))
 
         def psum(bank, l, buf, c, start, stop):
             a, b = CHUNKS[c]
-            mms(bank, b - a, [(l, T[buf][:, a:b], 0)], start, stop, keys(buf, a, b))
+            mms(bank, b - a, [(l, T[buf][:, a:b])], start, stop, keys(buf, a, b))
 
         def bmax(m, c):
             a, b = CHUNKS[c]
             other, r = (xown(t, a, b), xk(t, a, b)) if m == "M1" else (T.XD[:, a:b], keys("XD", a, b))
             vtt(T[m][:, a:b], T[PB[c]][:, 0:b - a], other, A.max, [PB[c]] + r, keys(m, a, b))
 
-        def over(m, bank):
-            a, b = CHUNKS["C"]
-            relu("S", T[m][:, a:b], T[bank][:, 0:b - a], 0.0, [bank], keys(m, a, b))
+        def over(m, bank, c, o):
+            a, b = CHUNKS[c]
+            relu("S", T[m][:, a:b], T[bank][:, a - o:b - o], 0.0, [bank], keys(m, a, b))
 
         def ko(c, qu):
             a, b = CHUNKS[c]
@@ -489,98 +443,118 @@ def rank_program(g, core, T, topo):
             a, b = CHUNKS[c]
             send(T.KK[:, own + a:own + b], "aK%d" % t, "lK" + c, keys("Ko", a, b))
 
+        def list_of_d():
+            vcopy(T.KL[:, 128:192], T.C0[:, 0:64], ["C0"], ["KLd"])
+
         steps = {
             "m3": lambda c: gmax("M3", "XV", c), "m2": lambda c: gmax("M2", "XD", c),
-            "xb": lambda c: feat("XB", 0, c), "xd": lambda c: feat("XD", 1, c),
-            "pb": lambda c: psum(PB[c], "ID", "XB", c, True, True), "n1": lambda: psum("P1", "NI", "XB", "C", False, True),
+            "xb": lambda c: feat("XB", 0, c), "xd": lambda c, qu="S": feat("XD", 1, c, qu),
+            "pb": lambda c: psum(PB[c], "ID", "XB", c, True, True), "n1": lambda: psum("P1", "NI", "XB", DIFF, False, True),
             "n4": lambda: psum("C1", "NI", "XB", "C", True, False), "d4": lambda: psum("C1", "ID", "XD", "C", False, True),
             "m1": lambda c: bmax("M1", c), "m4": lambda c: bmax("M4", c),
-            "r1": lambda: over("M1", "P1"), "r4": lambda: over("M4", "C1"),
-            "kd": lambda: list_of_d(t), "s": summed, "ko": ko, "k": keys_out, "rs": lambda cut: order_lanes(0, int(cut)),
+            "r1": lambda c="C": over("M1", "P1", c, CHUNKS[DIFF][0]), "r4": lambda: over("M4", "C1", "C", CHUNKS["C"][0]),
+            "kd": list_of_d, "tc": lambda: look_up_c(0), "s": summed, "ko": ko, "k": keys_out,
         }
-        if not first and not last:
-            lay(t + 1, ["Xr%d" % u])
+        if not last:
+            drift_x(t, ["Xr%d" % u])
         if t + 2 < RO:
             drift_u(t + 1, ["Xr%d" % u])
         for step in (GAIN0 if first else GAIN).split():
             name, *args = step.split(":")
             steps[name](*args)
         arrival("aK%d" % t, ["Kr"], calls=2)
+        conv("F1", "ZK", "KK", own, keys("Ko"))
         if not last:
+            mms("P0", Q4, [("LO", T.TT[:, q * Q4:(q + 1) * Q4])], True, False, ["To"])
+            mms("P2", 64, [("I64", T.SV[:, 0:64]), ("ID", T.SV[:, 64:128])], True, False, ["SV"])
+            lane_mask(t + 1)
             drift_over(t)
-        if first:
-            late_constants()
-            statics(1, 2)
-            lay(1, ["Kr"])
-        elif not last:
-            order_lanes(t + 1)
-            if t + 2 < RO:
-                statics(t + 2, t + 3)
-        for h, (a, b) in enumerate(PART):
-            mms(DB[h], (b - a) // 2, pairs("Ao", T.KK, own + a, own + b), True, False, keys("Ko", a, b))
-        for h, (a, b) in enumerate(PART):
-            if first:
-                terms, r = pairs("Bt", T.T0, a, b), ["Tf"]
-            else:
-                terms, r = [("Bt", TT[u][:, (own + a) // 2:(own + b) // 2], 0)], ["To%d%d" % (u, h)]
-            mms(GB[h], (b - a) // 2, terms + pairs("Bc", RR[u], a, b), True, False, r + keys("RS%d" % u, a, b))
-        if not last:
-            mms("P2", 64, [("ID", T.SV[:, 0:64], 0), ("ID", T.SV[:, 64:128], 0)], True, False, ["SV"])
-        kr = keys("Ko", 0, S) + ["Kr"]
-        left = [3 * (b - a) for a, b in PART]
-        for step in DECIDE.split():
-            name, *args = step.split(":")
-            if name in "VSp":
-                j, a = "bde".index(args[0]), 256 * int(args[1])
-                gk, gks = j * S + a, keys("GK%d" % j, a, a + 256)
-                if name == "p":
-                    h = [a < b for _, b in PART].index(True)
-                    left[h] -= 256
-                    mms(DB[h], 128, pairs("A" + args[0], T.GK, gk, gk + 256), False, left[h] == 0, gks, o=(a - PART[h][0]) // 2)
-                else:
-                    gather(name, T.GK[:, gk:gk + 256], T.KK[:, :], T.KL[:, gk // 16:gk // 16 + 16], kr + ["KL" + args[0]], gks)
-            elif name == "ce":
-                conv("F2", "ZE", "GK", 0, keys("GK0", 0, S))
-            elif name == "le":
-                vcopy(T.KL[:, 128:192], T.F2[:, 0:64], ["F2"], ["KLe"])
-            else:
-                h = int(args[0])
-                a, b = PART[h]
-                sn = T.SN[:, a // 2:b // 2]
-                if name == "s":
-                    vts(sn, T[DB[h]][:, 0:(b - a) // 2], 0.0, col("cap"), A.max, A.min, [DB[h], "ccap"], ["SN%d" % h])
-                elif name == "bs":
-                    mms(GB[h], (b - a) // 2, [("Bs", sn, 0)], False, True, ["SN%d" % h])
-                else:
-                    relu(args[1], TT[un][:, (own + a) // 2:(own + b) // 2], T[GB[h]][:, 0:(b - a) // 2], col("bt"),
-                         [GB[h], "cbt"], ["To%d%d" % (un, h)])
-        to = ["To%d%d" % (un, h) for h in range(len(PART))]
+            minima(t + 1, lambda: pieces([T.JY[:, 64:128], T.JY[:, 128:192]], cand(t), ["IN0", "IN"], "JY"))
+        vts(lst("KP"), T.F1[:, 0:64], ZERO_GAIN, None, A.max, None, ["F1"], ["KP"])
+        vts(lst("NO"), T.F1[:, 0:64], ZERO_GAIN, -BIG, A.is_le, A.mult, ["F1"], ["NO"])
+        mms("C1", 64, [("N32", lst("KP"))], True, False, ["KP"])
         if last:
-            conv2("C0", "ZF", tn, to)
-            vcopy(T.Y[:, :], T.C0[:, 0:64], ["C0"], ["Y"])
-            dma("Y", T.ylink[:, :], T.Y[:, :], ["Y"], ["y"], "out")
+            vcopy(lst("B"), T.KL[:, 0:64], ["KLb"], ["B"])
+            vtt(lst("DC"), cand(t), lst("B"), A.subtract, ["IN", "B"], ["DC"])
+        else:
+            minima_out(t + 1)
+            open_table(t + 1)
+            vtt(T.DP[:, 0:128], T.JY[:, 64:192], T.BL[:, :], A.subtract, ["JYh", "JYl", "BL"], ["DC"])
+            mms("F1", 128, [("NI", T.BL[:, :])], True, False, ["BL"])
+        vtt(lst("KA"), lst("KP"), lst("NO"), A.add, ["KP", "NO"], ["KA"])
+        kr = keys("Ko") + ["Kr"]
+        ca, cb, qa, qb = [T.FL[:, 64 * n:64 * n + 64] for n in range(4)]
+
+        def look_up(buf, at, cut, key):
+            for qu, a, b in [("V", 0, cut), ("S", cut, S)]:
+                gather(qu, T[buf][:, a:b], T.KK[:, :], T.KL[:, at + a // 16:at + b // 16], kr + [key], keys(buf, a, b))
+
+        for h in range(2):
+            for qu, a in [("V", 512 * h), ("S", 512 * h + 256)]:
+                gather(qu, T.GB[:, a:a + 256], T.KK[:, :], T.KL[:, 64 + a // 16:80 + a // 16], kr + ["KLb"], keys("GB", a, a + 256))
+            conv_half("F2", "ZE", "GB", h, True, True)
+        for h in range(2):
+            conv_half("C1", "ZK", "GB", h, False, True)
+        look_up("GD", 128, CUT_D, "KLd")
+        vcopy(T.KL[:, 192:256], T.F2[:, 0:64], ["F2"], ["KLe"])
+        if not last:
+            vcopy(T.JY[:, 0:64], T.F2[:, 0:64], ["F2"], ["JY0"])
+
+        def veto(out, sign, key):
+            add("S", lambda: SC.activation(out, T.C1[:, 0:64], AF.Relu, bias=BIG, scale=sign * BIG), r=["C1"], w=[key])
+
+        veto(qa, 1.0, "qa")
+        look_up("GZ", 192, CUT_E, "KLe")
+        veto(qb, -1.0, "qb")
+        conv("C0", "ZK", "GD", 0, keys("GD"), True, False)
+        mms("C0", 64, [("ID", qa)], False, True, ["qa"])
+        conv("F0", "ZK", "GZ", 0, keys("GZ"), True, False)
+        mms("F0", 64, [("ID", qb)], False, True, ["qb"])
+        if last:
+            vtt(ca, T.C0[:, 0:64], lst("KA"), A.is_lt, ["C0", "KA"], ["ca"])
+            vtt(lst("KB"), T.C1[:, 0:64], lst("KP"), A.add, ["C1", "KP"], ["KB"])
+            vtt(lst("DE"), T.F2[:, 0:64], lst("B"), A.subtract, ["F2", "B"], ["DE"])
+            vtt(lst("TA"), lst("DC"), ca, A.mult, ["DC", "ca"], ["TA"])
+            vtt(lst("YA"), lst("TA"), lst("B"), A.add, ["TA", "B"], ["YA"])
+            vtt(cb, T.F0[:, 0:64], lst("KB"), A.is_lt, ["F0", "KB"], ["cb"])
+            vtt(lst("TB"), lst("DE"), cb, A.mult, ["DE", "cb"], ["TB"])
+            vtt(lst("Y"), lst("TB"), lst("YA"), A.add, ["TB", "YA"], ["Y"])
+            dma(T.ylink[:, :], lst("Y"), ["Y"], ["y"], "out")
             break
-        send(TT[un][:, q * H:(q + 1) * H], "aT%d" % (t + 1), "lT%d" % un, to)
-        arrival("aT%d" % (t + 1), ["Tr%d" % un])
-        conv2("P2", "ZV%d" % u, tn, to, start=False)
+
+        def changes(n, flag, key, h):
+            at = 128 * n + 64 * h
+            buf, k = [("DP", "DC"), ("F1", "F1")][n]
+            vtt(T.PP[:, at:at + 64], T[buf][:, 64 * h:64 * h + 64], flag, A.mult, [k, key], ["PP%d%d" % (n, h)])
+
+        pieces([T.JY[:, 64:128], T.JY[:, 128:192]], T.JY[:, 0:64], ["JY0"], "JY")
+        vtt(ca, T.C0[:, 0:64], lst("KA"), A.is_lt, ["C0", "KA"], ["ca"])
+        vcopy(T.DP[:, 128:256], T.JY[:, 64:192], ["JYh", "JYl"], ["DE"])
+        for h in range(2):
+            changes(0, ca, "ca", h)
+        vtt(lst("KB"), T.C1[:, 0:64], lst("KP"), A.add, ["C1", "KP"], ["KB"])
+        mms("F1", 128, [("ID", T.DP[:, 128:256])], False, True, ["DE"])
+        mms("P2", 64, [("SH%d" % u, ca)], False, False, ["ca"])
+        spread([(T.PP[:, 0:64], 0), (T.PP[:, 64:128], 1)], ["PP00", "PP01"], False)
+        vtt(cb, T.F0[:, 0:64], lst("KB"), A.is_lt, ["F0", "KB"], ["cb"])
+        mms("P2", 64, [("SH%d" % u, cb)], False, True, ["cb"])
+        for h in range(2):
+            changes(1, cb, "cb", h)
+            spread([(T.PP[:, 128 + 64 * h:192 + 64 * h], h)], ["PP1%d" % h], h == 1)
         lo = min(XAT[u], NXAT[u])
         vts(T.AV[:, :], T.P2[:, 0:64], float(XAT[u] - lo), None, A.add, None, ["P2"], ["AV"])
-        for h, (a, b) in enumerate(hv):
-            gather("VS"[h], xown(t + 1, a, b), T.XX[:, lo:lo + S + W], T.AV[:, a // 16:b // 16],
-                   xr + ["N%d" % u, "AV"], xk(t + 1, a, b))
+        vtt(T.BL[:, :], T.BL[:, :], T.PP[:, 0:128], A.add, ["BL", "PP00", "PP01"], ["BL"])
+        table_out(t + 1)
+        for qu, a, b in [("V", 0, CUT_X), ("S", CUT_X, S)]:
+            gather(qu, xown(t + 1, a, b), T.XX[:, lo:lo + S + W], T.AV[:, a // 16:b // 16], xr + ["N%d" % u, "AV"], xk(t + 1, a, b))
         send(xown(t + 1), "aX%d" % (t + 1), "lX%d" % un, xk(t + 1))
         arrival("aX%d" % (t + 1), ["Xr%d" % un])
+        vtt(T.BL[:, :], T.BL[:, :], T.PP[:, 128:256], A.add, ["BL", "PP10", "PP11"], ["BL"])
         if t + 2 < RO:
-            drift_x(t + 1)
-        conv2("F2", "ZF", tn, to)
-        vcopy(T.KL[:, 0:64], T.F2[:, 0:64], ["F2"], ["KLb"])
-        if first:
-            order_lanes(1)
-            last_constants()
-        open_sums(t + 1)
-        partners_of_c(t + 1)
+            offsets(t + 2)
+        partner_lists()
+        open_diff(t + 1)
         add("S", lambda n=t + 1: SC.activation(T.XV[:, :], xown(n), AF.Copy), r=xk(t + 1), w=["XV"])
-        if first:
-            statics(2, 3)
+        look_up_c(t + 1)
 
     emit({"G": g, "V": V, "S": SC, "P": PE, "Y": SY}, T)

from concourse.bass import DstId, RemoteDMATransfer
from concourse.mybir import AluOpType as A, ActivationFunctionType as AF

RO, S, W, N = 6, 1024, 4096, 4
Q4 = S // 4
BF, F32, I32, U16 = "bfloat16", "float32", "int32", "uint16"
CHUNKS = {"A": (0, 448), "B": (448, 704), "C": (704, 1024), "D": (448, 1024), "a": (0, 256), "b": (256, 448)}
DIFF = "C"
MATS = ["BP", "BM", "Kg"]
ZERO_GAIN = -256.0 * 4096.0

TAIL = ("xd:C xd:B n1 pb:B m4:A s:2:A n4 s:4:A m3:C r1 ko:A:S k:A d4 m1:B s:3:C s:1:C r4 m2:C s:1:B m4:B s:2:C s:4:C m2:B "
        "ko:C:S s:4:B s:2:B ko:B:V k:D")
GAIN = ("xb:A m3:a s:5:A pb:A kd xd:A m3:b m3:B xb:D m1:A s:5:B s:3:A m2:A s:5:C s:3:B m4:A s:1:A m3:C xd:B xd:C n1 pb:B "
        "s:2:A m1:B r1 s:4:A n4 d4 ko:A:S s:1:C s:3:C m2:C r4 m4:B k:A s:1:B m2:B s:2:C s:4:B s:4:C ko:C:S s:2:B ko:B:V k:D")
GAIN0 = "xb:A m3:A pb:A tc xb:D m3:B m1:A kd xd:A s:3:A s:5:A s:1:A s:3:B s:5:B s:5:C m2:A " + TAIL
CUT_C = 768
CUT_D, CUT_E, CUT_X = 352, 640, 352
BIG = 2.0 ** 23

SCRATCH = {
    "XX": ("sbuf", [128, 2 * (S + W)], BF), "KK": ("sbuf", [128, W], BF), "TT": ("sbuf", [128, W // 4], BF),
    "SG": ("sbuf", [128, S], BF), "TC": ("sbuf", [128, S], BF), "MK": ("sbuf", [128, S], BF),
    "XV": ("sbuf", [128, S], BF), "XB": ("sbuf", [128, S], BF), "XD": ("sbuf", [128, S], BF),
    "M1": ("sbuf", [128, S], BF), "M2": ("sbuf", [128, S], BF), "M3": ("sbuf", [128, S], BF), "M4": ("sbuf", [128, S], BF),
    "GB": ("sbuf", [128, S], BF), "GZ": ("sbuf", [128, S], BF),
    "IN": ("sbuf", [128, 7 * 64], I32), "J": ("sbuf", [128, 320], I32), "JY": ("sbuf", [128, 192], I32),
    "BL": ("sbuf", [128, 128], BF), "MP": ("sbuf", [128, RO * 128], BF), "SV": ("sbuf", [128, 128], BF),
    "DP": ("sbuf", [128, 256], BF), "PP": ("sbuf", [128, 256], BF), "FL": ("sbuf", [128, 256], BF),
    "GD": ("sbuf", [128, S], BF), "N32": ("sbuf", [128, 128], F32),
    "CL": ("sbuf", [128, RO * 64], U16), "CU": ("sbuf", [128, RO * 128], U16),
    "KL": ("sbuf", [128, 256], U16), "ZP": ("sbuf", [128, 4, 144], BF), "AV": ("sbuf", [128, 64], U16), "L": ("sbuf", [128, 11, 64], F32),
    "VAL": ("sbuf", [128, 152], F32), "PC": ("sbuf", [128, 8], I32), "CF": ("sbuf", [128, 16], F32),
    "OH": ("sbuf", [128, 16], F32), "O4": ("sbuf", [128, 4], F32), "GM": ("sbuf", [128, 16], F32), "WC": ("sbuf", [128, 16], F32),
    "VR": ("sbuf", [128, 64], I32), "MT": ("sbuf", [128, 16], BF), "ZS": ("sbuf", [128, 4, 152], BF), "ZZ": ("sbuf", [128, Q4], BF),
    "ZD": ("sbuf", [128, 144], BF), "ZE": ("sbuf", [128, 144], BF), "ZK": ("sbuf", [128, 144], BF),
    "MAT": ("sbuf", [128, len(MATS) * 128], BF), "ID": ("sbuf", [128, 152], BF), "Z1": ("sbuf", [128, 144], BF), "NI": ("sbuf", [128, 128], BF),
    "I64": ("sbuf", [128, 128], BF), "SH0": ("sbuf", [128, 128], BF), "SH1": ("sbuf", [128, 128], BF),
    "F0": ("psum", [128, 512], F32), "F1": ("psum", [128, 512], F32), "F2": ("psum", [128, 512], F32),
    "P0": ("psum", [128, 512], F32), "P1": ("psum", [128, 512], F32), "P2": ("psum", [128, 512], F32),
    "C0": ("psum", [128, 512], F32), "C1": ("psum", [128, 512], F32),
}
PSUM = [k for k, v in SCRATCH.items() if v[0] == "psum"]
SEMAPHORES = (["sV", "sS", "sP", "sG", "ldl", "ldc", "ldx", "ldu", "out", "lT", "lX0", "lX1", "lKA", "lKD", "ldv"]
              + ["%s%d" % (n, t) for n in ("aX", "aK", "aT", "dU", "dX", "dS") for t in range(RO)])
LISTS = ["KP", "NO", "KA", "KB", "B", "DC", "DE", "TA", "TB", "YA", "Y"]


def make_plan():
    ops, last_w, readers, cnt = [], {}, {}, {}

    def add(q, fn, r=(), w=(), sem=None, inc=1, acc=False, whole=False):
        deps = set()
        for k in r:
            deps.add(last_w[k])
            if k in PSUM:
                deps.update(o for o in readers.get(k, ()) if ops[o]["q"] != q)
        for k in w:
            if k in last_w and not (acc and ops[last_w[k]]["q"] == q):
                deps.add(last_w[k])
            deps.update(readers.get(k, ()))
        sem = sem or {"V": "sV", "S": "sS", "P": "sP", "G": "sG"}[q]
        cnt[sem] = cnt.get(sem, 0) + inc
        me = len(ops)
        ops.append(dict(q=q, fn=fn, deps=sorted(deps), sem=sem, n=cnt[sem], inc=inc, whole=whole))
        for k in r:
            readers.setdefault(k, []).append(me)
        for k in w:
            last_w[k] = me
            readers[k] = []
        return me

    def emit(queues, T):
        clock = {q: {} for q in queues}
        seen = {}
        for me, o in enumerate(ops):
            q = o["q"]
            if q == "X":
                o["clock"] = {}
                seen[o["sem"]] = o["n"]
                continue
            ck = clock[q]
            for d in sorted(o["deps"], reverse=True):
                p = ops[d]
                n = seen[p["sem"]] if p["whole"] else p["n"]
                if ck.get(p["sem"], 0) >= n:
                    continue
                queues[q].wait_ge(T.sem[p["sem"]], n)
                ck[p["sem"]] = n
                for z in ([y for y in ops[:me] if y["sem"] == p["sem"]] if p["whole"] else [p]):
                    for s, v in z["clock"].items():
                        if ck.get(s, 0) < v:
                            ck[s] = v
            o["clock"] = dict(ck)
            seen[o["sem"]] = o["n"]
            ins = o["fn"]()
            if ins is not None:
                ins.then_inc(T.sem[o["sem"]], o["inc"])
        for s, n in cnt.items():
            if clock["G"].get(s, 0) < n:
                queues["G"].wait_ge(T.sem[s], n)

    return add, emit


def rank_program(g, core, T, topo):
    q = T.rank_of(core)
    if q is None:
        return
    V, SC, PE, SY = g.vector, g.scalar, g.tensor, g.sync
    add, emit = make_plan()
    peers = [c for c in T.cores if c != core]
    mask = topo.mask(core, peers[0])
    for c in peers:
        mask &= topo.mask(core, c)
    nen = bin(mask).count("1")

    def send(ap, rsem, lsem, r):
        def fn():
            ids = [DstId(rid=topo.addr(c)[0], pnc=topo.addr(c)[1]) for c in peers]
            g.remote_dma_fused([RemoteDMATransfer(dst_ids=ids, dma_engine_mask=mask, remote_sem=T.sem[rsem],
                                                  srcs=[ap], dsts=[ap] * len(ids))], local_sem=T.sem[lsem])
        add("G", fn, r=r, sem=lsem, inc=nen, whole=True)

    def arrival(sem, keys, calls=1):
        add("X", None, w=keys, sem=sem, inc=nen * len(peers) * calls)

    def dma(out, in_, r, w, sem):
        add("Y", lambda: SY.dma_start(out, in_), r=r, w=w, sem=sem, inc=16, whole=True)

    def vcopy(out, in_, r, w):
        add("V", lambda: V.tensor_copy(out, in_), r=r, w=w)

    def vts(out, in0, s1, s2, op0, op1, r, w):
        if op1 is None:
            add("V", lambda: V.tensor_scalar(out, in0, s1, None, op0), r=r, w=w)
        else:
            add("V", lambda: V.tensor_scalar(out, in0, s1, s2, op0, op1), r=r, w=w)

    def vtt(out, a, b, op, r, w):
        add("V", lambda: V.tensor_tensor(out, a, b, op), r=r, w=w)

    def relu(qu, out, in_, bias, r, w):
        if qu == "V":
            vts(out, in_, bias, 0.0, A.add, A.max, r, w)
        else:
            add("S", lambda: SC.activation(out, in_, AF.Relu, bias=bias), r=r, w=w)

    def gather(qu, out, win, off, r, w):
        if qu == "V":
            add("V", lambda: V.tensor_copy(out, win.indirect(off)), r=r, w=w)
        else:
            add("S", lambda: SC.activation(out, win.indirect(off), AF.Copy), r=r, w=w)

    def conv(bank, z, src, a, r, start=True, stop=True):
        def fn():
            for i in range(16):
                ins = PE.matmul(T[bank][:, 0:64], T[z][:, 15 - i:143 - i], T[src][:, a + i:a + S:16],
                                start and i == 0, stop and i == 15)
            return ins
        add("P", fn, r=r + [z], w=[bank], acc=not start)

    def conv_half(bank, z, src, h, start, stop):
        def fn():
            for m in range(8):
                i = 8 * h + m
                ins = PE.matmul(T[bank][:, 0:64], T[z][:, 15 - i:143 - i], T[src][:, 512 * h + m:512 * h + 512:8],
                                start and i == 0, stop and i == 15)
            return ins
        add("P", fn, r=keys(src, 512 * h, 512 * h + 512) + [z], w=[bank], acc=h == 1 or not start)

    def spread(lists, r, stop):
        def fn():
            todo = [(x, p, a) for x, p in lists for a in range(4)]
            for n, (x, p, a) in enumerate(todo):
                o = 12 + 4 * a - 4 * p
                ins = PE.matmul(T.P0[:, a:Q4:4], T.ZS[:, a, o:o + 128], x, False, stop and n == len(todo) - 1)
            return ins
        add("P", fn, r=r + ["ZS%d" % a for a in range(4)], w=["P0"], acc=True)

    matkeys = {m: [m] for m in ("ID", "NI", "I64", "N32", "SH0", "SH1")}
    matkeys.update({"ZZ": ["ZZ"], "LO": ["ZP2"]})

    def mat(l):
        if l in MATS:
            m = MATS.index(l)
            return T.MAT[:, m * 128:(m + 1) * 128]
        if l == "LO":
            return T.ZP[:, 2, 8:136]
        return T.ID[:, 12:140] if l == "ID" else T[l][:, 0:128]

    def mms(bank, n, terms, start, stop, r):
        def fn():
            for j, (l, x) in enumerate(terms):
                ins = PE.matmul(T[bank][:, 0:n], mat(l), x, start and j == 0, stop and j == len(terms) - 1)
            return ins
        add("P", fn, r=r + [k for l, _ in terms for k in matkeys[l]], w=[bank], acc=not start)

    own = q * S
    FB = {"A": "F0", "B": "F1", "C": "F2"}
    PB = {"A": "P0", "B": "P2"}
    XAT, NXAT = [S, S + W], [0, S + 2 * W]

    def keys(name, a=0, b=S):
        return ["%s_%d" % (name, k) for k in range(a // 32, (b + 31) // 32)]

    def lst(name):
        return T.L[:, LISTS.index(name), :]

    def xown(n, a=0, b=S):
        return T.XX[:, XAT[n % 2] + own + a:XAT[n % 2] + own + b]

    def xk(n, a=0, b=S):
        return keys("X%d" % (n % 2), a, b)

    def nx(n):
        return T.XX[:, NXAT[n % 2]:NXAT[n % 2] + S]

    def drift_u(n, extra):
        dma(nx(n), T.u[:, :], extra, ["N%d" % (n % 2)], "dU%d" % n)

    def drift_x(n, extra):
        add("G", lambda: g.dma_start(nx(n), xown(n), accum_op=A.add), r=xk(n) + ["N%d" % (n % 2)] + extra,
            w=["N%d" % (n % 2)], sem="dX%d" % n, inc=16, whole=True)

    def drift_over(n):
        vts(T.SG[:, :], nx(n), 32.0, -32.0, A.is_ge, A.mult, ["N%d" % (n % 2)], ["SG"])
        add("G", lambda: g.dma_start(nx(n), T.SG[:, :], accum_op=A.add), r=["SG", "N%d" % (n % 2)], w=["N%d" % (n % 2)],
            sem="dS%d" % n, inc=16, whole=True)

    def cand(t):
        return T.IN[:, 64 + t * 64:128 + t * 64]

    def pieces(out, x, r, w):
        vts(out[0], x, 6, None, A.arith_shift_right, None, r, [w + "h"])
        vts(out[1], x, 63, None, A.bitwise_and, None, r, [w + "l"])

    def minima(t, between):
        k = ["IN0" if t < 2 else "IN"]
        vtt(T.J[:, 0:64], cand(t), T.VR[:, :], A.min, k + ["VR"], ["J0"])
        between()
        pieces([T.J[:, 64:128], T.J[:, 128:192]], T.J[:, 0:64], ["J0"], "J1")

    def minima_out(t):
        vcopy(T.MP[:, 128 * t:128 * t + 128], T.J[:, 64:192], ["J1h", "J1l"], ["MP%d" % t])

    def offsets(t):
        k = ["IN0" if t < 2 else "IN"]
        vts(T.J[:, 192:256], cand(t), 2, None, A.arith_shift_right, None, k, ["J3"])
        vts(T.J[:, 256:320], cand(t), 3, None, A.bitwise_and, None, k, ["J4"])
        vcopy(T.CL[:, 64 * t:64 * t + 64], cand(t), k, ["CL%d" % t])
        vcopy(T.CU[:, 128 * t:128 * t + 128], T.J[:, 192:320], ["J3", "J4"], ["CU%d" % t])

    def lane_mask(t):
        gather("S", T.MK[:, :], T.MT[:, :], T.CU[:, 128 * t + 64:128 * t + 128], ["MT", "CU%d" % t], ["MK"])

    def open_table(t):
        if t == 0:
            mms("P0", Q4, [("ZZ", T.ZZ[:, :])], True, False, [])
            spread([(T.BL[:, 0:64], 0), (T.BL[:, 64:128], 1)], ["BL"], False)
        spread([(T.MP[:, 128 * t:128 * t + 64], 2), (T.MP[:, 128 * t + 64:128 * t + 128], 3)], ["MP%d" % t], t == 0)

    def table_out(t):
        vcopy(T.TT[:, q * Q4:(q + 1) * Q4], T.P0[:, 0:Q4], ["P0"], ["To"])
        send(T.TT[:, q * Q4:(q + 1) * Q4], "aT%d" % t, "lT", ["To"])
        arrival("aT%d" % t, ["Tr"])

    def look_up_c(t):
        cut = CUT_C
        r, k = ["To", "Tr", "CU%d" % t], 128 * t + cut // 16
        vtt(T.TC[:, 0:cut], T.TT[:, :].indirect(T.CU[:, 128 * t:k]), T.MK[:, 0:cut], A.mult, r + ["MK"], keys("TC", 0, cut))
        if cut < S:
            mms("C1", S - cut, [("I64", T.MK[:, cut:S])], True, False, ["MK"])
            gather("S", T.GZ[:, cut:S], T.TT[:, :], T.CU[:, k:128 * t + 64], r, keys("GZ", cut, S))
            mms("C1", S - cut, [("ID", T.GZ[:, cut:S])], False, True, keys("GZ", cut, S))
            relu("S", T.TC[:, cut:S], T.C1[:, 0:S - cut], -64.0, ["C1"], keys("TC", cut, S))
        conv("C0", "ZD", "TC", 0, keys("TC"))

    def partner_lists():
        mms("F1", 128, [("ZZ", T.ZZ[:, 0:128])], True, False, [])

        def fn():
            for p, l in enumerate(["I64", "ID"]):
                PE.matmul(T.F1[:, 0:64], mat(l), T.BL[:, 64 * p:64 * p + 64], False, False)
                for h in range(2):
                    for r in range(2):
                        o = 8 + 8 * h - 8 * r
                        ins = PE.matmul(T.F1[:, 64 + 32 * h:96 + 32 * h], T.ZP[:, 2 * p + h, o:o + 128],
                                        T.BL[:, 64 * p + r:64 * p + 64:2], False, p + h + r == 3)
            return ins
        add("P", fn, r=["BL", "ID", "I64"] + ["ZP%d" % n for n in range(4)], w=["F1"], acc=True)
        vcopy(T.KL[:, 0:128], T.F1[:, 0:128], ["F1"], ["KLb"])

    def open_diff(t):
        a, b = CHUNKS[DIFF]
        mms("P1", b - a, [("ID", xown(t, a, b))], True, False, xk(t, a, b))

    dma(xown(0), T.x[:, :], [], xk(0), "ldx")
    dma(T.IN[:, 0:64], T.link[:, :], [], ["INl"], "ldl")
    dma(T.IN[:, 64:192], T.cand[:, 0:128], [], ["IN0"], "ldc")
    dma(T.XV[:, :], T.x[:, :], [], ["XV"], "ldv")
    drift_u(0, [])
    dma(T.IN[:, 192:448], T.cand[:, 128:384], [], ["IN"], "ldu")
    add("G", lambda: g.iota(T.PC[:, 0:1], [[1, 1]], 0, 1), w=["PC0"])
    add("G", lambda: g.iota(T.VAL[:, :], [[1, 152]], 0, 0, allow_small_or_imprecise_dtypes=True), w=["VAL"])
    send(xown(0), "aX0", "lX0", xk(0))
    arrival("aX0", ["Xr0"])

    def cf(j):
        return T.CF[:, j:j + 1]

    def pc(j):
        return T.PC[:, j:j + 1]

    cols = {}

    def col(name):
        if name not in cols:
            cols[name] = len(cols)
        return T.WC[:, cols[name]:cols[name] + 1]

    def oh(l):
        return T.OH[:, l:l + 1]

    def o4(l):
        return T.O4[:, l:l + 1]

    def axpy(name, x, a, y, r):
        vts(col(name), x, a, y, A.mult, A.add, r, ["c" + name])

    def entries(table):
        for m, l, c, neg in table:
            base = MATS.index(m) * 128
            out, gm = T.MAT[:, base + l:base + 128:16], T.GM[:, 8 * neg:8 * neg + 8]
            key = "m%s%d" % (m, l)
            matkeys.setdefault(m, []).append(key)
            sc, r = (1.0, []) if c is None else (o4(c), ["O4"])
            add("S", lambda out=out, gm=gm, sc=sc: SC.activation(out, gm, AF.Identity, scale=sc), r=r + ["MAT", "GM%d" % neg], w=[key])

    def scaled(out, x, sc, r, w):
        if isinstance(sc, str):
            sc, r = col(sc), r + ["c" + sc]
        add("S", lambda: SC.activation(out, x, AF.Identity, scale=sc), r=r, w=w)

    add("V", lambda: V.memset(T.ZZ[:, :], 0.0), w=["ZZ"])
    add("V", lambda: V.memset(T.MAT[:, :], 0.0), w=["MAT"])
    vts(pc(1), pc(0), 15, None, A.bitwise_and, None, ["PC0"], ["PC1"])
    vts(pc(2), pc(0), 4, None, A.arith_shift_right, None, ["PC0"], ["PC2"])
    vts(pc(3), pc(0), 2, 3, A.arith_shift_right, A.bitwise_and, ["PC0"], ["PC3"])
    vts(pc(4), pc(0), 3, None, A.bitwise_and, None, ["PC0"], ["PC4"])
    vts(pc(5), pc(0), 112.0, None, A.add, None, ["PC0"], ["PC5"])
    vts(cf(6), pc(0), 12.0, None, A.add, None, ["PC0"], ["CF6"])
    vcopy(T.CF[:, 0:5], T.PC[:, 0:5], ["PC%d" % j for j in range(5)], ["CF"])
    vts(pc(6), pc(5), 127, None, A.bitwise_and, None, ["PC5"], ["PC6"])
    vts(T.O4[:, :], T.VAL[:, 0:4], cf(3), None, A.is_equal, None, ["VAL", "CF"], ["O4"])
    vts(cf(7), cf(1), float(own), None, A.add, None, ["CF"], ["CF7"])
    vts(T.GM[:, 0:8], T.VAL[:, 0:8], cf(2), None, A.is_equal, None, ["VAL", "CF"], ["GM0"])
    vts(T.GM[:, 8:16], T.VAL[:, 0:8], cf(2), -1.0, A.is_equal, A.mult, ["VAL", "CF"], ["GM1"])
    vts(T.VR[:, :], T.VAL[:, 0:64], 16.0, cf(7), A.mult, A.add, ["VAL", "CF7"], ["VR"])
    vts(T.ID[:, :], T.VAL[:, :], cf(6), None, A.is_equal, None, ["VAL", "CF6"], ["ID"])
    for a in range(4):
        scaled(T.ZS[:, a, :], T.ID[:, :], o4(a), ["ID", "O4"], ["ZS%d" % a])
    entries([("BP", 0, None, 0), ("BP", 1, None, 1), ("BM", 0, None, 1), ("BM", 1, None, 0),
             ("Kg", 4, 0, 0), ("Kg", 5, 1, 0), ("Kg", 2, 2, 0), ("Kg", 3, 3, 0)])
    vts(T.MT[:, :], T.VAL[:, 0:16], cf(4), None, A.is_equal, None, ["VAL", "CF"], ["MT"])
    vts(cf(8), cf(2), 16.0, 15.0, A.mult, A.add, ["CF"], ["CF8"])
    vcopy(cf(9), pc(6), ["PC6"], ["CF9"])
    vts(T.OH[:, :], T.VAL[:, 0:16], cf(1), None, A.is_equal, None, ["VAL", "CF"], ["OH"])
    axpy("wd", o4(0), 64.0, o4(1), ["O4"])
    vts(T.Z1[:, :], T.VAL[:, 0:144], cf(8), None, A.is_equal, None, ["VAL", "CF8"], ["Z1"])
    for m, sc in [("I64", 64.0), ("NI", -1.0)]:
        scaled(mat(m), mat("ID"), sc, ["ID"], [m])
    scaled(T.ZD[:, :], T.Z1[:, :], "wd", ["Z1"], ["ZD"])
    for h in range(2):
        vts(col("l%d" % h), o4(2 * h), o4(2 * h + 1), None, A.add, None, ["O4"], ["cl%d" % h])
        vts(col("h%d" % h), o4(2 * h), o4(2 * h + 1), 64.0, A.add, A.mult, ["O4"], ["ch%d" % h])
    for n, c in enumerate(["h0", "h1", "l0", "l1"]):
        scaled(T.ZP[:, n, :], T.ID[:, 4:148], c, ["ID"], ["ZP%d" % n])
    minima(0, lambda: pieces([T.JY[:, 64:128], T.JY[:, 128:192]], T.IN[:, 0:64], ["INl"], "JY"))
    vcopy(T.BL[:, :], T.JY[:, 64:192], ["JYh", "JYl"], ["BL"])
    minima_out(0)
    open_table(0)
    offsets(0)
    lane_mask(0)
    table_out(0)
    vts(col("k0"), oh(0), oh(1), None, A.subtract, None, ["OH"], ["ck0"])
    axpy("k1", oh(2), 64.0, oh(3), ["OH"])
    axpy("we", oh(4), 64.0, oh(5), ["OH"])
    vts(col("wk"), col("k0"), 4096.0, col("k1"), A.mult, A.subtract, ["ck0", "ck1"], ["cwk"])
    vts(col("bk"), col("k0"), -256.0, None, A.mult, None, ["ck0"], ["cbk"])
    partner_lists()
    for z, c in [("ZK", "wk"), ("ZE", "we")]:
        scaled(T[z][:, :], T.Z1[:, :], c, ["Z1"], [z])
    scaled(T.N32[:, :], mat("ID"), -1.0, ["ID"], ["N32"])
    for u in range(2):
        vts(T["SH%d" % u][:, :], T.VAL[:, 0:128], cf(9), float(NXAT[u] - XAT[u] - own), A.is_equal, A.mult, ["VAL", "CF9"], ["SH%d" % u])
    pieces([T.JY[:, 64:128], T.JY[:, 128:192]], T.VR[:, :], ["VR"], "JY")
    offsets(1)
    vcopy(T.SV[:, :], T.JY[:, 64:192], ["JYh", "JYl"], ["SV"])
    open_diff(0)

    for t in range(RO):
        first, last = t == 0, t + 1 == RO
        u, un = t % 2, (t + 1) % 2
        xw = T.XX[:, XAT[u]:XAT[u] + W]
        xr = xk(t) + ["Xr%d" % u]
        ck = "CL%d" % t
        todo = {c: 5 for c in "ABC"}

        def gmax(m, other, c):
            a, b = CHUNKS[c]
            vtt(T[m][:, a:b], xw.indirect(T.CL[:, t * 64 + a // 16:t * 64 + b // 16]), T[other][:, a:b], A.max,
                xr + [ck] + (["XV"] if other == "XV" else keys(other, a, b)), keys(m, a, b))

        def summed(term, c):
            a, b = CHUNKS[c]
            todo[c] -= 1
            l, buf = ("Kg", "TC") if term == "5" else ("BP" if term in "12" else "BM", "M" + term)
            mms(FB[c], b - a, [(l, T[buf][:, a:b])], todo[c] == 4, todo[c] == 0, keys(buf, a, b))

        def feat(buf, j, c, qu="S"):
            a, b = CHUNKS[c]
            gather(qu, T[buf][:, a:b], xw, T.KL[:, j * 128 + a // 16:j * 128 + b // 16], xr + ["KL" + "bd"[j]], keys(buf, a, b))

        def psum(bank, l, buf, c, start, stop):
            a, b = CHUNKS[c]
            mms(bank, b - a, [(l, T[buf][:, a:b])], start, stop, keys(buf, a, b))

        def bmax(m, c):
            a, b = CHUNKS[c]
            other, r = (xown(t, a, b), xk(t, a, b)) if m == "M1" else (T.XD[:, a:b], keys("XD", a, b))
            vtt(T[m][:, a:b], T[PB[c]][:, 0:b - a], other, A.max, [PB[c]] + r, keys(m, a, b))

        def over(m, bank, c, o):
            a, b = CHUNKS[c]
            relu("S", T[m][:, a:b], T[bank][:, a - o:b - o], 0.0, [bank], keys(m, a, b))

        def ko(c, qu):
            a, b = CHUNKS[c]
            relu(qu, T.KK[:, own + a:own + b], T[FB[c]][:, 0:b - a], col("bk"), [FB[c], "cbk"], keys("Ko", a, b))

        def keys_out(c):
            a, b = CHUNKS[c]
            send(T.KK[:, own + a:own + b], "aK%d" % t, "lK" + c, keys("Ko", a, b))

        def list_of_d():
            vcopy(T.KL[:, 128:192], T.C0[:, 0:64], ["C0"], ["KLd"])

        steps = {
            "m3": lambda c: gmax("M3", "XV", c), "m2": lambda c: gmax("M2", "XD", c),
            "xb": lambda c: feat("XB", 0, c), "xd": lambda c, qu="S": feat("XD", 1, c, qu),
            "pb": lambda c: psum(PB[c], "ID", "XB", c, True, True), "n1": lambda: psum("P1", "NI", "XB", DIFF, False, True),
            "n4": lambda: psum("C1", "NI", "XB", "C", True, False), "d4": lambda: psum("C1", "ID", "XD", "C", False, True),
            "m1": lambda c: bmax("M1", c), "m4": lambda c: bmax("M4", c),
            "r1": lambda c="C": over("M1", "P1", c, CHUNKS[DIFF][0]), "r4": lambda: over("M4", "C1", "C", CHUNKS["C"][0]),
            "kd": list_of_d, "tc": lambda: look_up_c(0), "s": summed, "ko": ko, "k": keys_out,
        }
        if not last:
            drift_x(t, ["Xr%d" % u])
        if t + 2 < RO:
            drift_u(t + 1, ["Xr%d" % u])
        for step in (GAIN0 if first else GAIN).split():
            name, *args = step.split(":")
            steps[name](*args)
        arrival("aK%d" % t, ["Kr"], calls=2)
        conv("F1", "ZK", "KK", own, keys("Ko"))
        if not last:
            mms("P0", Q4, [("LO", T.TT[:, q * Q4:(q + 1) * Q4])], True, False, ["To"])
            mms("P2", 64, [("I64", T.SV[:, 0:64]), ("ID", T.SV[:, 64:128])], True, False, ["SV"])
            lane_mask(t + 1)
            drift_over(t)
            minima(t + 1, lambda: pieces([T.JY[:, 64:128], T.JY[:, 128:192]], cand(t), ["IN0", "IN"], "JY"))
        vts(lst("KP"), T.F1[:, 0:64], ZERO_GAIN, None, A.max, None, ["F1"], ["KP"])
        vts(lst("NO"), T.F1[:, 0:64], ZERO_GAIN, -BIG, A.is_le, A.mult, ["F1"], ["NO"])
        mms("C1", 64, [("N32", lst("KP"))], True, False, ["KP"])
        if last:
            vcopy(lst("B"), T.KL[:, 0:64], ["KLb"], ["B"])
            vtt(lst("DC"), cand(t), lst("B"), A.subtract, ["IN", "B"], ["DC"])
        else:
            minima_out(t + 1)
            open_table(t + 1)
            vtt(T.DP[:, 0:128], T.JY[:, 64:192], T.BL[:, :], A.subtract, ["JYh", "JYl", "BL"], ["DC"])
            mms("F1", 128, [("NI", T.BL[:, :])], True, False, ["BL"])
        vtt(lst("KA"), lst("KP"), lst("NO"), A.add, ["KP", "NO"], ["KA"])
        kr = keys("Ko") + ["Kr"]
        ca, cb, qa, qb = [T.FL[:, 64 * n:64 * n + 64] for n in range(4)]

        def look_up(buf, at, cut, key):
            for qu, a, b in [("V", 0, cut), ("S", cut, S)]:
                gather(qu, T[buf][:, a:b], T.KK[:, :], T.KL[:, at + a // 16:at + b // 16], kr + [key], keys(buf, a, b))

        for h in range(2):
            for qu, a in [("V", 512 * h), ("S", 512 * h + 256)]:
                gather(qu, T.GB[:, a:a + 256], T.KK[:, :], T.KL[:, 64 + a // 16:80 + a // 16], kr + ["KLb"], keys("GB", a, a + 256))
            conv_half("F2", "ZE", "GB", h, True, True)
        for h in range(2):
            conv_half("C1", "ZK", "GB", h, False, True)
        look_up("GD", 128, CUT_D, "KLd")
        vcopy(T.KL[:, 192:256], T.F2[:, 0:64], ["F2"], ["KLe"])
        if not last:
            vcopy(T.JY[:, 0:64], T.F2[:, 0:64], ["F2"], ["JY0"])

        def veto(out, sign, key):
            add("S", lambda: SC.activation(out, T.C1[:, 0:64], AF.Relu, bias=BIG, scale=sign * BIG), r=["C1"], w=[key])

        veto(qa, 1.0, "qa")
        look_up("GZ", 192, CUT_E, "KLe")
        veto(qb, -1.0, "qb")
        conv("C0", "ZK", "GD", 0, keys("GD"), True, False)
        mms("C0", 64, [("ID", qa)], False, True, ["qa"])
        conv("F0", "ZK", "GZ", 0, keys("GZ"), True, False)
        mms("F0", 64, [("ID", qb)], False, True, ["qb"])
        if last:
            vtt(ca, T.C0[:, 0:64], lst("KA"), A.is_lt, ["C0", "KA"], ["ca"])
            vtt(lst("KB"), T.C1[:, 0:64], lst("KP"), A.add, ["C1", "KP"], ["KB"])
            vtt(lst("DE"), T.F2[:, 0:64], lst("B"), A.subtract, ["F2", "B"], ["DE"])
            vtt(lst("TA"), lst("DC"), ca, A.mult, ["DC", "ca"], ["TA"])
            vtt(lst("YA"), lst("TA"), lst("B"), A.add, ["TA", "B"], ["YA"])
            vtt(cb, T.F0[:, 0:64], lst("KB"), A.is_lt, ["F0", "KB"], ["cb"])
            vtt(lst("TB"), lst("DE"), cb, A.mult, ["DE", "cb"], ["TB"])
            vtt(lst("Y"), lst("TB"), lst("YA"), A.add, ["TB", "YA"], ["Y"])
            dma(T.ylink[:, :], lst("Y"), ["Y"], ["y"], "out")
            break

        def changes(n, flag, key, h):
            at = 128 * n + 64 * h
            buf, k = [("DP", "DC"), ("F1", "F1")][n]
            vtt(T.PP[:, at:at + 64], T[buf][:, 64 * h:64 * h + 64], flag, A.mult, [k, key], ["PP%d%d" % (n, h)])

        pieces([T.JY[:, 64:128], T.JY[:, 128:192]], T.JY[:, 0:64], ["JY0"], "JY")
        vtt(ca, T.C0[:, 0:64], lst("KA"), A.is_lt, ["C0", "KA"], ["ca"])
        vcopy(T.DP[:, 128:256], T.JY[:, 64:192], ["JYh", "JYl"], ["DE"])
        for h in range(2):
            changes(0, ca, "ca", h)
        vtt(lst("KB"), T.C1[:, 0:64], lst("KP"), A.add, ["C1", "KP"], ["KB"])
        mms("F1", 128, [("ID", T.DP[:, 128:256])], False, True, ["DE"])
        mms("P2", 64, [("SH%d" % u, ca)], False, False, ["ca"])
        spread([(T.PP[:, 0:64], 0), (T.PP[:, 64:128], 1)], ["PP00", "PP01"], False)
        vtt(cb, T.F0[:, 0:64], lst("KB"), A.is_lt, ["F0", "KB"], ["cb"])
        mms("P2", 64, [("SH%d" % u, cb)], False, True, ["cb"])
        for h in range(2):
            changes(1, cb, "cb", h)
            spread([(T.PP[:, 128 + 64 * h:192 + 64 * h], h)], ["PP1%d" % h], h == 1)
        lo = min(XAT[u], NXAT[u])
        vts(T.AV[:, :], T.P2[:, 0:64], float(XAT[u] - lo), None, A.add, None, ["P2"], ["AV"])
        vtt(T.BL[:, :], T.BL[:, :], T.PP[:, 0:128], A.add, ["BL", "PP00", "PP01"], ["BL"])
        table_out(t + 1)
        for qu, a, b in [("V", 0, CUT_X), ("S", CUT_X, S)]:
            gather(qu, xown(t + 1, a, b), T.XX[:, lo:lo + S + W], T.AV[:, a // 16:b // 16], xr + ["N%d" % u, "AV"], xk(t + 1, a, b))
        send(xown(t + 1), "aX%d" % (t + 1), "lX%d" % un, xk(t + 1))
        arrival("aX%d" % (t + 1), ["Xr%d" % un])
        vtt(T.BL[:, :], T.BL[:, :], T.PP[:, 128:256], A.add, ["BL", "PP10", "PP11"], ["BL"])
        if t + 2 < RO:
            offsets(t + 2)
        partner_lists()
        open_diff(t + 1)
        add("S", lambda n=t + 1: SC.activation(T.XV[:, :], xown(n), AF.Copy), r=xk(t + 1), w=["XV"])
        look_up_c(t + 1)

    emit({"G": g, "V": V, "S": SC, "P": PE, "Y": SY}, T)
